import numpy as np, ml_dtypes
CORES = [40,41,42,43,44,45,46,47]
N = 8
import mx_ref
BF = ml_dtypes.bfloat16
def gentries(a):
    return np.ascontiguousarray(a.reshape(8, 16, -1).transpose(0, 2, 1)).reshape(8, -1)
def gtable(e):
    e = np.asarray(e); return np.ascontiguousarray(e.reshape(8, -1, 16).transpose(0, 2, 1)).reshape(128, -1).astype(np.int32)
def gcols(t, e):
    v = np.concatenate([t.reshape(8, 16, -1, 4), np.zeros((8, 16, 1, 4), BF)], axis=2)
    return np.ascontiguousarray(np.stack([v[g][:, e[g]] for g in range(8)])).reshape(128, -1)
def gpick(z, e):
    return np.concatenate([z[16 * g:16 * g + 16][:, e[g]] for g in range(8)])
def tile(rs):
    return np.stack(rs, axis=2).reshape(128, -1).astype(BF)
def pick(q, e):
    c = np.concatenate([q[0].reshape(128, -1, 4), np.zeros((128, 1, 4), np.uint8)], axis=1); s = np.concatenate([q[1], np.ones((16, 1), np.uint8)], axis=1)
    return (np.ascontiguousarray(c[:, e].reshape(128, -1)), np.ascontiguousarray(s[:, e]))
def join(*qs):
    return (np.concatenate([q[0] for q in qs], axis=1), np.concatenate([q[1] for q in qs], axis=1))
def put(q, e, v):
    c, s = q[0].reshape(128, -1, 4).copy(), q[1].copy(); c[:, e] = v[0].reshape(128, -1, 4); s[:, e] = v[1]
    return (c.reshape(128, -1), s)
def pk(c, s):
    return (np.ascontiguousarray(c), mx_ref.live(s))
def emit(q):
    return q[0], q[1]
def packed(v, rng):
    q = [mx_ref.quantize(np.ascontiguousarray(v[r])) for r in range(N)]
    return np.stack([a for a, b in q]), np.stack([mx_ref.plane(b, rng) for a, b in q])
def values_of_codes():
    e, c = np.zeros((128, 128, 4), np.float32), np.zeros((128, 2, 4), np.uint8)
    e[np.arange(128), np.arange(128), 0] = 1
    c[:127, :, 0] = np.arange(256).reshape(2, 128).T[:127]
    return mx_ref.matmul(mx_ref.quantize(e.reshape(128, 512).astype(BF)), (c.reshape(128, 8), np.full((16, 2), 127, np.uint8))).T.reshape(-1).astype(np.float64)
CODE_VALUE, SCALE_VALUE = values_of_codes(), 2.0 ** (np.arange(256) - 127.0)
def decode(q):
    return (CODE_VALUE[q[0]].reshape(16, 8, -1, 4) * SCALE_VALUE[q[1]][:, None, :, None] + 0.0).reshape(128, -1).astype(np.float32)
def f(rng, *shape):
    return mx_ref.flush((rng.standard_normal(shape, dtype=np.float32) * np.exp2(rng.integers(-2, 3, shape[:-1] + (1,)))).astype(BF))
def wide(rng, *shape, cols=0):
    v = rng.standard_normal(shape, dtype=np.float32) * np.exp2(rng.integers(-12, 13, shape)).astype(np.float32)
    if cols: v *= np.repeat(np.exp2(rng.integers(-cols, cols + 1, shape[:-2] + (1, shape[-1] // 4))) * (rng.random(shape[:-2] + (1, shape[-1] // 4)) > 0.0625), 4, axis=-1).astype(np.float32)
    return mx_ref.flush(v.astype(BF))
C, K, P, R = 384, 96, 192, 3
def numbers_of(rng):
    return {"x": np.array(f(rng, N, 128, 4 * C)), "u": np.array(f(rng, N, 128, 512)), "v": np.array(f(rng, N, 128, 512))}
def mixed(rng):
    return rng.permuted(np.tile(np.arange(C), (N, 8, 1)), axis=2)
def links(e):
    return np.stack([gtable(e[r]) for r in range(N)])
def packedw(rng, w):
    c, p = packed(np.ascontiguousarray(w).reshape(N, 128, 2048), rng)
    return {"wc": c, "ws": p}
def weights(rng, still=()):
    w = np.array(f(rng, N, 128, 2048)).reshape(N, 8, 16, 4, 8, 16, 4)
    for i in still:
        w[:, :, i] = 0
        w[:, :, :, :, :, i] = 0
    return packedw(rng, w)
def setup_inputs(rng):
    return {**numbers_of(rng), "link": links(mixed(rng)), **weights(rng)}
def setup_inputs_ties(rng):
    d = numbers_of(rng)
    e = rng.permutation(N)
    x = d["x"].reshape(N, 8, 16, C, 4)
    for r in range(N):
        k = rng.permutation(C) % 3
        if r == e[0]: k = np.zeros(C, int)
        elif r in e[2::2]: k = rng.permutation(3)[np.arange(C) % 3]
        a = x[r][:, :8, :3].copy()
        a[:, :, 2] = 0
        x[r][:, :8] = a[:, :, k]
    x[e[1]] = 0
    u = d["u"].reshape(N, 8, 16, 128, 4)
    u[:, :, 8:, ::16] = 0
    u[:, :, 8:, 1::16] = 0
    t = mixed(rng)
    t[e[2]] = np.arange(C)
    t[e[3]] = t[e[3], :1].copy()
    return {"x": x.reshape(N, 128, 4 * C), "u": u.reshape(N, 128, 512), "v": d["v"], "link": links(t), **weights(rng, range(8))}
def setup_inputs_near(rng):
    d = numbers_of(rng)
    x = d["x"].astype(np.float32).reshape(N, 8, 16, C, 4)
    x[:, :, 0] = 0
    x[:, :, 8:] = 0
    u = d["u"].reshape(N, 128, 128, 4)
    u[:, :, ::16] = 0
    u[:, :, 1::16] = 0
    o = rng.permutation(N) % 4
    s = rng.integers(0, 256, (N, 8, C))
    for r in range(N):
        low = 2.0 ** -29 if o[r] == 3 else 2.0 ** -23
        for i in range(2): x[r, :, 8 + i] = ((s[r][:, :, None] >> (4 * i + np.arange(4))) & 1) * np.exp2(4.0 * i + np.arange(4)) * low
        x[r, :, 12, :, 0] = rng.integers(-1, 2, (8, C)) * (2.0 ** -29 if o[r] == 3 else 2.0 ** -20)
        if o[r] == 3: x[r, :, 13, :, 0] = x[r, :, 12, :, 0]
        if o[r] < 2:
            x[r, :, 0, :, 0] = rng.integers(0, 2, (8, C)) * 2.0 - 1.0
            x[r, :, 11, :, 0] = 2.0 ** -10
        if o[r] == 2:
            for g in range(8): x[r, g, 0, rng.permutation(C)[:2], 0] = np.array([1.0, -1.0])
        for g in rng.permutation(8)[:4]: x[r, g, 12, rng.integers(C), 0] = 2.0 ** 29 * rng.choice([-1.0, 1.0])
        k = 1.0 if o[r] == 0 else 2.0 ** -30
        for h in range(0, 128, 16):
            if o[r] < 2:
                u[r, h, h, 0] = k
                u[r, h + 11, h, 0] = k
            if o[r] == 2: u[r, h, h, 0] = 1.0
            u[r, h + 8, h] = k
            u[r, h + 9, h] = k
            u[r, h + 12, h + 1, 0] = 1.125 * 2.0 ** -30 if o[r] == 3 else 2.0 ** -30
            if o[r] == 3: u[r, h + 13, h + 1, 0] = -1.0 * 2.0 ** -30
    return {"x": x.reshape(N, 128, 4 * C).astype(BF), "u": u.reshape(N, 128, 512), "v": d["v"], "link": links(mixed(rng)), **weights(rng, [0, 8, 9, 10, 11, 12, 13, 14, 15])}
def setup_inputs_caps(rng):
    d = numbers_of(rng)
    x = np.zeros((N, 8, 16, C, 4))
    z = (N, 8, 8, C, 4)
    x[:, :, :8] = rng.choice([-1.0, 1.0], z) * (1.0 + (2 * rng.integers(0, 64, z) + 1) * 2.0 ** -7) * np.exp2(-1.0 * rng.integers(8, 15, z))
    x[:, :, 0, :, 0] = rng.choice([1.96875, 1.84375], (N, 8, C))
    s = mixed(rng)
    for i in range(3): x[:, :, 8 + i] = ((s[:, :, :, None] >> (4 * i + np.arange(4))) & 1) * np.exp2(4.0 * i + np.arange(4))
    side = rng.permutation(N) % 2 * 2 - 1
    q = np.argsort(-s * side[:, None, None], axis=2)[:, :, 1::2]
    one = rng.random((N, 8, C)) < 0.5
    a = rng.permutation(8)
    for i in range(6):
        g, t, k = a[i], i % R, 0
        for r in range(N):
            if (r >> t) & 1: one[r, g] = True
            else:
                n = K if i < 3 else K - 1 + 2 * (k % 2)
                k += 1
                one[r, g, q[r, g]] = rng.permutation(P) < n
    one[:, a[6]] = (((np.arange(N) >> (R - 1)) & 1) == 1)[:, None]
    one[:, a[7]] = ((np.arange(N) & 1) == 1)[:, None]
    x[:, :, 12, :, 0] = np.where(one, 1.0, -1.0 * rng.integers(0, 2, (N, 8, C)))
    u = d["u"].reshape(N, 128, 128, 4)
    u[:, :, ::16] = 0
    u[:, :, 1::16] = 0
    for r in range(N):
        for h in range(0, 128, 16):
            u[r, h + 8:h + 11, h] = float(side[r])
            u[r, h + 12, h + 1, 0] = 1.0
    return {"x": x.astype(np.float32).reshape(N, 128, 4 * C).astype(BF), "u": u.reshape(N, 128, 512), "v": d["v"], "link": links(mixed(rng)), **weights(rng, range(8, 16))}
def setup_inputs_huge(rng):
    d = numbers_of(rng)
    o = rng.permutation(N)
    c = rng.integers(0, 2, (N, 1, 1, C, 1)) * 2.0 - 1.0
    c[:, :, :, :2] = np.array([1.0, -1.0])[:, None]
    c[o == 1] = -1.0
    c[o == 2] = 1.0
    x = 0.6 + 0.09 * rng.random((N, 8, 16, C, 4))
    x[o == 0] = np.where(rng.random((1, 8, 16, C, 4)) < 0.125, 0.8125, 0.875)
    u = d["u"].reshape(N, 128, 128, 4)
    for i in range(2):
        a = 2.0 ** 29 * (1.0 - 0.1 * rng.random((N, 128, 8, 4)))
        a[o == 0] = 2.0 ** 30 * np.where(rng.random((1, 128, 8, 4)) < 0.03125, 0.875, 1.0)
        turned = (o % 2 == 1) if i else (o == 0) | (o > N // 2)
        for r in range(N):
            if turned[r]: a[r] *= (rng.permutation(8) % 2 * 2.0 - 1.0)[None, :, None]
        u[:, :, i::16] = a.astype(np.float32).astype(BF)
    w = np.zeros((N, 128, 4, 128, 4), np.float32)
    i = np.arange(128)
    for b in range(4): w[:, i, b, i, b] = 1
    return {"x": (2.0 ** 30 * x * c).astype(np.float32).reshape(N, 128, 4 * C).astype(BF), "u": u.reshape(N, 128, 512), "v": d["v"], "link": links(mixed(rng)), **packedw(rng, w.astype(BF))}
def setup_inputs_spread(rng):
    d = setup_inputs(rng)
    d["x"] = wide(rng, N, 128, 4 * C, cols=6)
    return d
def check_inputs(d):
    b = []
    for k in ("x", "u", "v"):
        a = np.abs(d[k].astype(np.float32))
        if not (np.isfinite(a).all() and ((a == 0) | (a >= 2.0 ** -30) & (a <= 2.0 ** 30)).all()): b.append("a value of " + k)
    none, least, most = [emit(mx_ref.quantize(np.full((128, 16), k, np.float32).astype(BF)))[1][0, 0] for k in (0.0, 2.0 ** -30, 2.0 ** 30)]
    for r in range(N):
        if (np.sort(gentries(d["link"][r]), axis=1) != np.arange(C)).any(): b.append("link: a group's entries are no permutation")
        if ((d["wc"][r] == 0x7F) | (d["wc"][r] == 0xFF)).any(): b.append("wc: a code that is no number")
        s = mx_ref.live(d["ws"][r])
        if ((s != none) & ((s < least) | (s > most))).any(): b.append("ws: a scale out of range")
    return b
def at(a, e):
    return np.take_along_axis(a, e, axis=1)
def reference(x, u, v, link, wc, ws):
    qu = [mx_ref.quantize(u[r]) for r in range(N)]
    lay = [pk(wc[r], ws[r]) for r in range(N)]
    now = [x[r] for r in range(N)]
    to = [gentries(link[r]) for r in range(N)]
    for t in range(R):
        d = 2 ** t
        own, order, bit = [], [], []
        for r in range(N):
            q = mx_ref.quantize(now[r])
            own.append(decode(q))
            s = mx_ref.matmul(qu[r], q)
            order.append(np.argsort(-(s[::16] + np.float32(0.0)), axis=1, kind="stable"))
            bit.append(s[1::16] > 0)
        kept, names, left, places, turned = [], [], [], [], []
        for r in range(N):
            k, q = order[r][:, 0::2], order[r][:, 1::2]
            there = at(to[r], q)
            fails = at(bit[r], q) != at(bit[(r + d) % N], there)
            j = np.argsort(fails.astype(np.int64), axis=1, kind="stable")
            k, q, there = at(k, j), at(q, j), at(there, j)
            h = own[r].astype(BF)
            a = ((gcols(h, k).astype(np.float32) + gcols(h, q).astype(np.float32)) * np.float32(0.5)).astype(BF)
            kept.append(mx_ref.quantize(np.ascontiguousarray(a[:, :4 * K])))
            left.append(mx_ref.quantize(np.ascontiguousarray(a[:, 4 * K:])))
            names.append(there[:, :K])
            places.append(q[:, K:])
            m = np.tile(np.arange(C), (8, 1))
            np.put_along_axis(m, k[:, K:], q[:, K:], axis=1)
            np.put_along_axis(m, q[:, K:], k[:, K:], axis=1)
            turned.append(at(to[r], m))
        to = [at(turned[(r + d) % N], to[r]) for r in range(N)]
        for r in range(N):
            c = (r - d) % N
            slots = join(kept[c], left[r])
            e = np.full((8, C), P)
            np.put_along_axis(e, places[r], np.tile(np.arange(K, P), (8, 1)), axis=1)
            np.put_along_axis(e, names[c], np.tile(np.arange(K), (8, 1)), axis=1)
            made = []
            for b in range(4):
                h = mx_ref.matmul(pick(lay[r], np.arange(128 * b, 128 * b + 128)), slots)
                h = np.concatenate([h, np.zeros((128, 1), np.float32)], axis=1)
                made.append(gpick(h, e) * np.float32(0.03125) + own[r][:, b::4])
            now[r] = tile(made)
    y, lk = np.zeros((N, 128, C), np.float32), np.zeros((N, 8, C), np.float32)
    oc, osc = np.zeros((N, 128, 4 * C), np.uint8), np.zeros((N, 16, C), np.uint8)
    for r in range(N):
        q = mx_ref.quantize(now[r])
        y[r] = mx_ref.matmul(mx_ref.quantize(v[r]), q)
        lk[r] = to[r]
        oc[r], osc[r] = emit(q)
    return {"y": y, "lk": lk, "oc": oc, "osc": osc}

@@ -1,0 +1,442 @@
+from concourse.mybir import dt, AluOpType, ActivationFunctionType
+
+AL, AF = AluOpType, ActivationFunctionType
+NR = 3
+BIG = 1.0e29
+BV = float(2 ** 20)
+TILES = [("fa", [23, 22, 21], 384), ("fb", [20, 19, 18, 17], 320), ("fc", [16, 15, 14, 13], 256),
+         ("fd", [12, 11, 10, 9], 192), ("fe", [8, 7, 6, 5], 128), ("ff", [4, 3, 2, 1], 128)]
+
+SCRATCH, WHERE = {}, {}
+
+
+def _s(names, dtype, where="sbuf", buf=None):
+    buf, n = buf or names[0][0], 0
+    for name, w in names:
+        WHERE[name] = (buf, n, w)
+        if dtype == "codes":
+            WHERE[name + "s"] = (buf + "s", n, w)
+        n += w
+    SCRATCH[buf] = (where, [128, n], "float8_e4m3fn_x4" if dtype == "codes" else dtype)
+    if dtype == "codes":
+        SCRATCH[buf + "s"] = (where, [128, n], "uint8")
+
+
+def _each(text, dtype):
+    for w in text.split():
+        n, c = w.split(":")
+        _s([(n, int(c))], dtype)
+
+
+_each("xt0:1536 xt1:1536 xt2:1536 xt3:1536 fh:1536 ut:512 vt:512 iet:2048 bot:512 zt:512 ak:512 al:512 one:512 sg:384 bt:384 rds:384 "
+      "r0:384 tb:384 w2:768 fl:192 flc:192 junk:4416 rl:384 ra:384 sgl:1104", "bfloat16")
+_s([("r0w", 16), ("tbw", 16), ("cw", 16), ("cv", 16)], "bfloat16", buf="kb")
+_s([(_n, 4 * _w) for _n, _l, _w in TILES], "bfloat16", buf="ft")
+_s([("q" + _n, _w) for _n, _l, _w in TILES], "codes", buf="qf")
+_each("xq:384 uq:128 urs:128 urb:128 vq:128 eq:512 bo:128 wq:512 ql:128", "codes")
+for _t in "012":
+    _each("qk%s:128 vb%s:128" % (_t, _t), "codes")
+    _each(" ".join(_n + _t + ":24" for _n in ("sb", "lb", "sn", "ln", "st", "lt")), "uint16")
+_s([(_n, 16) for _n in ("ks", "ks4", "mbw", "rsw", "t16w", "t4w", "ta", "tn", "cols")], "float32", buf="kw")
+_s([("c4", 192), ("c16", 192), ("fc2", 192), ("fcum", 192)], "float32", buf="cc")
+_s([("kq", 384), ("lqk", 96), ("nmc", 96)], "float32", buf="kn")
+_s([("mc", 384), ("tuc", 384), ("lc", 384)], "float32", buf="sc3")
+_each("kj:36 iota0:384 alt:384 mb:384 rs:384 t16:384 t4:192 m2:384 hs:384 ru:24 kr:72 ow:72 pay:384 sp:384 kqs:192 pp:60 "
+      "fq:768 fl32:384 fn32:384 sl:384 sa:384 val:192 tu:384 tr:384 lr0:384 lr1:384 lr2:384 lr3:384 ys:384", "float32")
+_each("li:24 pi:12 kqi:180", "int32")
+_each("pmo:24 uo16:16 lt16:24 off16:24 rk16:24 n16:12 t4q:48 t4k:48 tqk:6 tll:12", "uint16")
+_s([("p%d" % _b, 512) for _b in range(8)], "float32", "psum", "ps")
+
+SEMAPHORES = "v a p gc ls dx du dw ds dv dl oy oz ok oc_ o0 o1 o2 o3 rb0 rb1 rb2 rn0 rn1 rn2 rc0 rc1 rc2 rt0 rt1 rt2".split()
+
+
+def R(name, lo=0, hi=None, step=1, bit=None):
+    buf, at, w = WHERE[name]
+    return (buf, at + lo, at + (w if hi is None else hi), step, bit)
+
+
+def IND(win, off):
+    return ("ind", win, off)
+
+
+def flat(rs):
+    return [x for r in rs for x in (r[1:] if r[0] == "ind" else (r,))]
+
+
+def meets(x, y):
+    if x[1] <= y[0] or y[1] <= x[0]:
+        return False
+    return not (x[2] == y[2] and x[2] > 1 and (x[0] - y[0]) % x[2])
+
+
+def rank_program(g, core, T, topo):
+    rank = T.rank_of(core)
+    if rank is None:
+        return
+    ENG = {"v": g.vector, "a": g.scalar, "p": g.tensor, "g": g, "s": g.sync}
+    CNT = {"v": 0, "a": 0, "p": 0, "gc": 0, "ls": 0}
+    know = {q: {} for q in ENG}
+    clocks, writes, reads, seq = {}, {}, {}, [0]
+
+    def ap(r):
+        if r[0] == "ind":
+            return ap(r[1]).indirect(ap(r[2]))
+        n, lo, hi, st, bit = r
+        w = T[n][:, lo:hi] if st == 1 else T[n][:, lo:hi:st]
+        return w if bit is None else w.bitcast(dt.uint8 if bit == "u8" else dt.uint32)
+
+    def hold(q, rd, wr, loose=False):
+        need = {}
+        for r in flat(rd):
+            for x, ev, own in writes.get(r[0], []):
+                if meets(x, r[1:4]):
+                    need[ev] = 1
+        for r in flat(wr):
+            for x, ev, own in writes.get(r[0], []) + reads.get(r[0], []):
+                if meets(x, r[1:4]) and not (loose and own == q):
+                    need[ev] = 1
+        for ev in sorted(need, key=lambda e: -clocks[e]["#"]):
+            if know[q].get(ev[0], 0) < ev[1]:
+                ENG[q].wait_ge(T.sem[ev[0]], ev[1])
+                for k, n in clocks[ev].items():
+                    if know[q].get(k, 0) < n:
+                        know[q][k] = n
+
+    def done(q, rd, wr, ev):
+        c = dict(know[q])
+        seq[0] += 1
+        c.update({ev[0]: max(c.get(ev[0], 0), ev[1]), "#": seq[0]})
+        clocks[ev] = c
+        for r in flat(rd):
+            reads.setdefault(r[0], []).append((r[1:4], ev, q))
+        for r in flat(wr):
+            x = r[1:4]
+            if x[2] == 1:
+                for d in (writes, reads):
+                    d[r[0]] = [e for e in d.get(r[0], []) if not (x[0] <= e[0][0] and e[0][1] <= x[1])]
+            writes.setdefault(r[0], []).append((x, ev, q))
+
+    def op(q, rd, wr, call, loose=False):
+        hold(q, rd, wr, loose)
+        sem = "gc" if q == "g" else q
+        CNT[sem] += 1
+        call().then_inc(T.sem[sem], 1)
+        done(q, rd, wr, (sem, CNT[sem]))
+
+    def tt(o, a, b, f):
+        op("v", [a, b], [o], lambda: g.vector.tensor_tensor(ap(o), ap(a), ap(b), f))
+
+    def ts(o, a, s1, f1, s2=None, f2=None):
+        rd = [a] + [s for s in (s1, s2) if isinstance(s, tuple)]
+        x1, x2 = [ap(s) if isinstance(s, tuple) else s for s in (s1, s2)]
+        op("v", rd, [o], lambda: g.vector.tensor_scalar(ap(o), ap(a), x1, x2, f1, *([f2] if f2 is not None else [])))
+
+    def cp(o, a):
+        op("v", [a], [o], lambda: g.vector.tensor_copy(ap(o), ap(a)))
+
+    def scan(o, d0, d1, f0=AL.add, f1=AL.max):
+        op("v", [d0, d1], [o], lambda: g.vector.tensor_tensor_scan(ap(o), ap(d0), ap(d1), 0.0, f0, f1))
+
+    def fill(o, x):
+        op("v", [], [o], lambda: g.vector.memset(ap(o), x))
+
+    def quant(qn, i):
+        a, b = R(qn), R(qn + "s")
+        op("v", [i], [a, b], lambda: g.vector.quantize_mx(ap(a), ap(b), ap(i)))
+
+    def act(o, i, f=AF.Copy, scale=None, accum=None, bias=None):
+        kw = {} if scale is None else {"scale": scale}
+        if bias is not None:
+            kw["bias"] = ap(bias)
+        if accum is not None:
+            kw["accum_out"] = ap(accum)
+        op("a", [i] + ([bias] if bias else []), [o] + ([accum] if accum else []), lambda: g.scalar.activation(ap(o), ap(i), f, **kw))
+
+    def mm(o, wn, wlo, xn, n, start=True, stop=True, lo=0):
+        w, ws = R(wn, wlo, wlo + 128), R(wn + "s", wlo, wlo + 128)
+        x, xs = R(xn, lo, lo + n), R(xn + "s", lo, lo + n)
+        op("p", [w, ws, x, xs], [o], lambda: g.tensor.matmul_mx(ap(o), ap(w), ap(ws), ap(x), ap(xs), start, stop), loose=not start)
+
+    def iota(o, pat, cm=0, **kw):
+        op("g", [], [o], lambda: g.iota(ap(o), pat, 0, cm, **kw))
+
+    def asel(o, i, pat, f, base, cm):
+        op("g", [i], [o], lambda: g.affine_select(ap(o), ap(i), pat, f, 0.0, base, cm))
+
+    def dma(q, o, i, rd, wr, sem):
+        hold(q, rd, wr)
+        ENG[q].dma_start(o, i).then_inc(T.sem[sem], 16)
+        done(q, rd, wr, (sem, 16))
+
+    def send(to, rsem, *pairs):
+        c = T.cores[to % 8]
+        adr, ne = topo.addr(c), len(topo.engines(core, c))
+        for dst, src in pairs:
+            hold("g", [src], [])
+            CNT["ls"] += ne
+            g.remote_dma(ap(dst), ap(src), T.sem[rsem], T.sem["ls"], adr[1], adr[0], topo.mask(core, c))
+        seq[0] += 1
+        ev = (rsem, ne * len(pairs))
+        clocks[ev] = {ev[0]: ev[1], "#": seq[0]}
+        for r, src in pairs:
+            writes.setdefault(r[0], []).append((r[1:4], ev, "far"))
+
+    dma("s", ap(R("xt0")), T.x[:, :], [], [R("xt0")], "dx")
+    dma("a", ap(R("ut")), T.u[:, :], [], [R("ut")], "du")
+    dma("a", ap(R("li")), T.link[:, :], [], [R("li")], "dl")
+    dma("s", ap(R("wq", bit="u8")), T.wc[:, :], [], [R("wq")], "dw")
+    dma("s", ap(R("wqs")), T.ws[:, :], [], [R("wqs")], "ds")
+    dma("s", ap(R("vt")), T.v[:, :], [], [R("vt")], "dv")
+
+    KCB, JB, UO = R("kj", 0, 24), R("kj", 24, 36), R("pi", 4, 12)
+    fine = {"allow_small_or_imprecise_dtypes": True}
+    iota(R("pi", 0, 1), [[1, 1]], 1)
+    iota(R("ks"), [[1, 16]], **fine)
+    iota(UO, [[16, 8]])
+    iota(KCB, [[16, 24]], **fine)
+    iota(JB, [[16, 12]], **fine)
+    iota(R("ks4"), [[0, 4], [1, 4]], **fine)
+    iota(R("iota0"), [[1, 384]], **fine)
+    iota(R("alt"), [[0, 192], [1024, 2]], **fine)
+
+    col = {n: R("cols", i, i + 1) for i, n in enumerate(("pm", "pm1", "p4", "p41", "b16", "b4", "bb", "thr", "k2", "pb4", "pbn", "z"))}
+    fill(R("one"), 1.0)
+    ts(R("pi", 1, 2), R("pi", 0, 1), 15, AL.bitwise_and)
+    ts(R("pi", 2, 3), R("pi", 0, 1), 2, AL.logical_shift_right, 3, AL.bitwise_and)
+    ts(R("pi", 3, 4), R("pi", 0, 1), 3, AL.bitwise_and)
+    fill(R("ow", 0, 24), 0.0)
+    cp(col["pm"], R("pi", 1, 2))
+    cp(col["p4"], R("pi", 2, 3))
+    ts(col["pm1"], R("pi", 1, 2), 1.0, AL.add)
+    ts(col["p41"], R("pi", 2, 3), 1.0, AL.add)
+    ts(col["b16"], col["pm"], 14.5, AL.is_lt, BV, AL.mult)
+    ts(col["b4"], col["p4"], 2.5, AL.is_lt, BV, AL.mult)
+    ts(R("pmo"), R("ow", 0, 24), col["pm"], AL.add)
+    for b in range(4):
+        act(R("iet", 512 * b, 512 * b + 512), R("one"), scale=0.0)
+    asel(R("bot"), R("one"), [[-16, 8], [0, 64]], AL.is_ge, 0, 1)
+    asel(R("bot"), R("bot"), [[16, 8], [0, 64]], AL.is_ge, 15, -1)
+    for b in range(4):
+        asel(R("iet", 512 * b + b, 512 * b + 512, 4), R("one", 0, 128), [[-1, 128]], AL.is_equal, 0, 1)
+    ts(R("ta"), R("ks"), col["pm"], AL.is_equal, 2 * BIG, AL.mult)
+    ts(R("rsw"), R("ks"), 0.5, AL.is_gt, 2 * BIG, AL.mult)
+    ts(R("r0w"), R("ks"), 0.5, AL.is_gt)
+    ts(R("mbw"), R("ta"), -BIG, AL.add)
+    ts(R("rsw"), R("rsw"), -BIG, AL.add)
+    act(R("mb"), IND(R("mbw"), R("pmo")))
+    act(R("rs"), IND(R("rsw"), R("pmo")))
+    ts(R("ta"), R("ks"), col["pm"], AL.is_equal, -2 * BV, AL.mult)
+    ts(R("tn"), R("ks"), col["pm1"], AL.is_equal, BV, AL.mult)
+    ts(R("t16w"), R("ks"), 0.5, AL.is_lt, -8 * BV, AL.mult)
+    tt(R("ta"), R("ta"), R("tn"), AL.add)
+    ts(R("uo16", 0, 8), UO, 0.0, AL.add)
+    ts(R("uo16", 8, 16), UO, 1.0, AL.add)
+    tt(R("t16w"), R("t16w"), R("ta"), AL.add)
+    ts(col["bb"], col["b16"], 2.0 ** -18, AL.mult)
+    ts(col["thr"], col["b16"], 2.0 ** -18, AL.mult, 0.5, AL.add)
+    ts(R("tbw"), R("t16w"), 2.0 ** -18, AL.mult)
+    act(R("tb"), IND(R("tbw"), R("pmo")))
+    act(R("r0"), IND(R("r0w"), R("pmo")))
+    act(R("t16"), IND(R("t16w"), R("pmo")))
+    for n, ls, w in TILES[:2]:
+        fill(R(n, 64 * ls[-1], 4 * w), 0.0)
+    fill(R("ru", 0, 1), 0.0)
+    quant("uq", R("ut"))
+    for n, lo in (("urs", 0), ("urb", 8)):
+        cp(R(n, bit="u32"), IND(R("uq", bit="u32"), R("uo16", lo, lo + 8)))
+        cp(R(n + "s"), IND(R("uqs"), R("uo16", lo, lo + 8)))
+    fill(R("zt"), 0.0)
+    fill(R("ak", 384, 512), 0.0)
+    fill(R("al", 384, 512), 0.0)
+
+    xin = "xt0"
+    for t in range(NR):
+        d = 2 ** t
+        xn, lr, qk, vb = "xt%d" % (t + 1), "lr%d" % t, "qk%d" % t, "vb%d" % t
+        sb, lb, sn, ln, st, lt = ["%s%d" % (n, t) for n in ("sb", "lb", "sn", "ln", "st", "lt")]
+        P = [R("p%d" % b, 0, 384) for b in range(8)]
+        quant("xq", R(xin))
+        mm(P[0], "urs", 0, "xq", 384)
+        mm(P[1], "urb", 0, "xq", 384)
+        mm(P[7], "urs", 0, "xq", 384)
+        if t:
+            for b in range(4):
+                mm(P[2 + b], "eq", 128 * b, "xq", 384)
+            scan(R("lc"), R("t16"), R(lr))
+        else:
+            for k in range(NR):
+                quant("vb%d" % k, R("zt"))
+        act(R("sg"), P[1], AF.Sign)
+        tt(R("m2"), P[0], R("mb"), AL.min)
+        if t:
+            ts(R("ow", 48, 72), R("lc", 15, 384, 16), col["b16"], AL.subtract)
+            ts(R("lt16"), R("lc", 15, 384, 16), col["b16"], AL.subtract)
+        else:
+            cp(R("lt16"), R("li"))
+            cp(R("ow", 48, 72), R("li"))
+        scan(R("hs"), R("rs"), R("m2"), AL.min)
+        scan(R("bt"), R("tb"), R("sg"))
+        tt(R("fa", 3, 1536, 4), P[0], R("hs"), AL.is_le)
+        ts(R(sb), R("bt", 15, 384, 16), col["thr"], AL.is_gt)
+        send(rank - d, "rb%d" % t, (R(lb), R(sb)))
+        for n, ls, w in TILES[2:] if t == 0 else []:
+            iota(R(n, 64 * ls[-1], 4 * w), [[0, 4 * w - 64 * ls[-1]]], **fine)
+        if t:
+            for b in range(2):
+                act(R(xn, b, 1536, 4), P[2 + b])
+        for k, c in enumerate((23, 22, 21)):
+            act(R("sgl", 368 * k, 368 * k + 16 * c), R("p7", 0, 16 * c), AF.Sign, scale=-1.0, bias=R("hs", 16 * c + 15, 16 * c + 16))
+        ju = [0]
+
+        def layer(fn, k, c, by=None):
+            n = 16 * c
+            if by is None:
+                ts(R(fn, k, 4 * n, 4), R("p0", 0, n), R("hs", n + 15, n + 16), AL.is_lt)
+            else:
+                ts(R(fn, k, 4 * n, 4), R("sgl", 368 * by, 368 * by + n), 0.5, AL.is_gt)
+            act(R("junk", ju[0], ju[0] + n), R(fn, k, 4 * n, 4), accum=R("ru", c, c + 1))
+            ju[0] += n
+
+        for k in range(4):
+            layer("fb", k, 20 - k)
+        for k in range(3):
+            layer("fa", k, 23 - k, k)
+        for ti, (fn, ls, w) in enumerate(TILES):
+            todo = [(TILES[ti + 1][0], k, c) for k, c in enumerate(TILES[ti + 1][1]) if c < 17] if ti < 5 else []
+            for x in todo[:1]:
+                layer(*x)
+            if ti == 0:
+                if t == 0:
+                    act(R(lr), IND(R("iota0"), R("lt16")))
+                    quant("bo", R("bot"))
+                    ts(KCB, KCB, 15.0, AL.add, col["pm"], AL.subtract)
+                    ts(JB, JB, col["pm"], AL.add, col["b16"], AL.add)
+                    ts(col["k2"], col["b16"], -1.0, AL.mult, 191.0, AL.add)
+                    ts(KCB, KCB, col["b16"], AL.subtract)
+                scan(R("rds"), R("r0"), R("fa", 3, 1536, 4), AL.mult, AL.add)
+            if ti == 5:
+                cp(R("off16"), R("ow", 24, 48))
+            quant("q" + fn, R(fn))
+            mm(R("p6", 0, w), "bo", 0, "q" + fn, w, start=ti == 0, stop=ti == 5)
+            if ti == 0:
+                tt(R("kr", 0, 24), KCB, R("rds", 15, 384, 16), AL.subtract)
+                if t == 0:
+                    ts(R("ta"), R("ks4"), col["p4"], AL.is_equal, -2 * BV, AL.mult)
+                    ts(R("tn"), R("ks4"), col["p41"], AL.is_equal, BV, AL.mult)
+                    ts(R("t4w"), R("ks4"), 0.5, AL.is_lt, -8 * BV, AL.mult)
+                    tt(R("ta"), R("ta"), R("tn"), AL.add)
+                    cp(col["pb4"], R("pi", 3, 4))
+                    ts(col["z"], col["b4"], -4.0, AL.mult)
+                    tt(R("t4w"), R("t4w"), R("ta"), AL.add)
+                    tt(col["pbn"], col["z"], col["pb4"], AL.add)
+                    ts(R("cw"), R("ks"), 512.0, AL.mult)
+                    ts(R("cv"), R("ks"), -512.0, AL.mult, 512.0, AL.add)
+                    act(R("t4"), IND(R("t4w"), R("pmo", 0, 12)))
+            if ti == 2:
+                act(R("w2", 0, 384), IND(R("cw"), R(lb)))
+                act(R("w2", 384, 768), IND(R("cv"), R(lb)))
+                ts(R("ow", 0, 24), R("bt", 15, 384, 16), col["thr"], AL.is_gt, 384.0, AL.mult)
+            if ti == 3:
+                tt(R("ow", 24, 48), R("ow", 0, 24), R("ow", 48, 72), AL.add)
+            for x in todo[1:]:
+                layer(*x)
+        if t == 0:
+            quant("eq", R("iet"))
+            for b in range(4):
+                mm(P[2 + b], "eq", 128 * b, "xq", 384)
+        tt(R("pay"), IND(R("w2"), R("off16")), R("iota0"), AL.add)
+        scan(R("mc"), R("t16"), P[6])
+        tt(R("kr", 24, 48), R("kr", 0, 24), R("ru"), AL.subtract)
+        tt(R("kr", 48, 72), R("mc", 15, 384, 16), R("kr", 24, 48), AL.add)
+        cp(R("rk16"), R("kr", 48, 72))
+        cp(IND(R("sp"), R("rk16")), R("pay"))
+        for b in range(2 if t else 0, 4):
+            act(R(xn, b, 1536, 4), P[2 + b])
+        act(R("fh"), R(xn), scale=0.5)
+
+        def pairs(a, b):
+            scan(R("kq", a, b), R("alt", a, b), R("sp", a, b), AL.mult, AL.add)
+
+        flt, pp1, pp2, pp3, nn = [R("pp", 12 * i, 12 * i + 12) for i in range(5)]
+        ts(R("fl"), R("sp", 1, 384, 2), 511.5, AL.is_gt)
+        pairs(0, 128)
+        scan(R("fcum"), R("fl"), R("fl"))
+        scan(R("flc"), R("tb", 0, 192), R("fl"))
+        scan(R("fc2"), R("t16", 0, 192), R("fcum"))
+        ts(flt, R("flc", 15, 192, 16), col["bb"], AL.subtract)
+        ts(pp2, R("fc2", 15, 192, 16), R("fcum", 191, 192), AL.subtract, col["k2"], AL.add)
+        tt(pp1, JB, R("fc2", 15, 192, 16), AL.subtract)
+        tt(pp3, pp2, flt, AL.mult)
+        pairs(128, 256)
+        tt(nn, pp1, pp3, AL.max)
+        pairs(256, 384)
+        cp(R("n16"), nn)
+        cp(IND(R("kqs"), R("n16")), R("kq", 1, 384, 2))
+        scan(R("c4"), R("t4"), R("kqs"))
+        scan(R("c16"), R("t16", 0, 192), R("kqs"))
+        ts(R("kqi", 0, 48), R("c4", 3, 192, 4), col["b4"], AL.subtract)
+        ts(R("kqi", 48, 60), R("c16", 15, 192, 16), col["b16"], AL.subtract)
+        ts(R("kqi", 60, 108), R("kqi", 0, 48), 511, AL.bitwise_and)
+        ts(R("kqi", 120, 168), R("kqi", 0, 48), 10, AL.logical_shift_right, 511, AL.bitwise_and)
+        ts(R("t4q"), R("kqi", 60, 108), 4.0, AL.mult, col["pb4"], AL.add)
+        ts(R("kqi", 108, 120), R("kqi", 48, 60), 511, AL.bitwise_and)
+        ts(R("t4k"), R("kqi", 120, 168), 4.0, AL.mult, col["pb4"], AL.add)
+        cp(R("tqk"), R("kqi", 108, 114))
+        ts(R("kqi", 168, 180), R("kqi", 48, 60), 10, AL.logical_shift_right, 511, AL.bitwise_and)
+        act(R("fq", 0, 192), IND(R("fh"), R("t4q", 0, 12)))
+        act(R("fq", 192, 384), IND(R("fh"), R("t4q", 12, 24)))
+        act(R("fq", 384, 768), IND(R("fh"), R("t4q", 24, 48)))
+        cp(R("lqk"), IND(R(lr), R("tqk")))
+        tt(R("ak", 0, 192), IND(R("fh"), R("t4k", 0, 12)), R("fq", 0, 192), AL.add)
+        scan(R("nmc"), R("t4", 0, 96), R("lqk"))
+        cp(R("tll", 0, 6), R("kqi", 114, 120))
+        ts(R(sn), R("nmc", 3, 96, 4), 4.0, AL.mult, col["pbn"], AL.add)
+        send(rank + d, "rn%d" % t, (R(ln), R(sn)))
+        tt(R("ak", 192, 384), IND(R("fh"), R("t4k", 12, 24)), R("fq", 192, 384), AL.add)
+        cp(R("tll", 6, 12), R("kqi", 174, 180))
+        quant(qk, R("ak"))
+        send(rank + d, "rc%d" % t, (R(vb, 0, 96, 1, "u8"), R(qk, 0, 96, 1, "u8")), (R(vb + "s", 0, 96), R(qk + "s", 0, 96)))
+        tt(R("al", 0, 384), IND(R("fh"), R("t4k", 24, 48)), R("fq", 384, 768), AL.add)
+        quant("ql", R("al"))
+        act(R("val", 0, 96), IND(R(lr), R("tll", 6, 12)))
+        act(R("val", 96, 192), IND(R(lr), R("tll", 0, 6)))
+        act(R("tu"), R(lr))
+        act(R("fl32"), R("fq", 384, 768), scale=64.0)
+        left = ("p0", "p1", "p6", "p7")
+        for b in range(4):
+            mm(R(left[b], 0, 128), "wq", 128 * b, "ql", 128)
+        cp(IND(R("tu"), R("tll")), R("val"))
+        for b in range(4):
+            tt(R("sl", b, 384, 4), R(left[b], 0, 96), R("fl32", b, 384, 4), AL.add)
+        act(R("rl"), R("sl"), scale=0.03125)
+        scan(R("tuc"), R("t16"), R("tu"))
+        if t == 0:
+            quant("vq", R("vt"))
+        ts(R(st), R("tuc", 15, 384, 16), col["b16"], AL.subtract)
+        send(rank - d, "rt%d" % t, (R(lt), R(st)))
+        cp(IND(R(xn), R("t4q", 24, 48)), R("rl"))
+        act(R("fn32"), IND(R("fh"), R(ln)), scale=64.0)
+        for b in range(4):
+            mm(R("p%d" % (2 + b), 0, 128), "wq", 128 * b, vb, 128)
+        for b in range(4):
+            tt(R("sa", b, 384, 4), R("p%d" % (2 + b), 0, 96), R("fn32", b, 384, 4), AL.add)
+            act(R("ra", b, 384, 4), R("sa", b, 384, 4), scale=0.03125)
+        act(R("tr"), IND(R("iota0"), R(lt)))
+        act(R("lr%d" % (t + 1)), IND(R("tr"), R("lt16")))
+        cp(IND(R(xn), R(ln)), R("ra"))
+        xin = xn
+    quant("xq", R(xin))
+    for b in range(2):
+        mm(R("p%d" % b, 0, 192), "vq", 0, "xq", 192, lo=192 * b)
+    dma("s", T.oc[:, :], ap(R("xq", bit="u8")), [R("xq")], [], "oc_")
+    for k in range(4):
+        dma("s", T.osc[4 * k:4 * k + 4, :], T.xqs[32 * k:32 * k + 4, 0:384], [R("xqs")], [], "o%d" % k)
+    dma("s", T.lk[:, :], T.lr3[0:128:16, :], [R("lr3")], [], "ok")
+    act(R("ys", 0, 192), R("p0", 0, 192))
+    dma("a", T.y[:, 0:192], ap(R("ys", 0, 192)), [R("ys", 0, 192)], [], "oy")
+    cp(R("ys", 192, 384), R("p1", 0, 192))
+    dma("s", T.y[:, 192:384], ap(R("ys", 192, 384)), [R("ys", 192, 384)], [], "oz")
+    for s in ("oc_", "o0", "o1", "o2", "o3", "oy", "oz", "ok"):
+        g.wait_ge(T.sem[s], 16)
+    for s in ("v", "a", "p", "gc", "ls"):
+        g.wait_ge(T.sem[s], CNT[s])

@@ -1,11 +1,16 @@
+from concourse.bass import DstId, RemoteDMATransfer
 from concourse.mybir import dt, AluOpType, ActivationFunctionType
 
 AL, AF = AluOpType, ActivationFunctionType
 NR = 3
-BIG = 1.0e29
-BV = float(2 ** 20)
+BIG = 2.0 ** 90
+BV = 2048.0
+NS = 7
+NV = 23 - NS
+XA = 176
 TILES = [("fa", [23, 22, 21], 384), ("fb", [20, 19, 18, 17], 320), ("fc", [16, 15, 14, 13], 256),
-         ("fd", [12, 11, 10, 9], 192), ("fe", [8, 7, 6, 5], 128), ("ff", [4, 3, 2, 1], 128)]
+         ("fd", [12, 11, 10, 9], 192), ("fe", [8, 7, 6, 5], 128), ("ff", [4, 3, 2, 1], 64)]
+LANE = {_c: (_n, _k) for _n, _l, _w in TILES for _k, _c in enumerate(_l)}
 
 SCRATCH, WHERE = {}, {}
 
@@ -17,8 +22,10 @@ def _s(names, dtype, where="sbuf", buf=None):
         if dtype == "codes":
             WHERE[name + "s"] = (buf + "s", n, w)
         n += w
+    WHERE.setdefault(buf, (buf, 0, n))
     SCRATCH[buf] = (where, [128, n], "float8_e4m3fn_x4" if dtype == "codes" else dtype)
     if dtype == "codes":
+        WHERE.setdefault(buf + "s", (buf + "s", 0, n))
         SCRATCH[buf + "s"] = (where, [128, n], "uint8")
 
 
@@ -28,26 +35,29 @@ def _each(text, dtype):
         _s([(n, int(c))], dtype)
 
 
-_each("xt0:1536 xt1:1536 xt2:1536 xt3:1536 fh:1536 ut:512 vt:512 iet:2048 bot:512 zt:512 ak:512 al:512 one:512 sg:384 bt:384 rds:384 "
-      "r0:384 tb:384 w2:768 fl:192 flc:192 junk:4416 rl:384 ra:384 sgl:1104", "bfloat16")
-_s([("r0w", 16), ("tbw", 16), ("cw", 16), ("cv", 16)], "bfloat16", buf="kb")
+_each("xt0:1536 xt1:1536 xt2:1536 xt3:1536 ut:512 vt:512 iet:2048 bot:512 zt:512 ak:512 al:512 one:128 sg:384 bt:384 rds:384 "
+      "tw:384 twc:384 sgl:3072 jk:2176", "bfloat16")
+_s([("k16", 384), ("mb", 384), ("rs", 384), ("r0", 384), ("tb", 384), ("t16", 384), ("t4", 384), ("alt", 384), ("mn", 192)], "bfloat16", buf="kb")
+_s([("fl", 192), ("flc", 192), ("fcum", 192), ("fc2", 192)], "bfloat16", buf="fs")
+_s([("fh", 1536), ("rl", 384), ("ra", 384)], "bfloat16", buf="fw")
 _s([(_n, 4 * _w) for _n, _l, _w in TILES], "bfloat16", buf="ft")
-_s([("q" + _n, _w) for _n, _l, _w in TILES], "codes", buf="qf")
+_s([("q" + _n, _w) for _n, _l, _w in TILES] + [("qz", 64)], "codes", buf="qf")
 _each("xq:384 uq:128 urs:128 urb:128 vq:128 eq:512 bo:128 wq:512 ql:128", "codes")
 for _t in "012":
     _each("qk%s:128 vb%s:128" % (_t, _t), "codes")
-    _each(" ".join(_n + _t + ":24" for _n in ("sb", "lb", "sn", "ln", "st", "lt")), "uint16")
-_s([(_n, 16) for _n in ("ks", "ks4", "mbw", "rsw", "t16w", "t4w", "ta", "tn", "cols")], "float32", buf="kw")
-_s([("c4", 192), ("c16", 192), ("fc2", 192), ("fcum", 192)], "float32", buf="cc")
-_s([("kq", 384), ("lqk", 96), ("nmc", 96)], "float32", buf="kn")
-_s([("mc", 384), ("tuc", 384), ("lc", 384)], "float32", buf="sc3")
-_each("kj:36 iota0:384 alt:384 mb:384 rs:384 t16:384 t4:192 m2:384 hs:384 ru:24 kr:72 ow:72 pay:384 sp:384 kqs:192 pp:60 "
-      "fq:768 fl32:384 fn32:384 sl:384 sa:384 val:192 tu:384 tr:384 lr0:384 lr1:384 lr2:384 lr3:384 ys:384", "float32")
-_each("li:24 pi:12 kqi:180", "int32")
-_each("pmo:24 uo16:16 lt16:24 off16:24 rk16:24 n16:12 t4q:48 t4k:48 tqk:6 tll:12", "uint16")
+    _each("sn%s:32 ln%s:32 st%s:24 lp%s:24 lo%s:24" % (_t, _t, _t, _t, _t), "uint16")
+    _each("sb%s:24 lb%s:24" % (_t, _t), "float32")
+_each("lo3:24", "uint16")
+_s([(_n, 16) for _n in ("ks", "ks4", "t16w", "t4w", "ta", "tn", "bw")] + [("cols", 24), ("kcb", 24), ("jc", 24), ("jb", 12), ("bi", 32)], "float32", buf="kw")
+_s([("c4", 192), ("c16", 192), ("kq", 384), ("lqk", 96), ("nm4", 96), ("nm16", 96)], "float32", buf="cc")
+_s([("mc", 384), ("nl", 384), ("nlc", 384), ("ec", 384)], "float32", buf="sc3")
+_each("iota0:576 pw:1152 m2:384 hs:384 ru:24 kr:72 ow:24 pay:384 sp:384 spa:384 kqs:192 pp:60 "
+      "fq:768 fl32:384 fn32:384 sl:384 sa:384 val:192 tu:384 ew:384 lr:384 lr3:384 ys:384", "float32")
+_each("li:24 pi:12 kqi:108", "int32")
+_each("pmo:24 uo16:16 bo16:32 off16:24 rk16:24 n16:12 t4q:48 t4k:48 q16:18 e4:96", "uint16")
 _s([("p%d" % _b, 512) for _b in range(8)], "float32", "psum", "ps")
 
-SEMAPHORES = "v a p gc ls dx du dw ds dv dl oy oz ok oc_ o0 o1 o2 o3 rb0 rb1 rb2 rn0 rn1 rn2 rc0 rc1 rc2 rt0 rt1 rt2".split()
+SEMAPHORES = ("v a p gc ls dx dx2 du dw ds dv dl oy oz ok oc_ oc2 o0 o1 o2 o3 rb0 rb1 rb2 rn0 rn1 rn2 rc0 rc1 rc2 rl0 rt0 rt1 rt2").split()
 
 
 def R(name, lo=0, hi=None, step=1, bit=None):
@@ -60,7 +70,8 @@ def IND(win, off):
 
 
 def flat(rs):
-    return [x for r in rs for x in (r[1:] if r[0] == "ind" else (r,))]
+    out = [x for r in rs for x in (r[1:] if r[0] == "ind" else (r,))]
+    return [(x[0], x[1] // 512 * 512, x[1] // 512 * 512 + 512, 1, None) if x[0] == "ps" else x for x in out]
 
 
 def meets(x, y):
@@ -90,6 +101,9 @@ def rank_program(g, core, T, topo):
         for r in flat(rd):
             for x, ev, own in writes.get(r[0], []):
                 if meets(x, r[1:4]):
+                    need[ev] = 1
+            for x, ev, own in reads.get(r[0], []) if r[0] == "ps" else []:
+                if own != q and meets(x, r[1:4]):
                     need[ev] = 1
         for r in flat(wr):
             for x, ev, own in writes.get(r[0], []) + reads.get(r[0], []):
@@ -132,16 +146,17 @@ def rank_program(g, core, T, topo):
         op("v", rd, [o], lambda: g.vector.tensor_scalar(ap(o), ap(a), x1, x2, f1, *([f2] if f2 is not None else [])))
 
     def cp(o, a):
-        op("v", [a], [o], lambda: g.vector.tensor_copy(ap(o), ap(a)))
+        rd, wr = ([a, o[2]], [o[1]]) if o[0] == "ind" else ([a], [o])
+        op("v", rd, wr, lambda: g.vector.tensor_copy(ap(o), ap(a)))
 
-    def scan(o, d0, d1, f0=AL.add, f1=AL.max):
-        op("v", [d0, d1], [o], lambda: g.vector.tensor_tensor_scan(ap(o), ap(d0), ap(d1), 0.0, f0, f1))
+    def scan(o, d0, d1, f0=AL.add, f1=AL.max, first=0.0):
+        op("v", [d0, d1], [o], lambda: g.vector.tensor_tensor_scan(ap(o), ap(d0), ap(d1), first, f0, f1))
 
     def fill(o, x):
         op("v", [], [o], lambda: g.vector.memset(ap(o), x))
 
-    def quant(qn, i):
-        a, b = R(qn), R(qn + "s")
+    def quant(qn, i, lo=0, hi=None):
+        a, b = R(qn, lo, hi), R(qn + "s", lo, hi)
         op("v", [i], [a, b], lambda: g.vector.quantize_mx(ap(a), ap(b), ap(i)))
 
     def act(o, i, f=AF.Copy, scale=None, accum=None, bias=None):
@@ -157,8 +172,8 @@ def rank_program(g, core, T, topo):
         x, xs = R(xn, lo, lo + n), R(xn + "s", lo, lo + n)
         op("p", [w, ws, x, xs], [o], lambda: g.tensor.matmul_mx(ap(o), ap(w), ap(ws), ap(x), ap(xs), start, stop), loose=not start)
 
-    def iota(o, pat, cm=0, **kw):
-        op("g", [], [o], lambda: g.iota(ap(o), pat, 0, cm, **kw))
+    def iota(o, pat, cm=0, base=0, **kw):
+        op("g", [], [o], lambda: g.iota(ap(o), pat, base, cm, **kw))
 
     def asel(o, i, pat, f, base, cm):
         op("g", [i], [o], lambda: g.affine_select(ap(o), ap(i), pat, f, 0.0, base, cm))
@@ -168,6 +183,12 @@ def rank_program(g, core, T, topo):
         ENG[q].dma_start(o, i).then_inc(T.sem[sem], 16)
         done(q, rd, wr, (sem, 16))
 
+    def landed(rsem, n, places):
+        seq[0] += 1
+        clocks[rsem, n] = {rsem: n, "#": seq[0]}
+        for r in places:
+            writes.setdefault(r[0], []).append((r[1:4], (rsem, n), "far"))
+
     def send(to, rsem, *pairs):
         c = T.cores[to % 8]
         adr, ne = topo.addr(c), len(topo.engines(core, c))
@@ -175,268 +196,320 @@ def rank_program(g, core, T, topo):
             hold("g", [src], [])
             CNT["ls"] += ne
             g.remote_dma(ap(dst), ap(src), T.sem[rsem], T.sem["ls"], adr[1], adr[0], topo.mask(core, c))
-        seq[0] += 1
-        ev = (rsem, ne * len(pairs))
-        clocks[ev] = {ev[0]: ev[1], "#": seq[0]}
-        for r, src in pairs:
-            writes.setdefault(r[0], []).append((r[1:4], ev, "far"))
+        landed(rsem, ne * len(pairs), [r for r, src in pairs])
 
-    dma("s", ap(R("xt0")), T.x[:, :], [], [R("xt0")], "dx")
+    def send2(src, rsem, *ends):
+        cs = [T.cores[to % 8] for to, dst in ends]
+        mask = topo.mask(core, cs[0]) & topo.mask(core, cs[-1])
+        ne = len([e for e in topo.engines(core, cs[0]) if mask >> e & 1])
+        hold("g", [src], [])
+        CNT["ls"] += ne
+        g.remote_dma_fused([RemoteDMATransfer(dst_ids=[DstId(rid=topo.addr(c)[0], pnc=topo.addr(c)[1]) for c in cs], dma_engine_mask=mask,
+                                              remote_sem=T.sem[rsem], srcs=[ap(src)], dsts=[ap(dst) for to, dst in ends])], local_sem=T.sem["ls"])
+        landed(rsem, ne * len(ends), [dst for to, dst in ends])
+
     dma("a", ap(R("ut")), T.u[:, :], [], [R("ut")], "du")
+    dma("s", ap(R("xt0", 0, 4 * XA)), T.x[:, 0:4 * XA], [], [R("xt0", 0, 4 * XA)], "dx")
     dma("a", ap(R("li")), T.link[:, :], [], [R("li")], "dl")
+    dma("s", ap(R("xt0", 4 * XA, 1536)), T.x[:, 4 * XA:1536], [], [R("xt0", 4 * XA, 1536)], "dx2")
     dma("s", ap(R("wq", bit="u8")), T.wc[:, :], [], [R("wq")], "dw")
     dma("s", ap(R("wqs")), T.ws[:, :], [], [R("wqs")], "ds")
     dma("s", ap(R("vt")), T.v[:, :], [], [R("vt")], "dv")
 
-    KCB, JB, UO = R("kj", 0, 24), R("kj", 24, 36), R("pi", 4, 12)
+    UO = R("pi", 4, 12)
     fine = {"allow_small_or_imprecise_dtypes": True}
     iota(R("pi", 0, 1), [[1, 1]], 1)
     iota(R("ks"), [[1, 16]], **fine)
     iota(UO, [[16, 8]])
-    iota(KCB, [[16, 24]], **fine)
-    iota(JB, [[16, 12]], **fine)
+    iota(R("k16"), [[0, 24], [1, 16]], **fine)
     iota(R("ks4"), [[0, 4], [1, 4]], **fine)
-    iota(R("iota0"), [[1, 384]], **fine)
-    iota(R("alt"), [[0, 192], [1024, 2]], **fine)
+    iota(R("bi"), [[1, 8], [0, 4]], **fine)
+    iota(R("kcb"), [[16, 24]], **fine)
+    iota(R("iota0"), [[1, 576]], **fine)
 
-    col = {n: R("cols", i, i + 1) for i, n in enumerate(("pm", "pm1", "p4", "p41", "b16", "b4", "bb", "thr", "k2", "pb4", "pbn", "z"))}
-    fill(R("one"), 1.0)
+    col = {n: R("cols", i, i + 1) for i, n in enumerate(("pm", "pm1", "p4", "p41", "b1", "nb1", "pg", "b16", "b4", "bb1", "h4", "h16", "pbn", "tiny", "z", "z2"))}
+    fill(R("zt"), 0.0)
     ts(R("pi", 1, 2), R("pi", 0, 1), 15, AL.bitwise_and)
     ts(R("pi", 2, 3), R("pi", 0, 1), 2, AL.logical_shift_right, 3, AL.bitwise_and)
     ts(R("pi", 3, 4), R("pi", 0, 1), 3, AL.bitwise_and)
-    fill(R("ow", 0, 24), 0.0)
+    fill(col["tiny"], -1.0e-36)
     cp(col["pm"], R("pi", 1, 2))
     cp(col["p4"], R("pi", 2, 3))
     ts(col["pm1"], R("pi", 1, 2), 1.0, AL.add)
     ts(col["p41"], R("pi", 2, 3), 1.0, AL.add)
+    ts(R("pmo"), R("zt", 0, 24), col["pm"], AL.add)
+    ts(R("ta"), R("ks"), col["pm"], AL.is_equal, -3 * BV, AL.mult)
+    ts(R("tn"), R("ks"), col["pm1"], AL.is_equal, BV, AL.mult)
     ts(col["b16"], col["pm"], 14.5, AL.is_lt, BV, AL.mult)
     ts(col["b4"], col["p4"], 2.5, AL.is_lt, BV, AL.mult)
-    ts(R("pmo"), R("ow", 0, 24), col["pm"], AL.add)
-    for b in range(4):
-        act(R("iet", 512 * b, 512 * b + 512), R("one"), scale=0.0)
-    asel(R("bot"), R("one"), [[-16, 8], [0, 64]], AL.is_ge, 0, 1)
-    asel(R("bot"), R("bot"), [[16, 8], [0, 64]], AL.is_ge, 15, -1)
-    for b in range(4):
-        asel(R("iet", 512 * b + b, 512 * b + 512, 4), R("one", 0, 128), [[-1, 128]], AL.is_equal, 0, 1)
-    ts(R("ta"), R("ks"), col["pm"], AL.is_equal, 2 * BIG, AL.mult)
-    ts(R("rsw"), R("ks"), 0.5, AL.is_gt, 2 * BIG, AL.mult)
-    ts(R("r0w"), R("ks"), 0.5, AL.is_gt)
-    ts(R("mbw"), R("ta"), -BIG, AL.add)
-    ts(R("rsw"), R("rsw"), -BIG, AL.add)
-    act(R("mb"), IND(R("mbw"), R("pmo")))
-    act(R("rs"), IND(R("rsw"), R("pmo")))
-    ts(R("ta"), R("ks"), col["pm"], AL.is_equal, -2 * BV, AL.mult)
-    ts(R("tn"), R("ks"), col["pm1"], AL.is_equal, BV, AL.mult)
-    ts(R("t16w"), R("ks"), 0.5, AL.is_lt, -8 * BV, AL.mult)
-    tt(R("ta"), R("ta"), R("tn"), AL.add)
+    tt(R("t16w"), R("ta"), R("tn"), AL.add)
+    ts(R("pi", 0, 1), R("pi", 0, 1), 4, AL.logical_shift_right)
     ts(R("uo16", 0, 8), UO, 0.0, AL.add)
     ts(R("uo16", 8, 16), UO, 1.0, AL.add)
-    tt(R("t16w"), R("t16w"), R("ta"), AL.add)
-    ts(col["bb"], col["b16"], 2.0 ** -18, AL.mult)
-    ts(col["thr"], col["b16"], 2.0 ** -18, AL.mult, 0.5, AL.add)
-    ts(R("tbw"), R("t16w"), 2.0 ** -18, AL.mult)
-    act(R("tb"), IND(R("tbw"), R("pmo")))
-    act(R("r0"), IND(R("r0w"), R("pmo")))
     act(R("t16"), IND(R("t16w"), R("pmo")))
-    for n, ls, w in TILES[:2]:
-        fill(R(n, 64 * ls[-1], 4 * w), 0.0)
-    fill(R("ru", 0, 1), 0.0)
+    for b in range(4):
+        act(R("iet", 512 * b, 512 * b + 512), R("zt"))
+    ts(R("ta"), R("ks4"), col["p4"], AL.is_equal, -3 * BV, AL.mult)
+    ts(R("tn"), R("ks4"), col["p41"], AL.is_equal, BV, AL.mult)
+    cp(col["pg"], R("pi", 0, 1))
+    ts(col["b1"], R("pi", 3, 4), 1.0, AL.add)
+    tt(R("t4w"), R("ta"), R("tn"), AL.add)
+    ts(R("bw"), R("ks"), col["pg"], AL.is_equal)
+    cp(R("bo16"), R("bi"))
+    ts(col["nb1"], col["b1"], -1.0, AL.mult)
+    ts(R("mb"), R("k16"), col["pm"], AL.not_equal, -BIG, AL.mult)
+    ts(R("rs"), R("k16"), 0.5, AL.is_lt, -4 * BIG, AL.mult)
+    ts(R("tb"), R("t16"), 2.0 ** -9, AL.mult)
+    act(R("bot"), IND(R("bw"), R("bo16")))
+    fill(R("one"), 1.0)
+    cp(R("lo0"), R("li"))
+    send(rank + 1, "rl0", (R("lp0"), R("lo0")))
+    for b in range(4):
+        asel(R("iet", 512 * b + b, 512 * b + 512, 4), R("one"), [[-1, 128]], AL.is_equal, 0, 1)
     quant("uq", R("ut"))
+    ts(R("r0"), R("k16"), 0.5, AL.is_gt)
     for n, lo in (("urs", 0), ("urb", 8)):
         cp(R(n, bit="u32"), IND(R("uq", bit="u32"), R("uo16", lo, lo + 8)))
-        cp(R(n + "s"), IND(R("uqs"), R("uo16", lo, lo + 8)))
-    fill(R("zt"), 0.0)
-    fill(R("ak", 384, 512), 0.0)
-    fill(R("al", 384, 512), 0.0)
+        act(R(n + "s"), IND(R("uqs"), R("uo16", lo, lo + 8)))
+    for n, ls, w in TILES:
+        fill(R(n, 64 * ls[-1], 4 * w), 0.0)
+    act(R("t4"), IND(R("t4w"), R("pmo")))
+    act(R("pw", 0, 384), R("iota0", 0, 384), AF.Identity, scale=4.0, bias=col["b1"])
+    act(R("pw", 384, 768), R("iota0", 0, 384), AF.Identity, scale=-4.0, bias=col["nb1"])
 
-    xin = "xt0"
+    def xquant(xn):
+        quant("xq", R(xn, 0, 4 * XA), 0, XA)
+        quant("xq", R(xn, 4 * XA, 1536), XA, 384)
+
+    xquant("xt0")
     for t in range(NR):
         d = 2 ** t
-        xn, lr, qk, vb = "xt%d" % (t + 1), "lr%d" % t, "qk%d" % t, "vb%d" % t
-        sb, lb, sn, ln, st, lt = ["%s%d" % (n, t) for n in ("sb", "lb", "sn", "ln", "st", "lt")]
+        xn, qk, vb = "xt%d" % (t + 1), "qk%d" % t, "vb%d" % t
+        sb, lb, sn, ln, st, lp, lo = ["%s%d" % (n, t) for n in ("sb", "lb", "sn", "ln", "st", "lp", "lo")]
         P = [R("p%d" % b, 0, 384) for b in range(8)]
-        quant("xq", R(xin))
         mm(P[0], "urs", 0, "xq", 384)
         mm(P[1], "urb", 0, "xq", 384)
         mm(P[7], "urs", 0, "xq", 384)
         if t:
             for b in range(4):
                 mm(P[2 + b], "eq", 128 * b, "xq", 384)
-            scan(R("lc"), R("t16"), R(lr))
         else:
             for k in range(NR):
                 quant("vb%d" % k, R("zt"))
-        act(R("sg"), P[1], AF.Sign)
-        tt(R("m2"), P[0], R("mb"), AL.min)
-        if t:
-            ts(R("ow", 48, 72), R("lc", 15, 384, 16), col["b16"], AL.subtract)
-            ts(R("lt16"), R("lc", 15, 384, 16), col["b16"], AL.subtract)
-        else:
-            cp(R("lt16"), R("li"))
-            cp(R("ow", 48, 72), R("li"))
-        scan(R("hs"), R("rs"), R("m2"), AL.min)
-        scan(R("bt"), R("tb"), R("sg"))
-        tt(R("fa", 3, 1536, 4), P[0], R("hs"), AL.is_le)
-        ts(R(sb), R("bt", 15, 384, 16), col["thr"], AL.is_gt)
-        send(rank - d, "rb%d" % t, (R(lb), R(sb)))
-        for n, ls, w in TILES[2:] if t == 0 else []:
-            iota(R(n, 64 * ls[-1], 4 * w), [[0, 4 * w - 64 * ls[-1]]], **fine)
-        if t:
-            for b in range(2):
-                act(R(xn, b, 1536, 4), P[2 + b])
-        for k, c in enumerate((23, 22, 21)):
-            act(R("sgl", 368 * k, 368 * k + 16 * c), R("p7", 0, 16 * c), AF.Sign, scale=-1.0, bias=R("hs", 16 * c + 15, 16 * c + 16))
-        ju = [0]
-
-        def layer(fn, k, c, by=None):
-            n = 16 * c
-            if by is None:
-                ts(R(fn, k, 4 * n, 4), R("p0", 0, n), R("hs", n + 15, n + 16), AL.is_lt)
-            else:
-                ts(R(fn, k, 4 * n, 4), R("sgl", 368 * by, 368 * by + n), 0.5, AL.is_gt)
-            act(R("junk", ju[0], ju[0] + n), R(fn, k, 4 * n, 4), accum=R("ru", c, c + 1))
-            ju[0] += n
-
-        for k in range(4):
-            layer("fb", k, 20 - k)
-        for k in range(3):
-            layer("fa", k, 23 - k, k)
-        for ti, (fn, ls, w) in enumerate(TILES):
-            todo = [(TILES[ti + 1][0], k, c) for k, c in enumerate(TILES[ti + 1][1]) if c < 17] if ti < 5 else []
-            for x in todo[:1]:
-                layer(*x)
-            if ti == 0:
-                if t == 0:
-                    act(R(lr), IND(R("iota0"), R("lt16")))
-                    quant("bo", R("bot"))
-                    ts(KCB, KCB, 15.0, AL.add, col["pm"], AL.subtract)
-                    ts(JB, JB, col["pm"], AL.add, col["b16"], AL.add)
-                    ts(col["k2"], col["b16"], -1.0, AL.mult, 191.0, AL.add)
-                    ts(KCB, KCB, col["b16"], AL.subtract)
-                scan(R("rds"), R("r0"), R("fa", 3, 1536, 4), AL.mult, AL.add)
-            if ti == 5:
-                cp(R("off16"), R("ow", 24, 48))
-            quant("q" + fn, R(fn))
-            mm(R("p6", 0, w), "bo", 0, "q" + fn, w, start=ti == 0, stop=ti == 5)
-            if ti == 0:
-                tt(R("kr", 0, 24), KCB, R("rds", 15, 384, 16), AL.subtract)
-                if t == 0:
-                    ts(R("ta"), R("ks4"), col["p4"], AL.is_equal, -2 * BV, AL.mult)
-                    ts(R("tn"), R("ks4"), col["p41"], AL.is_equal, BV, AL.mult)
-                    ts(R("t4w"), R("ks4"), 0.5, AL.is_lt, -8 * BV, AL.mult)
-                    tt(R("ta"), R("ta"), R("tn"), AL.add)
-                    cp(col["pb4"], R("pi", 3, 4))
-                    ts(col["z"], col["b4"], -4.0, AL.mult)
-                    tt(R("t4w"), R("t4w"), R("ta"), AL.add)
-                    tt(col["pbn"], col["z"], col["pb4"], AL.add)
-                    ts(R("cw"), R("ks"), 512.0, AL.mult)
-                    ts(R("cv"), R("ks"), -512.0, AL.mult, 512.0, AL.add)
-                    act(R("t4"), IND(R("t4w"), R("pmo", 0, 12)))
-            if ti == 2:
-                act(R("w2", 0, 384), IND(R("cw"), R(lb)))
-                act(R("w2", 384, 768), IND(R("cv"), R(lb)))
-                ts(R("ow", 0, 24), R("bt", 15, 384, 16), col["thr"], AL.is_gt, 384.0, AL.mult)
-            if ti == 3:
-                tt(R("ow", 24, 48), R("ow", 0, 24), R("ow", 48, 72), AL.add)
-            for x in todo[1:]:
-                layer(*x)
+            quant("qf", R("zt"), 1344 - 64, 1344 + 64)
+            quant("bo", R("bot"))
+        act(R("sg"), P[1], AF.Sign, bias=col["tiny"])
+        tt(R("m2"), P[0], R("mb"), AL.add)
         if t == 0:
+            ts(R("jc"), R("kcb"), col["pm"], AL.add, 384.0, AL.add)
+            ts(col["z"], col["b16"], -192.0 * 2.0 ** -8, AL.mult)
+            fill(R("jk", 127, 128), 0.0)
+        scan(R("hs"), R("rs"), R("m2"), first=-4 * BIG)
+        scan(R("bt"), R("tb"), R("sg"))
+
+        def twins():
+            act(R("tw"), IND(R("sg"), R(lp)))
+
+        def twins2():
+            scan(R("twc"), R("tb"), R("tw"))
+
+        def twins3():
+            tt(R(sb), R("twc", 15, 384, 16), R("jc"), AL.add)
+            send(rank - d, "rb%d" % t, (R(lb), R(sb)))
+
+        def sign(c):
+            act(R("sgl", 384 * (23 - c), 384 * (23 - c) + 16 * c), R("p7", 0, 16 * c), AF.Sign, scale=-1.0, bias=R("hs", 16 * c + 15, 16 * c + 16))
+
+        def relu(c):
+            fn, k = LANE[c]
+            act(R(fn, k, 64 * c, 4), R("sgl", 384 * (23 - c), 384 * (23 - c) + 16 * c), AF.Relu, accum=R("ru", c, c + 1))
+
+        def layer(c):
+            fn, k = LANE[c]
+            ts(R(fn, k, 64 * c, 4), R("p0", 0, 16 * c), R("hs", 16 * c + 15, 16 * c + 16), AL.is_lt)
+
+        def rowsum(c):
+            fn, k = LANE[c]
+            scan(R("jk", 128 * c + 128 - 8 * c, 128 * c + 128), R(fn, k, 32 * c, 4), R(fn, 32 * c + k, 64 * c, 4), AL.add, AL.add)
+
+        def colsum(fn, w, start=False, stop=False):
+            mm(R("p6", 0, w), "bo", 0, "q" + fn, w, start=start, stop=stop)
+
+        tt(R("fa", 3, 1536, 4), P[0], R("hs"), AL.is_le)
+        if t == 0:
+            ts(R("jc"), R("jc"), col["z"], AL.add, 1.0 / 192.0, AL.mult)
+            ts(R("jb"), R("kcb", 0, 12), col["pm"], AL.add, -191.0, AL.add)
+            ts(R("kcb"), R("kcb"), 15.0, AL.add, col["pm"], AL.subtract)
+        if t:
+            twins()
+        sc = list(range(23, NV, -1))
+        sign(sc[0])
+        todo = []
+        for i, c in enumerate(sc):
+            if i + 1 < NS:
+                todo.append((sign, sc[i + 1]))
+            todo.append((relu, c))
+        for f, c in todo[:6]:
+            f(c)
+        if t == 0:
+            twins()
+        layer(NV)
+        scan(R("rds"), R("r0"), R("fa", 3, 1536, 4), AL.mult, AL.add)
+        if t == 0:
+            ts(R("kcb"), R("kcb"), col["b16"], AL.subtract)
+        for c in range(NV - 1, 0, -1):
+            layer(c)
+            rowsum(c + 1)
+            if c == (14 if t else 8):
+                twins2()
+            if c == (13 if t else 7):
+                twins3()
+            if c == 13:
+                tt(R("kr", 0, 24), R("kcb"), R("rds", 15, 384, 16), AL.subtract)
+            if c == 12 and NV == 16:
+                quant("qfc", R("fc"))
+            if c == 10:
+                quant("qfa", R("fa"))
+                colsum("fa", 384, start=True)
+                if NV == 16:
+                    colsum("fc", 256)
+                for f, k in todo[6:]:
+                    f(k)
+            if c == 8:
+                quant("qfd", R("fd"))
+                colsum("fd", 192)
+        if t == 0:
+            act(R("pw", 768, 1152), R("pw", 0, 384))
             quant("eq", R("iet"))
             for b in range(4):
                 mm(P[2 + b], "eq", 128 * b, "xq", 384)
-        tt(R("pay"), IND(R("w2"), R("off16")), R("iota0"), AL.add)
+        tt(R("ow"), R("bt", 15, 384, 16), R(lb), AL.add)
+        rowsum(1)
+        quant("qf", R("ft", 4 * 1152, 4 * 1344), 1152, 1344)
+        colsum("fe", 128)
+        mm(R("p6", 0, 128), "bo", 0, "qf", 128, False, False, lo=1280)
+        ts(R("off16"), R("ow"), 192.0, AL.mult, 0.25, AL.add)
+        tt(R("kr", 24, 25 + NV), R("kr", 0, NV + 1), R("jk", 127, 128 * (NV + 1), 128), AL.subtract)
+        if NV < 16:
+            quant("qfc", R("fc"))
+            colsum("fc", 256)
+        quant("qfb", R("fb"))
+        colsum("fb", 320, stop=True)
+        act(R("pay"), IND(R("pw"), R("off16")))
+        tt(R("kr", 25 + NV, 48), R("kr", NV + 1, 24), R("ru", NV + 1, 24), AL.subtract)
+        if t == 0:
+            fill(R("alt", 0, 384, 2), 0.0)
+            fill(R("alt", 1, 384, 2), 2.0 ** -12)
+            ts(R("mn"), R("k16", 0, 192), col["pm"], AL.is_le, 1024.0, AL.mult)
+            ts(col["bb1"], col["b16"], 2.0 ** -9, AL.mult, 1.0, AL.add)
+            ts(col["h4"], col["b4"], 1.0, AL.add)
+            tt(col["h16"], col["b16"], col["b1"], AL.add)
+            ts(col["z2"], col["b4"], -4.0, AL.mult, -1.0, AL.add)
         scan(R("mc"), R("t16"), P[6])
-        tt(R("kr", 24, 48), R("kr", 0, 24), R("ru"), AL.subtract)
+        if t == 0:
+            tt(col["pbn"], col["z2"], col["b1"], AL.add)
         tt(R("kr", 48, 72), R("mc", 15, 384, 16), R("kr", 24, 48), AL.add)
+        if t == 0:
+            fill(R("ak", 384, 512), 0.0)
+            fill(R("al", 384, 512), 0.0)
         cp(R("rk16"), R("kr", 48, 72))
         cp(IND(R("sp"), R("rk16")), R("pay"))
-        for b in range(2 if t else 0, 4):
-            act(R(xn, b, 1536, 4), P[2 + b])
-        act(R("fh"), R(xn), scale=0.5)
+        for b in range(4):
+            act(R("fh", b, 1536, 4), P[2 + b], scale=0.5)
+        act(R("spa"), R("sp"), AF.Abs)
+        act(R("lr"), IND(R("iota0", 0, 384), R(lo)))
+        act(R("ew"), R("iota0", 0, 384))
 
         def pairs(a, b):
-            scan(R("kq", a, b), R("alt", a, b), R("sp", a, b), AL.mult, AL.add)
+            scan(R("kq", a, b), R("alt", a, b), R("spa", a, b), AL.mult, AL.add)
 
-        flt, pp1, pp2, pp3, nn = [R("pp", 12 * i, 12 * i + 12) for i in range(5)]
-        ts(R("fl"), R("sp", 1, 384, 2), 511.5, AL.is_gt)
-        pairs(0, 128)
+        mk, jbf, pp1, pp2, nn = [R("pp", 12 * i, 12 * i + 12) for i in range(5)]
+        F = R("fcum", 191, 192)
+        ts(R("fl"), R("sp", 1, 384, 2), 0.0, AL.is_lt)
         scan(R("fcum"), R("fl"), R("fl"))
         scan(R("flc"), R("tb", 0, 192), R("fl"))
-        scan(R("fc2"), R("t16", 0, 192), R("fcum"))
-        ts(flt, R("flc", 15, 192, 16), col["bb"], AL.subtract)
-        ts(pp2, R("fc2", 15, 192, 16), R("fcum", 191, 192), AL.subtract, col["k2"], AL.add)
-        tt(pp1, JB, R("fc2", 15, 192, 16), AL.subtract)
-        tt(pp3, pp2, flt, AL.mult)
+        scan(R("fc2"), R("mn"), R("fcum"), AL.add, AL.min)
+        ts(jbf, R("jb"), F, AL.add)
+        ts(mk, R("flc", 15, 192, 16), col["bb1"], AL.subtract, 1024.0, AL.mult)
+        tt(pp1, jbf, R("fc2", 15, 192, 16), AL.subtract)
+        tt(pp2, R("fc2", 15, 192, 16), mk, AL.add)
+        pairs(0, 128)
+        tt(nn, pp1, pp2, AL.max)
         pairs(128, 256)
-        tt(nn, pp1, pp3, AL.max)
+        ts(R("n16"), nn, F, AL.subtract, 191.0, AL.add)
         pairs(256, 384)
-        cp(R("n16"), nn)
         cp(IND(R("kqs"), R("n16")), R("kq", 1, 384, 2))
-        scan(R("c4"), R("t4"), R("kqs"))
+        scan(R("c4"), R("t4", 0, 192), R("kqs"))
         scan(R("c16"), R("t16", 0, 192), R("kqs"))
-        ts(R("kqi", 0, 48), R("c4", 3, 192, 4), col["b4"], AL.subtract)
-        ts(R("kqi", 48, 60), R("c16", 15, 192, 16), col["b16"], AL.subtract)
-        ts(R("kqi", 60, 108), R("kqi", 0, 48), 511, AL.bitwise_and)
-        ts(R("kqi", 120, 168), R("kqi", 0, 48), 10, AL.logical_shift_right, 511, AL.bitwise_and)
-        ts(R("t4q"), R("kqi", 60, 108), 4.0, AL.mult, col["pb4"], AL.add)
-        ts(R("kqi", 108, 120), R("kqi", 48, 60), 511, AL.bitwise_and)
-        ts(R("t4k"), R("kqi", 120, 168), 4.0, AL.mult, col["pb4"], AL.add)
-        cp(R("tqk"), R("kqi", 108, 114))
-        ts(R("kqi", 168, 180), R("kqi", 48, 60), 10, AL.logical_shift_right, 511, AL.bitwise_and)
+        ts(R("t4q"), R("c4", 3, 192, 4), col["h4"], AL.subtract)
+        ts(R("kqi", 0, 48), R("c4", 3, 192, 4), 4096.0, AL.mult)
+        ts(R("kqi", 48, 54), R("c16", 96 + 15, 192, 16), 4096.0, AL.mult)
+        ts(R("q16", 0, 12), R("c16", 15, 192, 16), col["h16"], AL.subtract, 0.25, AL.mult)
+        ts(R("kqi", 54, 108), R("kqi", 0, 54), 4095, AL.bitwise_and)
         act(R("fq", 0, 192), IND(R("fh"), R("t4q", 0, 12)))
+        act(R("lqk"), IND(R("lr"), R("q16", 0, 6)))
         act(R("fq", 192, 384), IND(R("fh"), R("t4q", 12, 24)))
         act(R("fq", 384, 768), IND(R("fh"), R("t4q", 24, 48)))
-        cp(R("lqk"), IND(R(lr), R("tqk")))
+        act(R("tu"), R("lr"))
+        ts(R("t4k"), R("kqi", 54, 102), 1.0, AL.subtract)
+        ts(R("q16", 12, 18), R("kqi", 102, 108), col["b1"], AL.subtract, 0.25, AL.mult)
         tt(R("ak", 0, 192), IND(R("fh"), R("t4k", 0, 12)), R("fq", 0, 192), AL.add)
-        scan(R("nmc"), R("t4", 0, 96), R("lqk"))
-        cp(R("tll", 0, 6), R("kqi", 114, 120))
-        ts(R(sn), R("nmc", 3, 96, 4), 4.0, AL.mult, col["pbn"], AL.add)
-        send(rank + d, "rn%d" % t, (R(ln), R(sn)))
+        scan(R("nm4"), R("t4", 0, 96), R("lqk"))
+        scan(R("nm16"), R("t16", 0, 96), R("lqk"))
+        ts(R(sn, 0, 24), R("nm4", 3, 96, 4), 4.0, AL.mult, col["pbn"], AL.add)
+        ts(R(sn, 24, 30), R("nm16", 15, 96, 16), col["b16"], AL.subtract)
+        send(rank + d, "rn%d" % t, (R(ln, 0, 30), R(sn, 0, 30)))
         tt(R("ak", 192, 384), IND(R("fh"), R("t4k", 12, 24)), R("fq", 192, 384), AL.add)
-        cp(R("tll", 6, 12), R("kqi", 174, 180))
         quant(qk, R("ak"))
         send(rank + d, "rc%d" % t, (R(vb, 0, 96, 1, "u8"), R(qk, 0, 96, 1, "u8")), (R(vb + "s", 0, 96), R(qk + "s", 0, 96)))
         tt(R("al", 0, 384), IND(R("fh"), R("t4k", 24, 48)), R("fq", 384, 768), AL.add)
+        cp(IND(R("ew"), R("q16", 6, 12)), R("iota0", 384, 480))
         quant("ql", R("al"))
-        act(R("val", 0, 96), IND(R(lr), R("tll", 6, 12)))
-        act(R("val", 96, 192), IND(R(lr), R("tll", 0, 6)))
-        act(R("tu"), R(lr))
+        act(R("val", 0, 96), IND(R("lr"), R("q16", 12, 18)))
+        act(R("val", 96, 192), IND(R("lr"), R("q16", 6, 12)))
         act(R("fl32"), R("fq", 384, 768), scale=64.0)
+        act(R("fn32"), IND(R("fh"), R(ln, 0, 24)), scale=64.0)
         left = ("p0", "p1", "p6", "p7")
         for b in range(4):
             mm(R(left[b], 0, 128), "wq", 128 * b, "ql", 128)
-        cp(IND(R("tu"), R("tll")), R("val"))
+        cp(IND(R("tu"), R("q16", 6, 18)), R("val"))
+        act(R("nl"), IND(R("tu"), R(lp)))
         for b in range(4):
             tt(R("sl", b, 384, 4), R(left[b], 0, 96), R("fl32", b, 384, 4), AL.add)
-        act(R("rl"), R("sl"), scale=0.03125)
-        scan(R("tuc"), R("t16"), R("tu"))
+        act(R("rl"), R("sl"), scale=2.0 ** -6)
+        cp(IND(R("ew"), R(ln, 24, 30)), R("iota0", 480, 576))
         if t == 0:
             quant("vq", R("vt"))
-        ts(R(st), R("tuc", 15, 384, 16), col["b16"], AL.subtract)
-        send(rank - d, "rt%d" % t, (R(lt), R(st)))
-        cp(IND(R(xn), R("t4q", 24, 48)), R("rl"))
-        act(R("fn32"), IND(R("fh"), R(ln)), scale=64.0)
+        scan(R("ec"), R("t4"), R("ew"))
         for b in range(4):
             mm(R("p%d" % (2 + b), 0, 128), "wq", 128 * b, vb, 128)
         for b in range(4):
             tt(R("sa", b, 384, 4), R("p%d" % (2 + b), 0, 96), R("fn32", b, 384, 4), AL.add)
-            act(R("ra", b, 384, 4), R("sa", b, 384, 4), scale=0.03125)
-        act(R("tr"), IND(R("iota0"), R(lt)))
-        act(R("lr%d" % (t + 1)), IND(R("tr"), R("lt16")))
-        cp(IND(R(xn), R(ln)), R("ra"))
-        xin = xn
-    quant("xq", R(xin))
-    for b in range(2):
-        mm(R("p%d" % b, 0, 192), "vq", 0, "xq", 192, lo=192 * b)
-    dma("s", T.oc[:, :], ap(R("xq", bit="u8")), [R("xq")], [], "oc_")
+            act(R("ra", b, 384, 4), R("sa", b, 384, 4), scale=2.0 ** -6)
+            if b == 0:
+                ts(R("e4"), R("ec", 3, 384, 4), 4.0, AL.mult, col["pbn"], AL.add)
+        scan(R("nlc"), R("t16"), R("nl"))
+        act(R(xn, 4 * XA, 1536), IND(R("fw"), R("e4", XA // 4, 96)), scale=2.0)
+        ts(R(xn, 0, 4 * XA), IND(R("fw"), R("e4", 0, XA // 4)), 2.0, AL.mult)
+        ts(R(st), R("nlc", 15, 384, 16), col["b16"], AL.subtract)
+        if t + 1 < NR:
+            send2(R(st), "rt%d" % t, (rank - d, R("lo%d" % (t + 1))), (rank + d, R("lp%d" % (t + 1))))
+        else:
+            send(rank - d, "rt%d" % t, (R("lo3"), R(st)))
+        xquant(xn)
+    mm(R("p0", 0, XA), "vq", 0, "xq", XA)
+    mm(R("p1", 0, 384 - XA), "vq", 0, "xq", 384 - XA, lo=XA)
+    dma("s", T.oc[:, 0:4 * XA], ap(R("xq", 0, XA, 1, "u8")), [R("xq", 0, XA)], [], "oc_")
+    dma("s", T.oc[:, 4 * XA:1536], ap(R("xq", XA, 384, 1, "u8")), [R("xq", XA, 384)], [], "oc2")
+    act(R("ys", 0, XA), R("p0", 0, XA))
+    dma("a", T.y[:, 0:XA], ap(R("ys", 0, XA)), [R("ys", 0, XA)], [], "oy")
+    cp(R("ys", XA, 384), R("p1", 0, 384 - XA))
+    dma("s", T.y[:, XA:384], ap(R("ys", XA, 384)), [R("ys", XA, 384)], [], "oz")
     for k in range(4):
-        dma("s", T.osc[4 * k:4 * k + 4, :], T.xqs[32 * k:32 * k + 4, 0:384], [R("xqs")], [], "o%d" % k)
-    dma("s", T.lk[:, :], T.lr3[0:128:16, :], [R("lr3")], [], "ok")
-    act(R("ys", 0, 192), R("p0", 0, 192))
-    dma("a", T.y[:, 0:192], ap(R("ys", 0, 192)), [R("ys", 0, 192)], [], "oy")
-    cp(R("ys", 192, 384), R("p1", 0, 192))
-    dma("s", T.y[:, 192:384], ap(R("ys", 192, 384)), [R("ys", 192, 384)], [], "oz")
-    for s in ("oc_", "o0", "o1", "o2", "o3", "oy", "oz", "ok"):
+        dma("a", T.osc[4 * k:4 * k + 4, :], T.xqs[32 * k:32 * k + 4, 0:384], [R("xqs")], [], "o%d" % k)
+    act(R("lr3"), IND(R("iota0", 0, 384), R("lo3")))
+    dma("a", T.lk[:, :], T.lr3[0:128:16, :], [R("lr3")], [], "ok")
+    for s in ("oc_", "oc2", "o0", "o1", "o2", "o3", "oy", "oz", "ok"):
         g.wait_ge(T.sem[s], 16)
     for s in ("v", "a", "p", "gc", "ls"):
         g.wait_ge(T.sem[s], CNT[s])

@@ -5,11 +5,14 @@ AL, AF = AluOpType, ActivationFunctionType
 NR = 3
 BIG = 2.0 ** 90
 BV = 2048.0
-NS = 7
-NV = 23 - NS
-XA = 176
+NV = 17
+JW = 160
+QA = 8
+T0, T1 = 5, 11
+XA = 160
+XQ = 256
 TILES = [("fa", [23, 22, 21], 384), ("fb", [20, 19, 18, 17], 320), ("fc", [16, 15, 14, 13], 256),
-         ("fd", [12, 11, 10, 9], 192), ("fe", [8, 7, 6, 5], 128), ("ff", [4, 3, 2, 1], 64)]
+         ("fd", [12, 11, 10, 9], 192), ("fe", [8, 7, 6, 5], 128), ("ff", [4, 3, 2, 1], 128)]
 LANE = {_c: (_n, _k) for _n, _l, _w in TILES for _k, _c in enumerate(_l)}
 
 SCRATCH, WHERE = {}, {}
@@ -36,28 +39,30 @@ def _each(text, dtype):
 
 
 _each("xt0:1536 xt1:1536 xt2:1536 xt3:1536 ut:512 vt:512 iet:2048 bot:512 zt:512 ak:512 al:512 one:128 sg:384 bt:384 rds:384 "
-      "tw:384 twc:384 sgl:3072 jk:2176", "bfloat16")
+      "tw:384 twc:384 sgl:2688 jk:3360 fh:1536", "bfloat16")
 _s([("k16", 384), ("mb", 384), ("rs", 384), ("r0", 384), ("tb", 384), ("t16", 384), ("t4", 384), ("alt", 384), ("mn", 192)], "bfloat16", buf="kb")
 _s([("fl", 192), ("flc", 192), ("fcum", 192), ("fc2", 192)], "bfloat16", buf="fs")
-_s([("fh", 1536), ("rl", 384), ("ra", 384)], "bfloat16", buf="fw")
+_s([("f32", 1536), ("rl", 384), ("ra", 384)], "bfloat16", buf="fw")
 _s([(_n, 4 * _w) for _n, _l, _w in TILES], "bfloat16", buf="ft")
-_s([("q" + _n, _w) for _n, _l, _w in TILES] + [("qz", 64)], "codes", buf="qf")
+_s([("q" + _n, _w) for _n, _l, _w in TILES], "codes", buf="qf")
 _each("xq:384 uq:128 urs:128 urb:128 vq:128 eq:512 bo:128 wq:512 ql:128", "codes")
 for _t in "012":
     _each("qk%s:128 vb%s:128" % (_t, _t), "codes")
     _each("sn%s:32 ln%s:32 st%s:24 lp%s:24 lo%s:24" % (_t, _t, _t, _t, _t), "uint16")
     _each("sb%s:24 lb%s:24" % (_t, _t), "float32")
 _each("lo3:24", "uint16")
-_s([(_n, 16) for _n in ("ks", "ks4", "t16w", "t4w", "ta", "tn", "bw")] + [("cols", 24), ("kcb", 24), ("jc", 24), ("jb", 12), ("bi", 32)], "float32", buf="kw")
+_s([(_n, 16) for _n in ("ks", "ks4", "t16w", "t4w", "cmw", "ta", "tn", "ta2", "tn2", "bw")]
+   + [("cols", 24), ("kcb", 24), ("jc", 24), ("jb", 12), ("bi", 32)], "float32", buf="kw")
 _s([("c4", 192), ("c16", 192), ("kq", 384), ("lqk", 96), ("nm4", 96), ("nm16", 96)], "float32", buf="cc")
 _s([("mc", 384), ("nl", 384), ("nlc", 384), ("ec", 384)], "float32", buf="sc3")
-_each("iota0:576 pw:1152 m2:384 hs:384 ru:24 kr:72 ow:24 pay:384 sp:384 spa:384 kqs:192 pp:60 "
-      "fq:768 fl32:384 fn32:384 sl:384 sa:384 val:192 tu:384 ew:384 lr:384 lr3:384 ys:384", "float32")
-_each("li:24 pi:12 kqi:108", "int32")
+_each("iota0:576 pw:1152 m2:384 hs:384 cm:384 ru:24 kr:24 ow:24 pay:384 sp:384 spa:384 kqs:192 pp:60 "
+      "fq:768 fl32:384 fn32:384 val:192 tu:384 ew:384 lr:384 lr3:384 ys:384", "float32")
+_each("li:24 pi:14 kqi:108", "int32")
 _each("pmo:24 uo16:16 bo16:32 off16:24 rk16:24 n16:12 t4q:48 t4k:48 q16:18 e4:96", "uint16")
 _s([("p%d" % _b, 512) for _b in range(8)], "float32", "psum", "ps")
 
-SEMAPHORES = ("v a p gc ls dx dx2 du dw ds dv dl oy oz ok oc_ oc2 o0 o1 o2 o3 rb0 rb1 rb2 rn0 rn1 rn2 rc0 rc1 rc2 rl0 rt0 rt1 rt2").split()
+SEMAPHORES = ("v a p gc ls dx dx2 du dw ds dv dl z0 z1 z2 z3 oy oz ok oc_ oc2 o0 o1 o2 o3 "
+              "rb0 rb1 rb2 rn0 rn1 rn2 rc0 rc1 rc2 rl0 rt0 rt1 rt2").split()
 
 
 def R(name, lo=0, hi=None, step=1, bit=None):
@@ -208,78 +213,85 @@ def rank_program(g, core, T, topo):
                                               remote_sem=T.sem[rsem], srcs=[ap(src)], dsts=[ap(dst) for to, dst in ends])], local_sem=T.sem["ls"])
         landed(rsem, ne * len(ends), [dst for to, dst in ends])
 
-    dma("a", ap(R("ut")), T.u[:, :], [], [R("ut")], "du")
-    dma("s", ap(R("xt0", 0, 4 * XA)), T.x[:, 0:4 * XA], [], [R("xt0", 0, 4 * XA)], "dx")
     dma("a", ap(R("li")), T.link[:, :], [], [R("li")], "dl")
-    dma("s", ap(R("xt0", 4 * XA, 1536)), T.x[:, 4 * XA:1536], [], [R("xt0", 4 * XA, 1536)], "dx2")
+    dma("s", ap(R("ut")), T.u[:, :], [], [R("ut")], "du")
+    dma("a", ap(R("xt0", 0, 4 * XQ)), T.x[:, 0:4 * XQ], [], [R("xt0", 0, 4 * XQ)], "dx")
+    dma("s", ap(R("xt0", 4 * XQ, 1536)), T.x[:, 4 * XQ:1536], [], [R("xt0", 4 * XQ, 1536)], "dx2")
+    fill(R("zt"), 0.0)
+    for b in range(4):
+        dma("s", ap(R("iet", 512 * b, 512 * b + 512)), ap(R("zt")), [R("zt")], [R("iet", 512 * b, 512 * b + 512)], "z%d" % b)
     dma("s", ap(R("wq", bit="u8")), T.wc[:, :], [], [R("wq")], "dw")
     dma("s", ap(R("wqs")), T.ws[:, :], [], [R("wqs")], "ds")
     dma("s", ap(R("vt")), T.v[:, :], [], [R("vt")], "dv")
 
-    UO = R("pi", 4, 12)
+    UO = R("pi", 6, 14)
     fine = {"allow_small_or_imprecise_dtypes": True}
     iota(R("pi", 0, 1), [[1, 1]], 1)
     iota(R("ks"), [[1, 16]], **fine)
     iota(UO, [[16, 8]])
-    iota(R("k16"), [[0, 24], [1, 16]], **fine)
+    iota(R("iota0", 0, 384), [[1, 384]], **fine)
     iota(R("ks4"), [[0, 4], [1, 4]], **fine)
     iota(R("bi"), [[1, 8], [0, 4]], **fine)
     iota(R("kcb"), [[16, 24]], **fine)
-    iota(R("iota0"), [[1, 576]], **fine)
 
-    col = {n: R("cols", i, i + 1) for i, n in enumerate(("pm", "pm1", "p4", "p41", "b1", "nb1", "pg", "b16", "b4", "bb1", "h4", "h16", "pbn", "tiny", "z", "z2"))}
-    fill(R("zt"), 0.0)
+    col = {n: R("cols", i, i + 1) for i, n in enumerate(
+        ("pm", "pm1", "pm0", "p4", "p41", "b1", "nb1", "pg", "b16", "b4", "bb1", "h4", "h16", "pbn", "tiny", "z", "z2", "f0", "kc"))}
     ts(R("pi", 1, 2), R("pi", 0, 1), 15, AL.bitwise_and)
     ts(R("pi", 2, 3), R("pi", 0, 1), 2, AL.logical_shift_right, 3, AL.bitwise_and)
     ts(R("pi", 3, 4), R("pi", 0, 1), 3, AL.bitwise_and)
-    fill(col["tiny"], -1.0e-36)
+    ts(R("pi", 4, 5), R("pi", 0, 1), 4, AL.logical_shift_right)
     cp(col["pm"], R("pi", 1, 2))
-    cp(col["p4"], R("pi", 2, 3))
     ts(col["pm1"], R("pi", 1, 2), 1.0, AL.add)
-    ts(col["p41"], R("pi", 2, 3), 1.0, AL.add)
+    ts(col["pm0"], R("pi", 1, 2), -1.0, AL.add)
+    ts(col["b1"], R("pi", 3, 4), 1.0, AL.add)
     ts(R("pmo"), R("zt", 0, 24), col["pm"], AL.add)
     ts(R("ta"), R("ks"), col["pm"], AL.is_equal, -3 * BV, AL.mult)
     ts(R("tn"), R("ks"), col["pm1"], AL.is_equal, BV, AL.mult)
-    ts(col["b16"], col["pm"], 14.5, AL.is_lt, BV, AL.mult)
-    ts(col["b4"], col["p4"], 2.5, AL.is_lt, BV, AL.mult)
+    act(R("k16"), IND(R("ks"), R("pmo")))
+    ts(col["nb1"], col["b1"], -1.0, AL.mult)
+    ts(R("ta2"), R("ks"), col["pm0"], AL.is_equal, -3 * BV, AL.mult)
+    ts(R("tn2"), R("ks"), col["pm"], AL.is_equal, BV, AL.mult)
     tt(R("t16w"), R("ta"), R("tn"), AL.add)
-    ts(R("pi", 0, 1), R("pi", 0, 1), 4, AL.logical_shift_right)
+    cp(col["p4"], R("pi", 2, 3))
+    ts(col["p41"], R("pi", 2, 3), 1.0, AL.add)
+    tt(R("cmw"), R("ta2"), R("tn2"), AL.add)
+    act(R("t16"), IND(R("t16w"), R("pmo")))
+    act(R("pw", 0, 384), R("iota0", 0, 384), AF.Identity, scale=4.0, bias=col["b1"])
+    act(R("pw", 384, 768), R("iota0", 0, 384), AF.Identity, scale=-4.0, bias=col["nb1"])
     ts(R("uo16", 0, 8), UO, 0.0, AL.add)
     ts(R("uo16", 8, 16), UO, 1.0, AL.add)
-    act(R("t16"), IND(R("t16w"), R("pmo")))
-    for b in range(4):
-        act(R("iet", 512 * b, 512 * b + 512), R("zt"))
-    ts(R("ta"), R("ks4"), col["p4"], AL.is_equal, -3 * BV, AL.mult)
-    ts(R("tn"), R("ks4"), col["p41"], AL.is_equal, BV, AL.mult)
-    cp(col["pg"], R("pi", 0, 1))
-    ts(col["b1"], R("pi", 3, 4), 1.0, AL.add)
-    tt(R("t4w"), R("ta"), R("tn"), AL.add)
-    ts(R("bw"), R("ks"), col["pg"], AL.is_equal)
-    cp(R("bo16"), R("bi"))
-    ts(col["nb1"], col["b1"], -1.0, AL.mult)
-    ts(R("mb"), R("k16"), col["pm"], AL.not_equal, -BIG, AL.mult)
-    ts(R("rs"), R("k16"), 0.5, AL.is_lt, -4 * BIG, AL.mult)
-    ts(R("tb"), R("t16"), 2.0 ** -9, AL.mult)
-    act(R("bot"), IND(R("bw"), R("bo16")))
+    cp(col["pg"], R("pi", 4, 5))
+    ts(col["b16"], col["pm"], 14.5, AL.is_lt, BV, AL.mult)
+    ts(col["b4"], col["p4"], 2.5, AL.is_lt, BV, AL.mult)
+    ts(col["f0"], col["pm"], 0.5, AL.is_lt, 3 * BV, AL.mult)
+    fill(col["tiny"], -1.0e-36)
     fill(R("one"), 1.0)
+    for n, ls, w in TILES[:3]:
+        fill(R(n, 64 * ls[-1], 4 * w), 0.0)
+    ts(R("mb"), R("k16"), col["pm"], AL.not_equal, -BIG, AL.mult)
     cp(R("lo0"), R("li"))
+    ts(R("rs"), R("k16"), 0.5, AL.is_lt, -4 * BIG, AL.mult)
     send(rank + 1, "rl0", (R("lp0"), R("lo0")))
+    iota(R("iota0", 384, 576), [[1, 192]], base=384, **fine)
     for b in range(4):
         asel(R("iet", 512 * b + b, 512 * b + 512, 4), R("one"), [[-1, 128]], AL.is_equal, 0, 1)
+    ts(R("bw"), R("ks"), col["pg"], AL.is_equal)
+    cp(R("bo16"), R("bi"))
+    ts(R("ta"), R("ks4"), col["p4"], AL.is_equal, -3 * BV, AL.mult)
+    ts(R("tn"), R("ks4"), col["p41"], AL.is_equal, BV, AL.mult)
+    ts(R("tb"), R("t16"), 2.0 ** -9, AL.mult)
+    tt(R("t4w"), R("ta"), R("tn"), AL.add)
     quant("uq", R("ut"))
     ts(R("r0"), R("k16"), 0.5, AL.is_gt)
     for n, lo in (("urs", 0), ("urb", 8)):
         cp(R(n, bit="u32"), IND(R("uq", bit="u32"), R("uo16", lo, lo + 8)))
         act(R(n + "s"), IND(R("uqs"), R("uo16", lo, lo + 8)))
-    for n, ls, w in TILES:
-        fill(R(n, 64 * ls[-1], 4 * w), 0.0)
-    act(R("t4"), IND(R("t4w"), R("pmo")))
-    act(R("pw", 0, 384), R("iota0", 0, 384), AF.Identity, scale=4.0, bias=col["b1"])
-    act(R("pw", 384, 768), R("iota0", 0, 384), AF.Identity, scale=-4.0, bias=col["nb1"])
+    act(R("pw", 768, 1152), R("pw", 0, 384))
+    act(R("bot"), IND(R("bw"), R("bo16")))
 
     def xquant(xn):
-        quant("xq", R(xn, 0, 4 * XA), 0, XA)
-        quant("xq", R(xn, 4 * XA, 1536), XA, 384)
+        quant("xq", R(xn, 0, 4 * XQ), 0, XQ)
+        quant("xq", R(xn, 4 * XQ, 1536), XQ, 384)
 
     xquant("xt0")
     for t in range(NR):
@@ -287,7 +299,9 @@ def rank_program(g, core, T, topo):
         xn, qk, vb = "xt%d" % (t + 1), "qk%d" % t, "vb%d" % t
         sb, lb, sn, ln, st, lp, lo = ["%s%d" % (n, t) for n in ("sb", "lb", "sn", "ln", "st", "lp", "lo")]
         P = [R("p%d" % b, 0, 384) for b in range(8)]
-        mm(P[0], "urs", 0, "xq", 384)
+        PA, PB = R("p0", 0, XQ), R("p6", 0, 384 - XQ)
+        mm(PA, "urs", 0, "xq", XQ)
+        mm(PB, "urs", 0, "xq", 384 - XQ, lo=XQ)
         mm(P[1], "urb", 0, "xq", 384)
         mm(P[7], "urs", 0, "xq", 384)
         if t:
@@ -296,16 +310,13 @@ def rank_program(g, core, T, topo):
         else:
             for k in range(NR):
                 quant("vb%d" % k, R("zt"))
-            quant("qf", R("zt"), 1344 - 64, 1344 + 64)
-            quant("bo", R("bot"))
         act(R("sg"), P[1], AF.Sign, bias=col["tiny"])
-        tt(R("m2"), P[0], R("mb"), AL.add)
-        if t == 0:
-            ts(R("jc"), R("kcb"), col["pm"], AL.add, 384.0, AL.add)
-            ts(col["z"], col["b16"], -192.0 * 2.0 ** -8, AL.mult)
-            fill(R("jk", 127, 128), 0.0)
-        scan(R("hs"), R("rs"), R("m2"), first=-4 * BIG)
-        scan(R("bt"), R("tb"), R("sg"))
+        tt(R("m2", 0, XQ), PA, R("mb", 0, XQ), AL.add)
+        tt(R("m2", XQ, 384), PB, R("mb", XQ, 384), AL.add)
+        scan(R("hs", 0, XQ), R("rs", 0, XQ), R("m2", 0, XQ))
+        scan(R("hs", XQ, 384), R("rs", XQ, 384), R("m2", XQ, 384))
+        tt(R("fa", 3, 4 * XQ, 4), PA, R("hs", 0, XQ), AL.is_le)
+        tt(R("fa", 4 * XQ + 3, 1536, 4), PB, R("hs", XQ, 384), AL.is_le)
 
         def twins():
             act(R("tw"), IND(R("sg"), R(lp)))
@@ -328,97 +339,118 @@ def rank_program(g, core, T, topo):
             fn, k = LANE[c]
             ts(R(fn, k, 64 * c, 4), R("p0", 0, 16 * c), R("hs", 16 * c + 15, 16 * c + 16), AL.is_lt)
 
+        def half(c):
+            fn, k = LANE[c]
+            ts(R(fn, k, 64 * c, 4), R("sgl", 384 * (23 - c), 384 * (23 - c) + 16 * c), 0.5, AL.is_gt)
+
         def rowsum(c):
             fn, k = LANE[c]
-            scan(R("jk", 128 * c + 128 - 8 * c, 128 * c + 128), R(fn, k, 32 * c, 4), R(fn, 32 * c + k, 64 * c, 4), AL.add, AL.add)
+            scan(R("jk", JW * c + JW - 8 * c, JW * c + JW), R(fn, k, 32 * c, 4), R(fn, 32 * c + k, 64 * c, 4), AL.add, AL.add, first=-128.0)
 
         def colsum(fn, w, start=False, stop=False):
+            quant("q" + fn, R(fn))
             mm(R("p6", 0, w), "bo", 0, "q" + fn, w, start=start, stop=stop)
 
-        tt(R("fa", 3, 1536, 4), P[0], R("hs"), AL.is_le)
-        if t == 0:
-            ts(R("jc"), R("jc"), col["z"], AL.add, 1.0 / 192.0, AL.mult)
-            ts(R("jb"), R("kcb", 0, 12), col["pm"], AL.add, -191.0, AL.add)
-            ts(R("kcb"), R("kcb"), 15.0, AL.add, col["pm"], AL.subtract)
         if t:
             twins()
-        sc = list(range(23, NV, -1))
-        sign(sc[0])
-        todo = []
-        for i, c in enumerate(sc):
-            if i + 1 < NS:
-                todo.append((sign, sc[i + 1]))
+        todo = [(sign, 23), (sign, 22), (relu, 23), (sign, 21), (relu, 22)] + [(sign, c) for c in range(17, NV + 1)] + [(relu, 21)]
+        for c in range(20, NV, -1):
+            todo.insert(len(todo) - 1, (sign, c))
             todo.append((relu, c))
-        for f, c in todo[:6]:
+        for f, c in todo[:T0]:
             f(c)
         if t == 0:
             twins()
-        layer(NV)
+        for f, c in todo[T0:]:
+            f(c)
+        layer(16)
         scan(R("rds"), R("r0"), R("fa", 3, 1536, 4), AL.mult, AL.add)
         if t == 0:
-            ts(R("kcb"), R("kcb"), col["b16"], AL.subtract)
-        for c in range(NV - 1, 0, -1):
+            ts(R("jc"), R("kcb"), col["pm"], AL.add, 384.0, AL.add)
+            ts(col["z"], col["b16"], -192.0 * 2.0 ** -8, AL.mult)
+            ts(R("jb"), R("kcb", 0, 12), col["pm"], AL.add, -191.0, AL.add)
+            tt(col["kc"], col["b16"], col["f0"], AL.add)
+            fill(R("jk", JW - 1, JW), -128.0)
+            ts(R("kcb"), R("kcb"), 15.0, AL.add, col["pm"], AL.subtract)
+            ts(R("jc"), R("jc"), col["z"], AL.add, 1.0 / 192.0, AL.mult)
+            for n, ls, w in TILES[3:]:
+                fill(R(n, 64 * ls[-1], 4 * w), 0.0)
+            ts(R("kcb", 0, NV + 1), R("kcb", 0, NV + 1), col["kc"], AL.subtract, -128.0, AL.add)
+            ts(R("kcb", NV + 1, 24), R("kcb", NV + 1, 24), col["kc"], AL.subtract)
+            act(R("cm"), IND(R("cmw"), R("pmo")))
+        for c in range(15, 0, -1):
             layer(c)
-            rowsum(c + 1)
-            if c == (14 if t else 8):
+            if c >= 4:
+                rowsum(c + 1)
+            if c == (14 if t else T1):
                 twins2()
-            if c == (13 if t else 7):
+            if c == (13 if t else T1 - 1):
                 twins3()
             if c == 13:
-                tt(R("kr", 0, 24), R("kcb"), R("rds", 15, 384, 16), AL.subtract)
-            if c == 12 and NV == 16:
+                tt(R("kr"), R("kcb"), R("rds", 15, 384, 16), AL.subtract)
+            if c == 12:
                 quant("qfc", R("fc"))
-            if c == 10:
-                quant("qfa", R("fa"))
-                colsum("fa", 384, start=True)
-                if NV == 16:
-                    colsum("fc", 256)
-                for f, k in todo[6:]:
-                    f(k)
+                if t == 0:
+                    quant("bo", R("bot"))
+            if c == 11:
+                scan(R("bt"), R("tb"), R("sg"))
             if c == 8:
                 quant("qfd", R("fd"))
-                colsum("fd", 192)
+            if c == QA:
+                colsum("fa", 384, start=True)
+                mm(R("p6", 0, 256), "bo", 0, "qfc", 256, False, False)
+            if c == min(QA, 8):
+                mm(R("p6", 0, 192), "bo", 0, "qfd", 192, False, False)
+            if c == 7:
+                for k in range(17, NV + 1):
+                    half(k)
+            if c == 6:
+                for k in range(17, NV + 1):
+                    rowsum(k)
+            if c == 4:
+                colsum("fe", 128)
+        colsum("fb", 320)
+        colsum("ff", 128, stop=True)
         if t == 0:
-            act(R("pw", 768, 1152), R("pw", 0, 384))
             quant("eq", R("iet"))
             for b in range(4):
                 mm(P[2 + b], "eq", 128 * b, "xq", 384)
         tt(R("ow"), R("bt", 15, 384, 16), R(lb), AL.add)
-        rowsum(1)
-        quant("qf", R("ft", 4 * 1152, 4 * 1344), 1152, 1344)
-        colsum("fe", 128)
-        mm(R("p6", 0, 128), "bo", 0, "qf", 128, False, False, lo=1280)
+        for c in (1, 2):
+            rowsum(c)
         ts(R("off16"), R("ow"), 192.0, AL.mult, 0.25, AL.add)
-        tt(R("kr", 24, 25 + NV), R("kr", 0, NV + 1), R("jk", 127, 128 * (NV + 1), 128), AL.subtract)
-        if NV < 16:
-            quant("qfc", R("fc"))
-            colsum("fc", 256)
-        quant("qfb", R("fb"))
-        colsum("fb", 320, stop=True)
         act(R("pay"), IND(R("pw"), R("off16")))
-        tt(R("kr", 25 + NV, 48), R("kr", NV + 1, 24), R("ru", NV + 1, 24), AL.subtract)
+        for c in (3, 4):
+            rowsum(c)
+        tt(R("cm", 16 * (NV + 1) + 15, 384, 16), R("kr", NV + 1, 24), R("ru", NV + 1, 24), AL.subtract)
         if t == 0:
             fill(R("alt", 0, 384, 2), 0.0)
+        tt(R("cm", 15, 16 * (NV + 1), 16), R("kr", 0, NV + 1), R("jk", JW - 1, JW * (NV + 1), JW), AL.subtract)
+        if t == 0:
             fill(R("alt", 1, 384, 2), 2.0 ** -12)
             ts(R("mn"), R("k16", 0, 192), col["pm"], AL.is_le, 1024.0, AL.mult)
+        scan(R("mc"), P[6], R("cm"), AL.max, AL.add, first=-3 * BV)
+        if t == 0:
             ts(col["bb1"], col["b16"], 2.0 ** -9, AL.mult, 1.0, AL.add)
+            ts(col["z2"], col["b4"], -4.0, AL.mult, -1.0, AL.add)
+        ts(R("rk16"), R("mc", 15, 384, 16), col["f0"], AL.add)
+        if t == 0:
             ts(col["h4"], col["b4"], 1.0, AL.add)
             tt(col["h16"], col["b16"], col["b1"], AL.add)
-            ts(col["z2"], col["b4"], -4.0, AL.mult, -1.0, AL.add)
-        scan(R("mc"), R("t16"), P[6])
+        cp(IND(R("sp"), R("rk16")), R("pay"))
         if t == 0:
             tt(col["pbn"], col["z2"], col["b1"], AL.add)
-        tt(R("kr", 48, 72), R("mc", 15, 384, 16), R("kr", 24, 48), AL.add)
-        if t == 0:
             fill(R("ak", 384, 512), 0.0)
-            fill(R("al", 384, 512), 0.0)
-        cp(R("rk16"), R("kr", 48, 72))
-        cp(IND(R("sp"), R("rk16")), R("pay"))
         for b in range(4):
             act(R("fh", b, 1536, 4), P[2 + b], scale=0.5)
-        act(R("spa"), R("sp"), AF.Abs)
         act(R("lr"), IND(R("iota0", 0, 384), R(lo)))
+        act(R("spa"), R("sp"), AF.Abs)
+        if t == 0:
+            act(R("t4"), IND(R("t4w"), R("pmo")))
+        for b in range(4):
+            act(R("f32", b, 1536, 4), P[2 + b], scale=32.0)
         act(R("ew"), R("iota0", 0, 384))
+        act(R("tu"), R("lr"))
 
         def pairs(a, b):
             scan(R("kq", a, b), R("alt", a, b), R("spa", a, b), AL.mult, AL.add)
@@ -426,89 +458,91 @@ def rank_program(g, core, T, topo):
         mk, jbf, pp1, pp2, nn = [R("pp", 12 * i, 12 * i + 12) for i in range(5)]
         F = R("fcum", 191, 192)
         ts(R("fl"), R("sp", 1, 384, 2), 0.0, AL.is_lt)
+        if t == 0:
+            fill(R("al", 384, 512), 0.0)
+            quant("vq", R("vt"))
         scan(R("fcum"), R("fl"), R("fl"))
         scan(R("flc"), R("tb", 0, 192), R("fl"))
         scan(R("fc2"), R("mn"), R("fcum"), AL.add, AL.min)
         ts(jbf, R("jb"), F, AL.add)
         ts(mk, R("flc", 15, 192, 16), col["bb1"], AL.subtract, 1024.0, AL.mult)
+        pairs(0, 96)
         tt(pp1, jbf, R("fc2", 15, 192, 16), AL.subtract)
         tt(pp2, R("fc2", 15, 192, 16), mk, AL.add)
-        pairs(0, 128)
+        pairs(96, 240)
         tt(nn, pp1, pp2, AL.max)
-        pairs(128, 256)
+        pairs(240, 384)
         ts(R("n16"), nn, F, AL.subtract, 191.0, AL.add)
-        pairs(256, 384)
         cp(IND(R("kqs"), R("n16")), R("kq", 1, 384, 2))
         scan(R("c4"), R("t4", 0, 192), R("kqs"))
         scan(R("c16"), R("t16", 0, 192), R("kqs"))
-        ts(R("t4q"), R("c4", 3, 192, 4), col["h4"], AL.subtract)
         ts(R("kqi", 0, 48), R("c4", 3, 192, 4), 4096.0, AL.mult)
-        ts(R("kqi", 48, 54), R("c16", 96 + 15, 192, 16), 4096.0, AL.mult)
+        ts(R("t4q"), R("c4", 3, 192, 4), col["h4"], AL.subtract)
         ts(R("q16", 0, 12), R("c16", 15, 192, 16), col["h16"], AL.subtract, 0.25, AL.mult)
-        ts(R("kqi", 54, 108), R("kqi", 0, 54), 4095, AL.bitwise_and)
-        act(R("fq", 0, 192), IND(R("fh"), R("t4q", 0, 12)))
+        ts(R("kqi", 48, 54), R("c16", 96 + 15, 192, 16), 4096.0, AL.mult)
+        ts(R("kqi", 54, 102), R("kqi", 0, 48), 4095, AL.bitwise_and)
         act(R("lqk"), IND(R("lr"), R("q16", 0, 6)))
+        act(R("fq", 0, 192), IND(R("fh"), R("t4q", 0, 12)))
         act(R("fq", 192, 384), IND(R("fh"), R("t4q", 12, 24)))
         act(R("fq", 384, 768), IND(R("fh"), R("t4q", 24, 48)))
-        act(R("tu"), R("lr"))
+        ts(R("kqi", 102, 108), R("kqi", 48, 54), 4095, AL.bitwise_and)
         ts(R("t4k"), R("kqi", 54, 102), 1.0, AL.subtract)
-        ts(R("q16", 12, 18), R("kqi", 102, 108), col["b1"], AL.subtract, 0.25, AL.mult)
-        tt(R("ak", 0, 192), IND(R("fh"), R("t4k", 0, 12)), R("fq", 0, 192), AL.add)
         scan(R("nm4"), R("t4", 0, 96), R("lqk"))
         scan(R("nm16"), R("t16", 0, 96), R("lqk"))
+        ts(R("q16", 12, 18), R("kqi", 102, 108), col["b1"], AL.subtract, 0.25, AL.mult)
         ts(R(sn, 0, 24), R("nm4", 3, 96, 4), 4.0, AL.mult, col["pbn"], AL.add)
         ts(R(sn, 24, 30), R("nm16", 15, 96, 16), col["b16"], AL.subtract)
         send(rank + d, "rn%d" % t, (R(ln, 0, 30), R(sn, 0, 30)))
+        tt(R("ak", 0, 192), IND(R("fh"), R("t4k", 0, 12)), R("fq", 0, 192), AL.add)
         tt(R("ak", 192, 384), IND(R("fh"), R("t4k", 12, 24)), R("fq", 192, 384), AL.add)
         quant(qk, R("ak"))
         send(rank + d, "rc%d" % t, (R(vb, 0, 96, 1, "u8"), R(qk, 0, 96, 1, "u8")), (R(vb + "s", 0, 96), R(qk + "s", 0, 96)))
-        tt(R("al", 0, 384), IND(R("fh"), R("t4k", 24, 48)), R("fq", 384, 768), AL.add)
-        cp(IND(R("ew"), R("q16", 6, 12)), R("iota0", 384, 480))
-        quant("ql", R("al"))
         act(R("val", 0, 96), IND(R("lr"), R("q16", 12, 18)))
         act(R("val", 96, 192), IND(R("lr"), R("q16", 6, 12)))
         act(R("fl32"), R("fq", 384, 768), scale=64.0)
+        tt(R("al", 0, 384), IND(R("fh"), R("t4k", 24, 48)), R("fq", 384, 768), AL.add)
+        cp(IND(R("tu"), R("q16", 6, 18)), R("val"))
+        act(R("nl"), IND(R("tu"), R(lp)))
+        quant("ql", R("al"))
+        cp(IND(R("ew"), R("q16", 6, 12)), R("iota0", 384, 480))
         act(R("fn32"), IND(R("fh"), R(ln, 0, 24)), scale=64.0)
         left = ("p0", "p1", "p6", "p7")
         for b in range(4):
             mm(R(left[b], 0, 128), "wq", 128 * b, "ql", 128)
-        cp(IND(R("tu"), R("q16", 6, 18)), R("val"))
-        act(R("nl"), IND(R("tu"), R(lp)))
-        for b in range(4):
-            tt(R("sl", b, 384, 4), R(left[b], 0, 96), R("fl32", b, 384, 4), AL.add)
-        act(R("rl"), R("sl"), scale=2.0 ** -6)
-        cp(IND(R("ew"), R(ln, 24, 30)), R("iota0", 480, 576))
-        if t == 0:
-            quant("vq", R("vt"))
-        scan(R("ec"), R("t4"), R("ew"))
-        for b in range(4):
-            mm(R("p%d" % (2 + b), 0, 128), "wq", 128 * b, vb, 128)
-        for b in range(4):
-            tt(R("sa", b, 384, 4), R("p%d" % (2 + b), 0, 96), R("fn32", b, 384, 4), AL.add)
-            act(R("ra", b, 384, 4), R("sa", b, 384, 4), scale=2.0 ** -6)
-            if b == 0:
-                ts(R("e4"), R("ec", 3, 384, 4), 4.0, AL.mult, col["pbn"], AL.add)
+        tt(R("rl", 0, 384, 4), R(left[0], 0, 96), R("fl32", 0, 384, 4), AL.add)
+        tt(R("rl", 1, 384, 4), R(left[1], 0, 96), R("fl32", 1, 384, 4), AL.add)
         scan(R("nlc"), R("t16"), R("nl"))
-        act(R(xn, 4 * XA, 1536), IND(R("fw"), R("e4", XA // 4, 96)), scale=2.0)
-        ts(R(xn, 0, 4 * XA), IND(R("fw"), R("e4", 0, XA // 4)), 2.0, AL.mult)
+        cp(IND(R("ew"), R(ln, 24, 30)), R("iota0", 480, 576))
         ts(R(st), R("nlc", 15, 384, 16), col["b16"], AL.subtract)
         if t + 1 < NR:
             send2(R(st), "rt%d" % t, (rank - d, R("lo%d" % (t + 1))), (rank + d, R("lp%d" % (t + 1))))
         else:
             send(rank - d, "rt%d" % t, (R("lo3"), R(st)))
+        tt(R("rl", 2, 384, 4), R(left[2], 0, 96), R("fl32", 2, 384, 4), AL.add)
+        scan(R("ec"), R("t4"), R("ew"))
+        tt(R("rl", 3, 384, 4), R(left[3], 0, 96), R("fl32", 3, 384, 4), AL.add)
+        for b in range(4):
+            mm(R("p%d" % (2 + b), 0, 128), "wq", 128 * b, vb, 128)
+        for b in range(4):
+            tt(R("ra", b, 384, 4), R("p%d" % (2 + b), 0, 96), R("fn32", b, 384, 4), AL.add)
+            if b == 0:
+                ts(R("e4"), R("ec", 3, 384, 4), 4.0, AL.mult, col["pbn"], AL.add)
+        act(R(xn, 4 * XA, 4 * XQ), IND(R("fw"), R("e4", XA // 4, XQ // 4)), scale=2.0 ** -5)
+        act(R(xn, 4 * XQ, 1536), IND(R("fw"), R("e4", XQ // 4, 96)), scale=2.0 ** -5)
+        ts(R(xn, 0, 4 * XA), IND(R("fw"), R("e4", 0, XA // 4)), 2.0 ** -5, AL.mult)
         xquant(xn)
-    mm(R("p0", 0, XA), "vq", 0, "xq", XA)
-    mm(R("p1", 0, 384 - XA), "vq", 0, "xq", 384 - XA, lo=XA)
-    dma("s", T.oc[:, 0:4 * XA], ap(R("xq", 0, XA, 1, "u8")), [R("xq", 0, XA)], [], "oc_")
-    dma("s", T.oc[:, 4 * XA:1536], ap(R("xq", XA, 384, 1, "u8")), [R("xq", XA, 384)], [], "oc2")
-    act(R("ys", 0, XA), R("p0", 0, XA))
-    dma("a", T.y[:, 0:XA], ap(R("ys", 0, XA)), [R("ys", 0, XA)], [], "oy")
-    cp(R("ys", XA, 384), R("p1", 0, 384 - XA))
-    dma("s", T.y[:, XA:384], ap(R("ys", XA, 384)), [R("ys", XA, 384)], [], "oz")
-    for k in range(4):
-        dma("a", T.osc[4 * k:4 * k + 4, :], T.xqs[32 * k:32 * k + 4, 0:384], [R("xqs")], [], "o%d" % k)
     act(R("lr3"), IND(R("iota0", 0, 384), R("lo3")))
     dma("a", T.lk[:, :], T.lr3[0:128:16, :], [R("lr3")], [], "ok")
+    mm(R("p0", 0, XQ), "vq", 0, "xq", XQ)
+    mm(R("p1", 0, 384 - XQ), "vq", 0, "xq", 384 - XQ, lo=XQ)
+    dma("s", T.oc[:, 0:4 * XQ], ap(R("xq", 0, XQ, 1, "u8")), [R("xq", 0, XQ)], [], "oc_")
+    dma("s", T.oc[:, 4 * XQ:1536], ap(R("xq", XQ, 384, 1, "u8")), [R("xq", XQ, 384)], [], "oc2")
+    for k in range(4):
+        dma("s", T.osc[4 * k:4 * k + 4, :], T.xqs[32 * k:32 * k + 4, 0:384], [R("xqs")], [], "o%d" % k)
+    cp(R("ys", 0, XQ), R("p0", 0, XQ))
+    dma("s", T.y[:, 0:XQ], ap(R("ys", 0, XQ)), [R("ys", 0, XQ)], [], "oy")
+    act(R("ys", XQ, 384), R("p1", 0, 384 - XQ))
+    dma("a", T.y[:, XQ:384], ap(R("ys", XQ, 384)), [R("ys", XQ, 384)], [], "oz")
     for s in ("oc_", "oc2", "o0", "o1", "o2", "o3", "oy", "oz", "ok"):
         g.wait_ge(T.sem[s], 16)
     for s in ("v", "a", "p", "gc", "ls"):

@@ -5,14 +5,21 @@ AL, AF = AluOpType, ActivationFunctionType
 NR = 3
 BIG = 2.0 ** 90
 BV = 2048.0
-NV = 17
+NP2 = 3
+SORD = [15, 14, 13, 23, 22, 21, 20]
+NRS = 4
 JW = 160
-QA = 8
-T0, T1 = 5, 11
-XA = 160
-XQ = 256
-TILES = [("fa", [23, 22, 21], 384), ("fb", [20, 19, 18, 17], 320), ("fc", [16, 15, 14, 13], 256),
-         ("fd", [12, 11, 10, 9], 192), ("fe", [8, 7, 6, 5], 128), ("ff", [4, 3, 2, 1], 128)]
+LQ = 1
+WIN = ["al tu ql e1 l0 l1 nl e2 st l2 ec l3 a0 e4 a1 a2 a3"] * 3
+B0 = 1
+T0, T1 = [5, 3], [9, 5]
+_A = "L11 d2 L19 rds L18 L17 L16 kr fa R19 R18 R17 tw L10 sb L9 L12 L8 bt R16 R11 R10 R9 fd L7 L6 L5 L4 R12 R8 R7 R6 R5 fe fc L3 L2 L1 kr3 fb ff ow kr2 off cm"
+_B = "L11 d2 bo rds L19 L18 L17 L16 kr fa R19 R18 R17 L10 L9 L12 L8 bt R16 R11 R10 R9 tw fd L7 sb L6 L5 L4 R12 R8 R7 R6 R5 fe fc L3 L2 L1 kr3 fb ff eq ow kr2 off cm"
+ORDER = [_B.split(), _A.split()]
+PRE = ["q m0 m1 h0 h1 d0 m2 d1 h2", "m0 q m1 h0 h1 d0 m2 d1 h2"]
+XA = [0, 48]
+TILES = [("fa", [19, 18, 17], 384), ("fb", [23, 22, 21, 20], 368), ("fc", [15, 14, 13, 12], 240),
+         ("fd", [16, 11, 10, 9], 256), ("fe", [8, 7, 6, 5], 128), ("ff", [4, 3, 2, 1], 128)]
 LANE = {_c: (_n, _k) for _n, _l, _w in TILES for _k, _c in enumerate(_l)}
 
 SCRATCH, WHERE = {}, {}
@@ -38,11 +45,13 @@ def _each(text, dtype):
         _s([(n, int(c))], dtype)
 
 
-_each("xt0:1536 xt1:1536 xt2:1536 xt3:1536 ut:512 vt:512 iet:2048 bot:512 zt:512 ak:512 al:512 one:128 sg:384 bt:384 rds:384 "
-      "tw:384 twc:384 sgl:2688 jk:3360 fh:1536", "bfloat16")
-_s([("k16", 384), ("mb", 384), ("rs", 384), ("r0", 384), ("tb", 384), ("t16", 384), ("t4", 384), ("alt", 384), ("mn", 192)], "bfloat16", buf="kb")
-_s([("fl", 192), ("flc", 192), ("fcum", 192), ("fc2", 192)], "bfloat16", buf="fs")
-_s([("f32", 1536), ("rl", 384), ("ra", 384)], "bfloat16", buf="fw")
+_each("xt0:1536 xt1:1536 xt2:1536 xt3:1536 ut:512 vt:512 iet:2048 bot:512 zt:512 ak:512 al:512 one:128 sg:384 rds:384 "
+      "tw:384 sgl:3584 jk:3200 fh:1536 lr:384 tu:384 ew:384 ep:192", "bfloat16")
+_s([("k16", 384), ("mb", 128), ("rs", 128), ("r0", 384), ("t16", 384), ("t4", 192), ("t16h", 384), ("t4h", 384), ("alt", 384), ("mn", 192)],
+   "bfloat16", buf="kb")
+_s([("fl", 192), ("fcum", 192), ("fc2", 192), ("lqk", 96), ("val", 192), ("nl", 384)], "bfloat16", buf="fs")
+_s([("nm4", 96), ("nm16", 96), ("nlc", 384), ("ec", 384), ("bt", 384), ("twc", 384), ("flc", 192)], "float16", buf="hf")
+_s([("f32", 1536), ("rl", 384), ("gap", 136), ("ra", 768)], "bfloat16", buf="fw")
 _s([(_n, 4 * _w) for _n, _l, _w in TILES], "bfloat16", buf="ft")
 _s([("q" + _n, _w) for _n, _l, _w in TILES], "codes", buf="qf")
 _each("xq:384 uq:128 urs:128 urb:128 vq:128 eq:512 bo:128 wq:512 ql:128", "codes")
@@ -51,17 +60,16 @@ for _t in "012":
     _each("sn%s:32 ln%s:32 st%s:24 lp%s:24 lo%s:24" % (_t, _t, _t, _t, _t), "uint16")
     _each("sb%s:24 lb%s:24" % (_t, _t), "float32")
 _each("lo3:24", "uint16")
-_s([(_n, 16) for _n in ("ks", "ks4", "t16w", "t4w", "cmw", "ta", "tn", "ta2", "tn2", "bw")]
-   + [("cols", 24), ("kcb", 24), ("jc", 24), ("jb", 12), ("bi", 32)], "float32", buf="kw")
-_s([("c4", 192), ("c16", 192), ("kq", 384), ("lqk", 96), ("nm4", 96), ("nm16", 96)], "float32", buf="cc")
-_s([("mc", 384), ("nl", 384), ("nlc", 384), ("ec", 384)], "float32", buf="sc3")
-_each("iota0:576 pw:1152 m2:384 hs:384 cm:384 ru:24 kr:24 ow:24 pay:384 sp:384 spa:384 kqs:192 pp:60 "
-      "fq:768 fl32:384 fn32:384 val:192 tu:384 ew:384 lr:384 lr3:384 ys:384", "float32")
-_each("li:24 pi:14 kqi:108", "int32")
-_each("pmo:24 uo16:16 bo16:32 off16:24 rk16:24 n16:12 t4q:48 t4k:48 q16:18 e4:96", "uint16")
+_s([(_n, 24) for _n in ("ks", "t16w", "ta", "tn", "cols", "kcb", "jc")] + [(_n, 16) for _n in ("ks4", "t4w", "bw", "ui", "jb")] + [("bi", 32)],
+   "float32", buf="kw")
+_s([("c4", 192), ("c16", 192), ("kq", 384), ("mc", 384)], "float32", buf="cc")
+_each("iota0:384 pw:1152 m2:384 hs:384 cm:384 ru:24 kr:24 ow:24 pay:384 sp:384 spa:384 kqs:192 pp:60 "
+      "fq:768 fl32:384 fn32:384 lr3:384 ys:384", "float32")
+_each("li:24 pi:6 kqi:108", "int32")
+_each("pmo:24 pmo1:24 uo16:16 bo16:32 off16:24 rk16:24 n16:12 t4q:48 t4k:48 q16:18 e4:96", "uint16")
 _s([("p%d" % _b, 512) for _b in range(8)], "float32", "psum", "ps")
 
-SEMAPHORES = ("v a p gc ls dx dx2 du dw ds dv dl z0 z1 z2 z3 oy oz ok oc_ oc2 o0 o1 o2 o3 "
+SEMAPHORES = ("v a p gc ls dx0 dx1 dx2 du dw ds dv dl z0 z1 z2 z3 z4 z5 z6 z7 y0 y1 y2 y3 y4 y5 y6 y7 y8 y9 oy oz ok oc_ oc2 o0 o1 o2 o3 "
               "rb0 rb1 rb2 rn0 rn1 rn2 rc0 rc1 rc2 rl0 rt0 rt1 rt2").split()
 
 
@@ -167,10 +175,10 @@ def rank_program(g, core, T, topo):
     def act(o, i, f=AF.Copy, scale=None, accum=None, bias=None):
         kw = {} if scale is None else {"scale": scale}
         if bias is not None:
-            kw["bias"] = ap(bias)
+            kw["bias"] = ap(bias) if isinstance(bias, tuple) else bias
         if accum is not None:
             kw["accum_out"] = ap(accum)
-        op("a", [i] + ([bias] if bias else []), [o] + ([accum] if accum else []), lambda: g.scalar.activation(ap(o), ap(i), f, **kw))
+        op("a", [i] + ([bias] if isinstance(bias, tuple) else []), [o] + ([accum] if accum else []), lambda: g.scalar.activation(ap(o), ap(i), f, **kw))
 
     def mm(o, wn, wlo, xn, n, start=True, stop=True, lo=0):
         w, ws = R(wn, wlo, wlo + 128), R(wn + "s", wlo, wlo + 128)
@@ -215,242 +223,256 @@ def rank_program(g, core, T, topo):
 
     dma("a", ap(R("li")), T.link[:, :], [], [R("li")], "dl")
     dma("s", ap(R("ut")), T.u[:, :], [], [R("ut")], "du")
-    dma("a", ap(R("xt0", 0, 4 * XQ)), T.x[:, 0:4 * XQ], [], [R("xt0", 0, 4 * XQ)], "dx")
-    dma("s", ap(R("xt0", 4 * XQ, 1536)), T.x[:, 4 * XQ:1536], [], [R("xt0", 4 * XQ, 1536)], "dx2")
+    for i, q in ((0, "a"), (1, "s"), (2, "a")):
+        dma(q, ap(R("xt0", 512 * i, 512 * i + 512)), T.x[:, 512 * i:512 * i + 512], [], [R("xt0", 512 * i, 512 * i + 512)], "dx%d" % i)
     fill(R("zt"), 0.0)
+    for i, (n, ls, w) in enumerate(TILES):
+        z = R(n, 64 * ls[-1], 4 * w)
+        assert z[2] - z[1] <= 512
+        dma("s", ap(z), ap(R("zt", 0, z[2] - z[1])), [R("zt")], [z], "y%d" % i)
     for b in range(4):
         dma("s", ap(R("iet", 512 * b, 512 * b + 512)), ap(R("zt")), [R("zt")], [R("iet", 512 * b, 512 * b + 512)], "z%d" % b)
+    for i, z in enumerate((R("ak", 384, 512), R("al", 384, 512), R("fw", 1920, 2432), R("fw", 2432, 2824))):
+        dma("s", ap(z), ap(R("zt", 0, z[2] - z[1])), [R("zt")], [z], "y%d" % (6 + i))
     dma("s", ap(R("wq", bit="u8")), T.wc[:, :], [], [R("wq")], "dw")
     dma("s", ap(R("wqs")), T.ws[:, :], [], [R("wqs")], "ds")
     dma("s", ap(R("vt")), T.v[:, :], [], [R("vt")], "dv")
 
-    UO = R("pi", 6, 14)
     fine = {"allow_small_or_imprecise_dtypes": True}
     iota(R("pi", 0, 1), [[1, 1]], 1)
-    iota(R("ks"), [[1, 16]], **fine)
-    iota(UO, [[16, 8]])
-    iota(R("iota0", 0, 384), [[1, 384]], **fine)
+    iota(R("ks"), [[1, 24]], **fine)
+    iota(R("iota0"), [[1, 384]], **fine)
+    iota(R("ui"), [[1, 2], [16, 8]], **fine)
+    iota(R("kcb"), [[16, 24]], **fine)
     iota(R("ks4"), [[0, 4], [1, 4]], **fine)
     iota(R("bi"), [[1, 8], [0, 4]], **fine)
-    iota(R("kcb"), [[16, 24]], **fine)
 
     col = {n: R("cols", i, i + 1) for i, n in enumerate(
-        ("pm", "pm1", "pm0", "p4", "p41", "b1", "nb1", "pg", "b16", "b4", "bb1", "h4", "h16", "pbn", "tiny", "z", "z2", "f0", "kc"))}
+        ("pm", "pm1", "p4", "p41", "b1", "nb1", "pg", "b16", "b4", "bb1", "h4", "h16", "pbn", "pbe", "s16", "z", "z2", "f0", "kc"))}
     ts(R("pi", 1, 2), R("pi", 0, 1), 15, AL.bitwise_and)
     ts(R("pi", 2, 3), R("pi", 0, 1), 2, AL.logical_shift_right, 3, AL.bitwise_and)
     ts(R("pi", 3, 4), R("pi", 0, 1), 3, AL.bitwise_and)
     ts(R("pi", 4, 5), R("pi", 0, 1), 4, AL.logical_shift_right)
     cp(col["pm"], R("pi", 1, 2))
     ts(col["pm1"], R("pi", 1, 2), 1.0, AL.add)
-    ts(col["pm0"], R("pi", 1, 2), -1.0, AL.add)
     ts(col["b1"], R("pi", 3, 4), 1.0, AL.add)
+    fill(R("ru"), 0.0)
     ts(R("pmo"), R("zt", 0, 24), col["pm"], AL.add)
     ts(R("ta"), R("ks"), col["pm"], AL.is_equal, -3 * BV, AL.mult)
     ts(R("tn"), R("ks"), col["pm1"], AL.is_equal, BV, AL.mult)
     act(R("k16"), IND(R("ks"), R("pmo")))
     ts(col["nb1"], col["b1"], -1.0, AL.mult)
-    ts(R("ta2"), R("ks"), col["pm0"], AL.is_equal, -3 * BV, AL.mult)
-    ts(R("tn2"), R("ks"), col["pm"], AL.is_equal, BV, AL.mult)
+    ts(R("pmo1"), R("zt", 0, 24), col["pm1"], AL.add)
     tt(R("t16w"), R("ta"), R("tn"), AL.add)
     cp(col["p4"], R("pi", 2, 3))
     ts(col["p41"], R("pi", 2, 3), 1.0, AL.add)
-    tt(R("cmw"), R("ta2"), R("tn2"), AL.add)
     act(R("t16"), IND(R("t16w"), R("pmo")))
-    act(R("pw", 0, 384), R("iota0", 0, 384), AF.Identity, scale=4.0, bias=col["b1"])
-    act(R("pw", 384, 768), R("iota0", 0, 384), AF.Identity, scale=-4.0, bias=col["nb1"])
-    ts(R("uo16", 0, 8), UO, 0.0, AL.add)
-    ts(R("uo16", 8, 16), UO, 1.0, AL.add)
+    act(R("pw", 0, 384), R("iota0"), AF.Identity, scale=4.0, bias=col["b1"])
+    act(R("pw", 384, 768), R("iota0"), AF.Identity, scale=-4.0, bias=col["nb1"])
     cp(col["pg"], R("pi", 4, 5))
     ts(col["b16"], col["pm"], 14.5, AL.is_lt, BV, AL.mult)
-    ts(col["b4"], col["p4"], 2.5, AL.is_lt, BV, AL.mult)
     ts(col["f0"], col["pm"], 0.5, AL.is_lt, 3 * BV, AL.mult)
-    fill(col["tiny"], -1.0e-36)
-    fill(R("one"), 1.0)
-    for n, ls, w in TILES[:3]:
-        fill(R(n, 64 * ls[-1], 4 * w), 0.0)
-    ts(R("mb"), R("k16"), col["pm"], AL.not_equal, -BIG, AL.mult)
+    ts(col["b4"], col["p4"], 2.5, AL.is_lt, BV, AL.mult)
+    fill(R("ru", 17, 20), 128.0)
+    ts(col["z"], col["b16"], -192.0, AL.mult, col["pm"], AL.add)
+    ts(col["kc"], col["b16"], col["f0"], AL.add, col["pm"], AL.add)
+    ts(R("bw"), R("ks", 0, 16), col["pg"], AL.is_equal)
+    cp(R("uo16"), R("ui"))
+    ts(R("mb"), R("k16", 0, 128), col["pm"], AL.not_equal, -BIG, AL.mult)
+    ts(R("rs"), R("k16", 0, 128), 0.5, AL.is_lt, -4 * BIG, AL.mult)
+    ts(R("jc"), R("kcb"), col["z"], AL.add, 384.0, AL.add)
+    ts(R("jb", 0, 12), R("kcb", 0, 12), col["pm"], AL.add, -191.0, AL.add)
+    ts(R("r0"), R("k16"), 0.5, AL.is_gt)
     cp(R("lo0"), R("li"))
-    ts(R("rs"), R("k16"), 0.5, AL.is_lt, -4 * BIG, AL.mult)
     send(rank + 1, "rl0", (R("lp0"), R("lo0")))
-    iota(R("iota0", 384, 576), [[1, 192]], base=384, **fine)
+    iota(R("one"), [[0, 128]], base=1, **fine)
     for b in range(4):
         asel(R("iet", 512 * b + b, 512 * b + 512, 4), R("one"), [[-1, 128]], AL.is_equal, 0, 1)
-    ts(R("bw"), R("ks"), col["pg"], AL.is_equal)
+    iota(R("ep", 0, 96), [[1, 96]], base=128, **fine)
+    iota(R("ep", 96, 192), [[2, 96]], base=258, **fine)
+    ts(R("kcb"), R("kcb"), 15.0, AL.add, col["kc"], AL.subtract)
+    ts(R("jc"), R("jc"), 1.0 / 192.0, AL.mult)
     cp(R("bo16"), R("bi"))
-    ts(R("ta"), R("ks4"), col["p4"], AL.is_equal, -3 * BV, AL.mult)
-    ts(R("tn"), R("ks4"), col["p41"], AL.is_equal, BV, AL.mult)
-    ts(R("tb"), R("t16"), 2.0 ** -9, AL.mult)
-    tt(R("t4w"), R("ta"), R("tn"), AL.add)
+    ts(R("ta", 0, 16), R("ks4"), col["p4"], AL.is_equal, -3 * BV, AL.mult)
+    ts(R("tn", 0, 16), R("ks4"), col["p41"], AL.is_equal, BV, AL.mult)
+    ts(R("t16h"), R("t16"), 0.5, AL.mult)
     quant("uq", R("ut"))
-    ts(R("r0"), R("k16"), 0.5, AL.is_gt)
+    tt(R("t4w"), R("ta", 0, 16), R("tn", 0, 16), AL.add)
     for n, lo in (("urs", 0), ("urb", 8)):
         cp(R(n, bit="u32"), IND(R("uq", bit="u32"), R("uo16", lo, lo + 8)))
         act(R(n + "s"), IND(R("uqs"), R("uo16", lo, lo + 8)))
     act(R("pw", 768, 1152), R("pw", 0, 384))
     act(R("bot"), IND(R("bw"), R("bo16")))
 
-    def xquant(xn):
-        quant("xq", R(xn, 0, 4 * XQ), 0, XQ)
-        quant("xq", R(xn, 4 * XQ, 1536), XQ, 384)
+    P = [R("p%d" % b, 0, 384) for b in range(8)]
+    BANK, FB, LB = ("p4", "p5", "p7"), ("p4", "p5", "p7", "p2"), ("p1", "p0", "p3", "p6")
 
-    xquant("xt0")
+    def piece(xn, i, w="urs"):
+        quant("xq", R(xn, 512 * i, 512 * i + 512), 128 * i, 128 * i + 128)
+        mm(R(BANK[i], 0, 128), w, 0, "xq", 128, lo=128 * i)
+        if i == 1 and w == "urs":
+            mm(R("p2", 0, 240), w, 0, "xq", 240)
+
+    def masked(i):
+        tt(R("m2", 128 * i, 128 * i + 128), R(BANK[i], 0, 128), R("mb", 0, 128), AL.add)
+
+    def held(i):
+        scan(R("hs", 128 * i, 128 * i + 128), R("rs", 0, 128), R("m2", 128 * i, 128 * i + 128))
+
+    def diagonal(i):
+        tt(R("fa", 512 * i + 3, 512 * i + 512, 4), R(BANK[i], 0, 128), R("hs", 128 * i, 128 * i + 128), AL.is_le)
+
+    for i in range(3):
+        piece("xt0", i)
+    quant("vb0", R("zt"))
+    for k in (1, 2):
+        dma("s", ap(R("vb%d" % k, 96, 128, 1, "u8")), ap(R("vb0", 96, 128, 1, "u8")), [R("vb0")], [R("vb%d" % k)], "z%d" % (2 + 2 * k))
+        dma("s", ap(R("vb%ds" % k, 96, 128)), ap(R("vb0s", 96, 128)), [R("vb0s")], [R("vb%ds" % k)], "z%d" % (3 + 2 * k))
     for t in range(NR):
         d = 2 ** t
         xn, qk, vb = "xt%d" % (t + 1), "qk%d" % t, "vb%d" % t
         sb, lb, sn, ln, st, lp, lo = ["%s%d" % (n, t) for n in ("sb", "lb", "sn", "ln", "st", "lp", "lo")]
-        P = [R("p%d" % b, 0, 384) for b in range(8)]
-        PA, PB = R("p0", 0, XQ), R("p6", 0, 384 - XQ)
-        mm(PA, "urs", 0, "xq", XQ)
-        mm(PB, "urs", 0, "xq", 384 - XQ, lo=XQ)
-        mm(P[1], "urb", 0, "xq", 384)
-        mm(P[7], "urs", 0, "xq", 384)
-        if t:
-            for b in range(4):
-                mm(P[2 + b], "eq", 128 * b, "xq", 384)
-        else:
-            for k in range(NR):
-                quant("vb%d" % k, R("zt"))
-        act(R("sg"), P[1], AF.Sign, bias=col["tiny"])
-        tt(R("m2", 0, XQ), PA, R("mb", 0, XQ), AL.add)
-        tt(R("m2", XQ, 384), PB, R("mb", XQ, 384), AL.add)
-        scan(R("hs", 0, XQ), R("rs", 0, XQ), R("m2", 0, XQ))
-        scan(R("hs", XQ, 384), R("rs", XQ, 384), R("m2", XQ, 384))
-        tt(R("fa", 3, 4 * XQ, 4), PA, R("hs", 0, XQ), AL.is_le)
-        tt(R("fa", 4 * XQ + 3, 1536, 4), PB, R("hs", XQ, 384), AL.is_le)
+        for x in PRE[t > 0].split():
+            if x == "q":
+                if t:
+                    piece("xt%d" % t, 2)
+                mm(R("p3", 0, 304), "urs", 0, "xq", 304)
+                mm(P[1], "urb", 0, "xq", 384)
+                mm(R("p0", 0, 368), "urs", 0, "xq", 368)
+            else:
+                {"m": masked, "h": held, "d": diagonal}[x[0]](int(x[1]))
 
         def twins():
             act(R("tw"), IND(R("sg"), R(lp)))
 
         def twins2():
-            scan(R("twc"), R("tb"), R("tw"))
+            scan(R("twc"), R("t16h"), R("tw"))
 
         def twins3():
             tt(R(sb), R("twc", 15, 384, 16), R("jc"), AL.add)
             send(rank - d, "rb%d" % t, (R(lb), R(sb)))
 
         def sign(c):
-            act(R("sgl", 384 * (23 - c), 384 * (23 - c) + 16 * c), R("p7", 0, 16 * c), AF.Sign, scale=-1.0, bias=R("hs", 16 * c + 15, 16 * c + 16))
+            act(R("sgl", 384 * SORD.index(c), 384 * SORD.index(c) + 16 * c), R("p2" if c in SORD[:NP2] else "p0", 0, 16 * c), AF.Sign, scale=-1.0,
+                bias=R("hs", 16 * c + 15, 16 * c + 16))
 
         def relu(c):
             fn, k = LANE[c]
-            act(R(fn, k, 64 * c, 4), R("sgl", 384 * (23 - c), 384 * (23 - c) + 16 * c), AF.Relu, accum=R("ru", c, c + 1))
+            act(R(fn, k, 64 * c, 4), R("sgl", 384 * SORD.index(c), 384 * SORD.index(c) + 16 * c), AF.Relu, accum=R("ru", c, c + 1))
 
         def layer(c):
             fn, k = LANE[c]
-            ts(R(fn, k, 64 * c, 4), R("p0", 0, 16 * c), R("hs", 16 * c + 15, 16 * c + 16), AL.is_lt)
-
-        def half(c):
-            fn, k = LANE[c]
-            ts(R(fn, k, 64 * c, 4), R("sgl", 384 * (23 - c), 384 * (23 - c) + 16 * c), 0.5, AL.is_gt)
+            ts(R(fn, k, 64 * c, 4), R("p3", 0, 16 * c), R("hs", 16 * c + 15, 16 * c + 16), AL.is_lt)
 
         def rowsum(c):
             fn, k = LANE[c]
-            scan(R("jk", JW * c + JW - 8 * c, JW * c + JW), R(fn, k, 32 * c, 4), R(fn, 32 * c + k, 64 * c, 4), AL.add, AL.add, first=-128.0)
+            scan(R("jk", JW * c + JW - 8 * c, JW * c + JW), R(fn, k, 32 * c, 4), R(fn, 32 * c + k, 64 * c, 4), AL.add, AL.add,
+                 first=-128.0 if c > 16 else 0.0)
 
-        def colsum(fn, w, start=False, stop=False):
+        def rowsum2(c):
+            fn, k = LANE[c]
+            act(R("sgl", 3072 + 128 * (c % 4), 3072 + 128 * (c % 4) + 16 * c), R(fn, k, 64 * c, 4), accum=R("ru", c, c + 1))
+
+        order = ["fa"] + [n for n in ORDER[t > 0] if n[0] == "f" and n != "fa"]
+        ready = set()
+
+        def colsum(fn):
             quant("q" + fn, R(fn))
-            mm(R("p6", 0, w), "bo", 0, "q" + fn, w, start=start, stop=stop)
+            ready.add(fn)
+            while order and order[0] in ready:
+                n = order.pop(0)
+                w = WHERE["q" + n][2]
+                mm(R("p6", 0, w), "bo", 0, "q" + n, w, start=n == "fa", stop=not order)
 
-        if t:
-            twins()
-        todo = [(sign, 23), (sign, 22), (relu, 23), (sign, 21), (relu, 22)] + [(sign, c) for c in range(17, NV + 1)] + [(relu, 21)]
-        for c in range(20, NV, -1):
-            todo.insert(len(todo) - 1, (sign, c))
-            todo.append((relu, c))
-        for f, c in todo[:T0]:
+        nr, nv = NRS, min(SORD) - 1
+        todo = [(sign, SORD[0])]
+        for a, b in zip(SORD, SORD[1:]):
+            todo += [(sign, b), (relu, a)]
+        todo.append((relu, SORD[-1]))
+        for f, c in todo[:T0[t > 0]]:
+            f(c)
+        act(R("sg"), P[1], AF.Sign, bias=-1.0e-36)
+        for f, c in todo[T0[t > 0]:T1[t > 0]]:
+            f(c)
+        twins()
+        for f, c in todo[T1[t > 0]:]:
             f(c)
         if t == 0:
-            twins()
-        for f, c in todo[T0:]:
-            f(c)
-        layer(16)
-        scan(R("rds"), R("r0"), R("fa", 3, 1536, 4), AL.mult, AL.add)
-        if t == 0:
-            ts(R("jc"), R("kcb"), col["pm"], AL.add, 384.0, AL.add)
-            ts(col["z"], col["b16"], -192.0 * 2.0 ** -8, AL.mult)
-            ts(R("jb"), R("kcb", 0, 12), col["pm"], AL.add, -191.0, AL.add)
-            tt(col["kc"], col["b16"], col["f0"], AL.add)
-            fill(R("jk", JW - 1, JW), -128.0)
-            ts(R("kcb"), R("kcb"), 15.0, AL.add, col["pm"], AL.subtract)
-            ts(R("jc"), R("jc"), col["z"], AL.add, 1.0 / 192.0, AL.mult)
-            for n, ls, w in TILES[3:]:
-                fill(R(n, 64 * ls[-1], 4 * w), 0.0)
-            ts(R("kcb", 0, NV + 1), R("kcb", 0, NV + 1), col["kc"], AL.subtract, -128.0, AL.add)
-            ts(R("kcb", NV + 1, 24), R("kcb", NV + 1, 24), col["kc"], AL.subtract)
-            act(R("cm"), IND(R("cmw"), R("pmo")))
-        for c in range(15, 0, -1):
-            layer(c)
-            if c >= 4:
-                rowsum(c + 1)
-            if c == (14 if t else T1):
-                twins2()
-            if c == (13 if t else T1 - 1):
-                twins3()
-            if c == 13:
+            act(R("cm"), IND(R("t16w"), R("pmo1")))
+        for x in ORDER[t > 0]:
+            c = int(x[1:]) if x[0] in "LR" else 0
+            if x[0] == "L" and c not in SORD:
+                layer(c)
+                if c <= nr:
+                    rowsum2(c)
+            elif x[0] == "R" and nr < c and c not in SORD:
+                rowsum(c)
+            elif x == "kr3":
+                tt(R("kr", 16, 20), R("kr", 16, 20), R("jk", JW * 17 - 1, JW * 20, JW), AL.subtract)
+            elif x[0] == "f":
+                colsum(x)
+            elif x == "d2":
+                diagonal(2)
+                for b in range(4 if t else 0):
+                    mm(R(FB[b], 0, 384), "eq", 128 * b, "xq", 384)
+            elif x == "rds":
+                scan(R("rds"), R("r0"), R("fa", 3, 1536, 4), AL.mult, AL.add)
+            elif x == "kr":
                 tt(R("kr"), R("kcb"), R("rds", 15, 384, 16), AL.subtract)
-            if c == 12:
-                quant("qfc", R("fc"))
-                if t == 0:
-                    quant("bo", R("bot"))
-            if c == 11:
-                scan(R("bt"), R("tb"), R("sg"))
-            if c == 8:
-                quant("qfd", R("fd"))
-            if c == QA:
-                colsum("fa", 384, start=True)
-                mm(R("p6", 0, 256), "bo", 0, "qfc", 256, False, False)
-            if c == min(QA, 8):
-                mm(R("p6", 0, 192), "bo", 0, "qfd", 192, False, False)
-            if c == 7:
-                for k in range(17, NV + 1):
-                    half(k)
-            if c == 6:
-                for k in range(17, NV + 1):
-                    rowsum(k)
-            if c == 4:
-                colsum("fe", 128)
-        colsum("fb", 320)
-        colsum("ff", 128, stop=True)
-        if t == 0:
-            quant("eq", R("iet"))
-            for b in range(4):
-                mm(P[2 + b], "eq", 128 * b, "xq", 384)
-        tt(R("ow"), R("bt", 15, 384, 16), R(lb), AL.add)
-        for c in (1, 2):
-            rowsum(c)
-        ts(R("off16"), R("ow"), 192.0, AL.mult, 0.25, AL.add)
+            elif x == "kr2":
+                tt(R("kr", nr + 1, nv + 1), R("kr", nr + 1, nv + 1), R("jk", JW * (nr + 2) - 1, JW * (nv + 1), JW), AL.subtract)
+            elif x == "bt":
+                scan(R("bt"), R("t16h"), R("sg"))
+            elif x == "tw":
+                twins2()
+            elif x == "sb":
+                twins3()
+            elif x == "bo":
+                quant("bo", R("bot"))
+            elif x == "eq":
+                quant("eq", R("iet"))
+                for b in range(4):
+                    mm(R(FB[b], 0, 384), "eq", 128 * b, "xq", 384)
+            elif x == "ow":
+                tt(R("ow"), R("bt", 15, 384, 16), R(lb), AL.add)
+            elif x == "off":
+                ts(R("off16"), R("ow"), 192.0, AL.mult, 0.25, AL.add)
+            elif x == "cm":
+                tt(R("cm", 15, 384, 16), R("kr"), R("ru"), AL.subtract)
         act(R("pay"), IND(R("pw"), R("off16")))
-        for c in (3, 4):
-            rowsum(c)
-        tt(R("cm", 16 * (NV + 1) + 15, 384, 16), R("kr", NV + 1, 24), R("ru", NV + 1, 24), AL.subtract)
         if t == 0:
             fill(R("alt", 0, 384, 2), 0.0)
-        tt(R("cm", 15, 16 * (NV + 1), 16), R("kr", 0, NV + 1), R("jk", JW - 1, JW * (NV + 1), JW), AL.subtract)
-        if t == 0:
             fill(R("alt", 1, 384, 2), 2.0 ** -12)
             ts(R("mn"), R("k16", 0, 192), col["pm"], AL.is_le, 1024.0, AL.mult)
         scan(R("mc"), P[6], R("cm"), AL.max, AL.add, first=-3 * BV)
         if t == 0:
-            ts(col["bb1"], col["b16"], 2.0 ** -9, AL.mult, 1.0, AL.add)
-            ts(col["z2"], col["b4"], -4.0, AL.mult, -1.0, AL.add)
+            ts(col["bb1"], col["b16"], 0.5, AL.mult, 1.0, AL.add)
+            ts(col["z2"], col["b4"], -2.0, AL.mult, col["b1"], AL.add)
         ts(R("rk16"), R("mc", 15, 384, 16), col["f0"], AL.add)
         if t == 0:
             ts(col["h4"], col["b4"], 1.0, AL.add)
             tt(col["h16"], col["b16"], col["b1"], AL.add)
         cp(IND(R("sp"), R("rk16")), R("pay"))
         if t == 0:
-            tt(col["pbn"], col["z2"], col["b1"], AL.add)
-            fill(R("ak", 384, 512), 0.0)
+            ts(col["pbn"], col["z2"], 767.0, AL.add)
+            ts(col["pbe"], col["z2"], 1023.0, AL.add)
         for b in range(4):
-            act(R("fh", b, 1536, 4), P[2 + b], scale=0.5)
-        act(R("lr"), IND(R("iota0", 0, 384), R(lo)))
+            act(R("fh", b, 1536, 4), R(FB[b], 0, 384), scale=0.5)
+        if t:
+            act(R("lr"), IND(R("iota0"), R(lo)), AF.Identity, bias=-192.0)
         act(R("spa"), R("sp"), AF.Abs)
         if t == 0:
-            act(R("t4"), IND(R("t4w"), R("pmo")))
-        for b in range(4):
-            act(R("f32", b, 1536, 4), P[2 + b], scale=32.0)
-        act(R("ew"), R("iota0", 0, 384))
+            act(R("t4"), IND(R("t4w"), R("pmo", 0, 12)))
+            act(R("lr"), IND(R("iota0"), R(lo)), AF.Identity, bias=-192.0)
+            act(R("t4h"), IND(R("t4w"), R("pmo")), scale=0.5)
+
+        def bases(b0, b1):
+            for b in range(b0, b1):
+                act(R("f32", b, 1536, 4), R(FB[b], 0, 384), scale=32.0)
+
+        act(R("ew"), R("iota0"), AF.Identity, bias=-256.0)
         act(R("tu"), R("lr"))
+        bases(0, 4 if t else B0)
 
         def pairs(a, b):
             scan(R("kq", a, b), R("alt", a, b), R("spa", a, b), AL.mult, AL.add)
@@ -459,12 +481,12 @@ def rank_program(g, core, T, topo):
         F = R("fcum", 191, 192)
         ts(R("fl"), R("sp", 1, 384, 2), 0.0, AL.is_lt)
         if t == 0:
-            fill(R("al", 384, 512), 0.0)
+            ts(col["s16"], col["b16"], -0.5, AL.mult, 192.0, AL.add)
             quant("vq", R("vt"))
         scan(R("fcum"), R("fl"), R("fl"))
-        scan(R("flc"), R("tb", 0, 192), R("fl"))
+        scan(R("flc"), R("t16h", 0, 192), R("fl"))
         scan(R("fc2"), R("mn"), R("fcum"), AL.add, AL.min)
-        ts(jbf, R("jb"), F, AL.add)
+        ts(jbf, R("jb", 0, 12), F, AL.add)
         ts(mk, R("flc", 15, 192, 16), col["bb1"], AL.subtract, 1024.0, AL.mult)
         pairs(0, 96)
         tt(pp1, jbf, R("fc2", 15, 192, 16), AL.subtract)
@@ -481,17 +503,17 @@ def rank_program(g, core, T, topo):
         ts(R("q16", 0, 12), R("c16", 15, 192, 16), col["h16"], AL.subtract, 0.25, AL.mult)
         ts(R("kqi", 48, 54), R("c16", 96 + 15, 192, 16), 4096.0, AL.mult)
         ts(R("kqi", 54, 102), R("kqi", 0, 48), 4095, AL.bitwise_and)
-        act(R("lqk"), IND(R("lr"), R("q16", 0, 6)))
+        (cp if LQ else act)(R("lqk"), IND(R("lr"), R("q16", 0, 6)))
         act(R("fq", 0, 192), IND(R("fh"), R("t4q", 0, 12)))
         act(R("fq", 192, 384), IND(R("fh"), R("t4q", 12, 24)))
         act(R("fq", 384, 768), IND(R("fh"), R("t4q", 24, 48)))
         ts(R("kqi", 102, 108), R("kqi", 48, 54), 4095, AL.bitwise_and)
         ts(R("t4k"), R("kqi", 54, 102), 1.0, AL.subtract)
-        scan(R("nm4"), R("t4", 0, 96), R("lqk"))
-        scan(R("nm16"), R("t16", 0, 96), R("lqk"))
+        scan(R("nm4"), R("t4h", 0, 96), R("lqk"))
+        scan(R("nm16"), R("t16h", 0, 96), R("lqk"))
         ts(R("q16", 12, 18), R("kqi", 102, 108), col["b1"], AL.subtract, 0.25, AL.mult)
         ts(R(sn, 0, 24), R("nm4", 3, 96, 4), 4.0, AL.mult, col["pbn"], AL.add)
-        ts(R(sn, 24, 30), R("nm16", 15, 96, 16), col["b16"], AL.subtract)
+        ts(R(sn, 24, 30), R("nm16", 15, 96, 16), col["s16"], AL.add)
         send(rank + d, "rn%d" % t, (R(ln, 0, 30), R(sn, 0, 30)))
         tt(R("ak", 0, 192), IND(R("fh"), R("t4k", 0, 12)), R("fq", 0, 192), AL.add)
         tt(R("ak", 192, 384), IND(R("fh"), R("t4k", 12, 24)), R("fq", 192, 384), AL.add)
@@ -500,49 +522,66 @@ def rank_program(g, core, T, topo):
         act(R("val", 0, 96), IND(R("lr"), R("q16", 12, 18)))
         act(R("val", 96, 192), IND(R("lr"), R("q16", 6, 12)))
         act(R("fl32"), R("fq", 384, 768), scale=64.0)
-        tt(R("al", 0, 384), IND(R("fh"), R("t4k", 24, 48)), R("fq", 384, 768), AL.add)
-        cp(IND(R("tu"), R("q16", 6, 18)), R("val"))
-        act(R("nl"), IND(R("tu"), R(lp)))
-        quant("ql", R("al"))
-        cp(IND(R("ew"), R("q16", 6, 12)), R("iota0", 384, 480))
-        act(R("fn32"), IND(R("fh"), R(ln, 0, 24)), scale=64.0)
-        left = ("p0", "p1", "p6", "p7")
-        for b in range(4):
-            mm(R(left[b], 0, 128), "wq", 128 * b, "ql", 128)
-        tt(R("rl", 0, 384, 4), R(left[0], 0, 96), R("fl32", 0, 384, 4), AL.add)
-        tt(R("rl", 1, 384, 4), R(left[1], 0, 96), R("fl32", 1, 384, 4), AL.add)
-        scan(R("nlc"), R("t16"), R("nl"))
-        cp(IND(R("ew"), R(ln, 24, 30)), R("iota0", 480, 576))
-        ts(R(st), R("nlc", 15, 384, 16), col["b16"], AL.subtract)
-        if t + 1 < NR:
-            send2(R(st), "rt%d" % t, (rank - d, R("lo%d" % (t + 1))), (rank + d, R("lp%d" % (t + 1))))
-        else:
-            send(rank - d, "rt%d" % t, (R("lo3"), R(st)))
-        tt(R("rl", 2, 384, 4), R(left[2], 0, 96), R("fl32", 2, 384, 4), AL.add)
-        scan(R("ec"), R("t4"), R("ew"))
-        tt(R("rl", 3, 384, 4), R(left[3], 0, 96), R("fl32", 3, 384, 4), AL.add)
-        for b in range(4):
-            mm(R("p%d" % (2 + b), 0, 128), "wq", 128 * b, vb, 128)
-        for b in range(4):
-            tt(R("ra", b, 384, 4), R("p%d" % (2 + b), 0, 96), R("fn32", b, 384, 4), AL.add)
-            if b == 0:
-                ts(R("e4"), R("ec", 3, 384, 4), 4.0, AL.mult, col["pbn"], AL.add)
-        act(R(xn, 4 * XA, 4 * XQ), IND(R("fw"), R("e4", XA // 4, XQ // 4)), scale=2.0 ** -5)
-        act(R(xn, 4 * XQ, 1536), IND(R("fw"), R("e4", XQ // 4, 96)), scale=2.0 ** -5)
-        ts(R(xn, 0, 4 * XA), IND(R("fw"), R("e4", 0, XA // 4)), 2.0 ** -5, AL.mult)
-        xquant(xn)
-    act(R("lr3"), IND(R("iota0", 0, 384), R("lo3")))
+        if t == 0:
+            bases(B0, 4)
+        left = LB
+        for x in WIN[t].split():
+            if x == "al":
+                tt(R("al", 0, 384), IND(R("fh"), R("t4k", 24, 48)), R("fq", 384, 768), AL.add)
+            elif x == "tu":
+                cp(IND(R("tu"), R("q16", 6, 18)), R("val"))
+                act(R("nl"), IND(R("tu"), R(lp)))
+                act(R("fn32"), IND(R("fh"), R(ln, 0, 24)), scale=64.0)
+            elif x == "ql":
+                quant("ql", R("al"))
+                for b in range(4):
+                    mm(R(left[b], 0, 128), "wq", 128 * b, "ql", 128)
+            elif x == "e1":
+                cp(IND(R("ew"), R("q16", 6, 12)), R("ep", 0, 96))
+            elif x == "e2":
+                cp(IND(R("ew"), R(ln, 24, 30)), R("ep", 96, 192))
+            elif x[0] == "l":
+                b = int(x[1])
+                tt(R("rl", b, 384, 4), R(left[b], 0, 96), R("fl32", b, 384, 4), AL.add)
+            elif x == "nl":
+                scan(R("nlc"), R("t16h"), R("nl"))
+            elif x == "st":
+                ts(R(st), R("nlc", 15, 384, 16), col["s16"], AL.add)
+                if t + 1 < NR:
+                    send2(R(st), "rt%d" % t, (rank - d, R("lo%d" % (t + 1))), (rank + d, R("lp%d" % (t + 1))))
+                else:
+                    send(rank - d, "rt%d" % t, (R("lo3"), R(st)))
+            elif x == "ec":
+                scan(R("ec"), R("t4h"), R("ew"))
+            elif x == "e4":
+                ts(R("e4"), R("ec", 3, 384, 4), 4.0, AL.mult, col["pbe"], AL.add)
+            elif x[0] == "a":
+                b = int(x[1])
+                for k in range(0 if b else 4):
+                    mm(R(FB[k], 0, 128), "wq", 128 * k, vb, 128)
+                tt(R("ra", b, 768, 8), R(FB[b], 0, 96), R("fn32", b, 384, 4), AL.add)
+        last = t + 1 == NR
+        w, xa = ("vq", XA[1]) if last else ("urs", XA[0])
+        act(R(xn, 512, 1024), IND(R("fw"), R("e4", 32, 64)), scale=2.0 ** -5)
+        act(R(xn, 1024 + 4 * xa, 1536), IND(R("fw"), R("e4", 64 + xa // 4, 96)), scale=2.0 ** -5)
+        ts(R(xn, 0, 512), IND(R("fw"), R("e4", 0, 32)), 2.0 ** -5, AL.mult)
+        if xa:
+            ts(R(xn, 1024, 1024 + 4 * xa), IND(R("fw"), R("e4", 64, 64 + xa // 4)), 2.0 ** -5, AL.mult)
+        piece(xn, 0, w)
+        piece(xn, 1, w)
+        if last:
+            piece(xn, 2, w)
+    act(R("lr3"), IND(R("iota0"), R("lo3")))
     dma("a", T.lk[:, :], T.lr3[0:128:16, :], [R("lr3")], [], "ok")
-    mm(R("p0", 0, XQ), "vq", 0, "xq", XQ)
-    mm(R("p1", 0, 384 - XQ), "vq", 0, "xq", 384 - XQ, lo=XQ)
-    dma("s", T.oc[:, 0:4 * XQ], ap(R("xq", 0, XQ, 1, "u8")), [R("xq", 0, XQ)], [], "oc_")
-    dma("s", T.oc[:, 4 * XQ:1536], ap(R("xq", XQ, 384, 1, "u8")), [R("xq", XQ, 384)], [], "oc2")
+    dma("s", T.oc[:, 0:1024], ap(R("xq", 0, 256, 1, "u8")), [R("xq", 0, 256)], [], "oc_")
+    dma("s", T.oc[:, 1024:1536], ap(R("xq", 256, 384, 1, "u8")), [R("xq", 256, 384)], [], "oc2")
+    cp(R("ys", 0, 128), R(BANK[0], 0, 128))
+    cp(R("ys", 128, 256), R(BANK[1], 0, 128))
+    dma("s", T.y[:, 0:256], ap(R("ys", 0, 256)), [R("ys", 0, 256)], [], "oy")
+    cp(R("ys", 256, 384), R(BANK[2], 0, 128))
+    dma("s", T.y[:, 256:384], ap(R("ys", 256, 384)), [R("ys", 256, 384)], [], "oz")
     for k in range(4):
-        dma("s", T.osc[4 * k:4 * k + 4, :], T.xqs[32 * k:32 * k + 4, 0:384], [R("xqs")], [], "o%d" % k)
-    cp(R("ys", 0, XQ), R("p0", 0, XQ))
-    dma("s", T.y[:, 0:XQ], ap(R("ys", 0, XQ)), [R("ys", 0, XQ)], [], "oy")
-    act(R("ys", XQ, 384), R("p1", 0, 384 - XQ))
-    dma("a", T.y[:, XQ:384], ap(R("ys", XQ, 384)), [R("ys", XQ, 384)], [], "oz")
+        dma("a", T.osc[4 * k:4 * k + 4, :], T.xqs[32 * k:32 * k + 4, 0:384], [R("xqs")], [], "o%d" % k)
     for s in ("oc_", "oc2", "o0", "o1", "o2", "o3", "oy", "oz", "ok"):
         g.wait_ge(T.sem[s], 16)
     for s in ("v", "a", "p", "gc", "ls"):

@@ -5,20 +5,21 @@ AL, AF = AluOpType, ActivationFunctionType
 NR = 3
 BIG = 2.0 ** 90
 BV = 2048.0
-NP2 = 3
-SORD = [15, 14, 13, 23, 22, 21, 20]
-NRS = 4
 JW = 160
 LQ = 1
-WIN = ["al tu ql e1 l0 l1 nl e2 st l2 ec l3 a0 e4 a1 a2 a3"] * 3
-B0 = 1
-T0, T1 = [5, 3], [9, 5]
-_A = "L11 d2 L19 rds L18 L17 L16 kr fa R19 R18 R17 tw L10 sb L9 L12 L8 bt R16 R11 R10 R9 fd L7 L6 L5 L4 R12 R8 R7 R6 R5 fe fc L3 L2 L1 kr3 fb ff ow kr2 off cm"
-_B = "L11 d2 bo rds L19 L18 L17 L16 kr fa R19 R18 R17 L10 L9 L12 L8 bt R16 R11 R10 R9 tw fd L7 sb L6 L5 L4 R12 R8 R7 R6 R5 fe fc L3 L2 L1 kr3 fb ff eq ow kr2 off cm"
+WIN = (["al tu ng fn ql e2 l0 l1 ec l2 nl e3 l3 st e4 a0 S004 a1 a2 a3 S048 S104 S248 V204 V304 S148 V348 Q0 V38c Q1 S18c V28c S08c"] * 2
+       + ["al tu ng fn ql e2 l0 l1 ec l2 nl e3 l3 st e4 a0 S004 a1 a2 a3 S048 S104 S248 V204 V304 S148 V348 Q0 V38c Q1 S18c V28c S08c lk Q2"])
+B0, B1, EW = [0, 1], [1, 2], [0, 0]
+PEO = "310"
+KEEP = "ck cl qk ik il lq and ql n16 k16 s16 N a0 a1 a2 a3 q C"
+_A = ("m0 q m1 h0 h1 d0 m2 d1 h2 L11 d2 F L19 rds L18 L17 L16 kr fa tw R19 sb R18 R17 L10 L9 L12 L8 bt R16 R11 R10 R9 fd L7 L6 L5 L4 R12 R8 R7 fe fc L3 L2 L1 "
+      "kr2 fb ow cm ff off cm2 mc")
+_B = ("q m0 m1 h0 h1 L7 L6 L5 L4 m2 L3 L2 L1 h2 L8 d0 d1 d2 L19 L18 rds L17 R8 R7 L16 kr bo fa ff fe L12 tw L11 sb R19 R18 R17 L10 L9 bt R16 R12 R11 fc fd "
+      "R10 R9 kr2 fb ow cm2 cm off mc")
 ORDER = [_B.split(), _A.split()]
-PRE = ["q m0 m1 h0 h1 d0 m2 d1 h2", "m0 q m1 h0 h1 d0 m2 d1 h2"]
-XA = [0, 48]
-TILES = [("fa", [19, 18, 17], 384), ("fb", [23, 22, 21, 20], 368), ("fc", [15, 14, 13, 12], 240),
+SQ = ["s15 s14 r15 s13 r14 g s23 r13 t s22 r23 s21 r22 s20 r21 r20 A6 A5 A4 A3 A2 A1".split(),
+      "s15 s14 r15 g s13 t r14 s23 r13 s22 r23 s21 r22 s20 r21 r20 A6 A5 A4 A3 A2 A1".split()]
+TILES = [("fa", [19, 18, 17], 384), ("fb", [23, 22, 21, 20], 368), ("fc", [15, 14, 13, 12], 256),
          ("fd", [16, 11, 10, 9], 256), ("fe", [8, 7, 6, 5], 128), ("ff", [4, 3, 2, 1], 128)]
 LANE = {_c: (_n, _k) for _n, _l, _w in TILES for _k, _c in enumerate(_l)}
 
@@ -46,12 +47,12 @@ def _each(text, dtype):
 
 
 _each("xt0:1536 xt1:1536 xt2:1536 xt3:1536 ut:512 vt:512 iet:2048 bot:512 zt:512 ak:512 al:512 one:128 sg:384 rds:384 "
-      "tw:384 sgl:3584 jk:3200 fh:1536 lr:384 tu:384 ew:384 ep:192", "bfloat16")
+      "tw:384 sgl:4416 jk:3200 fh:1536 lr:384 tu:384 ew:384 ep:208 zr:384", "bfloat16")
 _s([("k16", 384), ("mb", 128), ("rs", 128), ("r0", 384), ("t16", 384), ("t4", 192), ("t16h", 384), ("t4h", 384), ("alt", 384), ("mn", 192)],
    "bfloat16", buf="kb")
 _s([("fl", 192), ("fcum", 192), ("fc2", 192), ("lqk", 96), ("val", 192), ("nl", 384)], "bfloat16", buf="fs")
 _s([("nm4", 96), ("nm16", 96), ("nlc", 384), ("ec", 384), ("bt", 384), ("twc", 384), ("flc", 192)], "float16", buf="hf")
-_s([("f32", 1536), ("rl", 384), ("gap", 136), ("ra", 768)], "bfloat16", buf="fw")
+_s([("w%d" % _b, 720) for _b in range(4)], "bfloat16", buf="fw")
 _s([(_n, 4 * _w) for _n, _l, _w in TILES], "bfloat16", buf="ft")
 _s([("q" + _n, _w) for _n, _l, _w in TILES], "codes", buf="qf")
 _each("xq:384 uq:128 urs:128 urb:128 vq:128 eq:512 bo:128 wq:512 ql:128", "codes")
@@ -60,16 +61,16 @@ for _t in "012":
     _each("sn%s:32 ln%s:32 st%s:24 lp%s:24 lo%s:24" % (_t, _t, _t, _t, _t), "uint16")
     _each("sb%s:24 lb%s:24" % (_t, _t), "float32")
 _each("lo3:24", "uint16")
-_s([(_n, 24) for _n in ("ks", "t16w", "ta", "tn", "cols", "kcb", "jc")] + [(_n, 16) for _n in ("ks4", "t4w", "bw", "ui", "jb")] + [("bi", 32)],
+_s([(_n, 24) for _n in ("ks", "t16w", "ta", "tn", "cols", "kcb", "jc", "j24")] + [(_n, 16) for _n in ("ks4", "t4w", "bw", "ui", "jb")] + [("bi", 32)],
    "float32", buf="kw")
 _s([("c4", 192), ("c16", 192), ("kq", 384), ("mc", 384)], "float32", buf="cc")
-_each("iota0:384 pw:1152 m2:384 hs:384 cm:384 ru:24 kr:24 ow:24 pay:384 sp:384 spa:384 kqs:192 pp:60 "
+_each("iota0:384 pw:1152 m2:384 hs:384 cm:384 ru:24 kr:24 ow:24 pay:384 sp:384 spa:384 kqs:192 pp:88 "
       "fq:768 fl32:384 fn32:384 lr3:384 ys:384", "float32")
 _each("li:24 pi:6 kqi:108", "int32")
-_each("pmo:24 pmo1:24 uo16:16 bo16:32 off16:24 rk16:24 n16:12 t4q:48 t4k:48 q16:18 e4:96", "uint16")
+_each("pmo:24 pmo1:24 uo16:16 bo16:32 off16:24 rk16:24 n16:12 q16:24 e4:24 o12:12", "uint16")
 _s([("p%d" % _b, 512) for _b in range(8)], "float32", "psum", "ps")
 
-SEMAPHORES = ("v a p gc ls dx0 dx1 dx2 du dw ds dv dl z0 z1 z2 z3 z4 z5 z6 z7 y0 y1 y2 y3 y4 y5 y6 y7 y8 y9 oy oz ok oc_ oc2 o0 o1 o2 o3 "
+SEMAPHORES = ("v a p gc ls dx0 dx1 dx2 du dw ds dv dl z0 z1 z2 z3 z4 z5 z6 z7 y0 y1 y2 y3 y4 y5 y6 y7 y8 y9 y10 y11 y12 y13 y14 tu0 tu1 tu2 oy oz ok oc_ oc2 o0 o1 o2 o3 "
               "rb0 rb1 rb2 rn0 rn1 rn2 rc0 rc1 rc2 rl0 rt0 rt1 rt2").split()
 
 
@@ -226,17 +227,19 @@ def rank_program(g, core, T, topo):
     for i, q in ((0, "a"), (1, "s"), (2, "a")):
         dma(q, ap(R("xt0", 512 * i, 512 * i + 512)), T.x[:, 512 * i:512 * i + 512], [], [R("xt0", 512 * i, 512 * i + 512)], "dx%d" % i)
     fill(R("zt"), 0.0)
+    fill(R("one"), 1.0)
+    dma("s", ap(R("bot")), ap(R("zt")), [R("zt")], [R("bot")], "y13")
     for i, (n, ls, w) in enumerate(TILES):
         z = R(n, 64 * ls[-1], 4 * w)
-        assert z[2] - z[1] <= 512
         dma("s", ap(z), ap(R("zt", 0, z[2] - z[1])), [R("zt")], [z], "y%d" % i)
     for b in range(4):
         dma("s", ap(R("iet", 512 * b, 512 * b + 512)), ap(R("zt")), [R("zt")], [R("iet", 512 * b, 512 * b + 512)], "z%d" % b)
-    for i, z in enumerate((R("ak", 384, 512), R("al", 384, 512), R("fw", 1920, 2432), R("fw", 2432, 2824))):
+    for i, z in enumerate([R("ak", 384, 512), R("al", 384, 512)] + [R("w%d" % b, 480, 720) for b in range(4)]):
         dma("s", ap(z), ap(R("zt", 0, z[2] - z[1])), [R("zt")], [z], "y%d" % (6 + i))
-    dma("s", ap(R("wq", bit="u8")), T.wc[:, :], [], [R("wq")], "dw")
-    dma("s", ap(R("wqs")), T.ws[:, :], [], [R("wqs")], "ds")
-    dma("s", ap(R("vt")), T.v[:, :], [], [R("vt")], "dv")
+    hold("s", [R("one")], [R("bot")])
+    for k in range(8):
+        g.sync.dma_start(T.bot[16 * k:16 * k + 16, 64 * k:64 * k + 64], T.one[16 * k:16 * k + 16, 0:64]).then_inc(T.sem.y12, 16)
+    done("s", [R("one")], [R("bot")], ("y12", 128))
 
     fine = {"allow_small_or_imprecise_dtypes": True}
     iota(R("pi", 0, 1), [[1, 1]], 1)
@@ -244,71 +247,67 @@ def rank_program(g, core, T, topo):
     iota(R("iota0"), [[1, 384]], **fine)
     iota(R("ui"), [[1, 2], [16, 8]], **fine)
     iota(R("kcb"), [[16, 24]], **fine)
-    iota(R("ks4"), [[0, 4], [1, 4]], **fine)
-    iota(R("bi"), [[1, 8], [0, 4]], **fine)
 
-    col = {n: R("cols", i, i + 1) for i, n in enumerate(
-        ("pm", "pm1", "p4", "p41", "b1", "nb1", "pg", "b16", "b4", "bb1", "h4", "h16", "pbn", "pbe", "s16", "z", "z2", "f0", "kc"))}
+    col = {n: R("cols", i, i + 1) for i, n in enumerate(("pm", "pm1", "b16", "bb1", "h16", "pbe", "s16", "z", "z2", "f0", "kc"))}
     ts(R("pi", 1, 2), R("pi", 0, 1), 15, AL.bitwise_and)
-    ts(R("pi", 2, 3), R("pi", 0, 1), 2, AL.logical_shift_right, 3, AL.bitwise_and)
-    ts(R("pi", 3, 4), R("pi", 0, 1), 3, AL.bitwise_and)
-    ts(R("pi", 4, 5), R("pi", 0, 1), 4, AL.logical_shift_right)
+    fill(R("ru"), 0.0)
+    fill(R("jk", JW * 13 - 1, JW * 16, JW), 0.0)
     cp(col["pm"], R("pi", 1, 2))
     ts(col["pm1"], R("pi", 1, 2), 1.0, AL.add)
-    ts(col["b1"], R("pi", 3, 4), 1.0, AL.add)
-    fill(R("ru"), 0.0)
+    fill(R("ru", 17, 20), 128.0)
     ts(R("pmo"), R("zt", 0, 24), col["pm"], AL.add)
     ts(R("ta"), R("ks"), col["pm"], AL.is_equal, -3 * BV, AL.mult)
     ts(R("tn"), R("ks"), col["pm1"], AL.is_equal, BV, AL.mult)
     act(R("k16"), IND(R("ks"), R("pmo")))
-    ts(col["nb1"], col["b1"], -1.0, AL.mult)
     ts(R("pmo1"), R("zt", 0, 24), col["pm1"], AL.add)
-    tt(R("t16w"), R("ta"), R("tn"), AL.add)
-    cp(col["p4"], R("pi", 2, 3))
-    ts(col["p41"], R("pi", 2, 3), 1.0, AL.add)
-    act(R("t16"), IND(R("t16w"), R("pmo")))
-    act(R("pw", 0, 384), R("iota0"), AF.Identity, scale=4.0, bias=col["b1"])
-    act(R("pw", 384, 768), R("iota0"), AF.Identity, scale=-4.0, bias=col["nb1"])
-    cp(col["pg"], R("pi", 4, 5))
     ts(col["b16"], col["pm"], 14.5, AL.is_lt, BV, AL.mult)
+    tt(R("t16w"), R("ta"), R("tn"), AL.add)
     ts(col["f0"], col["pm"], 0.5, AL.is_lt, 3 * BV, AL.mult)
-    ts(col["b4"], col["p4"], 2.5, AL.is_lt, BV, AL.mult)
-    fill(R("ru", 17, 20), 128.0)
+    act(R("t16"), IND(R("t16w"), R("pmo")))
+    act(R("pw", 0, 384), R("iota0"), AF.Identity, bias=1.0)
+    act(R("pw", 384, 768), R("iota0"), AF.Identity, scale=-1.0, bias=-1.0)
     ts(col["z"], col["b16"], -192.0, AL.mult, col["pm"], AL.add)
     ts(col["kc"], col["b16"], col["f0"], AL.add, col["pm"], AL.add)
-    ts(R("bw"), R("ks", 0, 16), col["pg"], AL.is_equal)
+    quant("vb0", R("zt"))
     cp(R("uo16"), R("ui"))
+    ts(R("mn"), R("k16", 0, 192), col["pm"], AL.is_le, 1024.0, AL.mult)
     ts(R("mb"), R("k16", 0, 128), col["pm"], AL.not_equal, -BIG, AL.mult)
     ts(R("rs"), R("k16", 0, 128), 0.5, AL.is_lt, -4 * BIG, AL.mult)
     ts(R("jc"), R("kcb"), col["z"], AL.add, 384.0, AL.add)
     ts(R("jb", 0, 12), R("kcb", 0, 12), col["pm"], AL.add, -191.0, AL.add)
-    ts(R("r0"), R("k16"), 0.5, AL.is_gt)
     cp(R("lo0"), R("li"))
+    ts(R("r0"), R("k16"), 0.5, AL.is_gt)
     send(rank + 1, "rl0", (R("lp0"), R("lo0")))
-    iota(R("one"), [[0, 128]], base=1, **fine)
     for b in range(4):
         asel(R("iet", 512 * b + b, 512 * b + 512, 4), R("one"), [[-1, 128]], AL.is_equal, 0, 1)
-    iota(R("ep", 0, 96), [[1, 96]], base=128, **fine)
-    iota(R("ep", 96, 192), [[2, 96]], base=258, **fine)
+    iota(R("alt"), [[0, 192], [1, 2]], **fine)
+    iota(R("j24"), [[16, 24]], base=-256, **fine)
+
+    def slots():
+        iota(R("ep", 0, 1), [[0, 1]], base=-512, **fine)
+        iota(R("ep", 1, 97), [[1, 96]], base=128, **fine)
+        iota(R("ep", 112, 208), [[2, 96]], base=258, **fine)
+        iota(R("zr", 0, 384, 2), [[0, 192]], base=-512, **fine)
+
     ts(R("kcb"), R("kcb"), 15.0, AL.add, col["kc"], AL.subtract)
     ts(R("jc"), R("jc"), 1.0 / 192.0, AL.mult)
-    cp(R("bo16"), R("bi"))
-    ts(R("ta", 0, 16), R("ks4"), col["p4"], AL.is_equal, -3 * BV, AL.mult)
-    ts(R("tn", 0, 16), R("ks4"), col["p41"], AL.is_equal, BV, AL.mult)
     ts(R("t16h"), R("t16"), 0.5, AL.mult)
+    dma("s", ap(R("pw", 768, 1152)), ap(R("pw", 0, 384)), [R("pw", 0, 384)], [R("pw", 768, 1152)], "y14")
     quant("uq", R("ut"))
-    tt(R("t4w"), R("ta", 0, 16), R("tn", 0, 16), AL.add)
-    for n, lo in (("urs", 0), ("urb", 8)):
+
+    def laid(n, lo):
         cp(R(n, bit="u32"), IND(R("uq", bit="u32"), R("uo16", lo, lo + 8)))
         act(R(n + "s"), IND(R("uqs"), R("uo16", lo, lo + 8)))
-    act(R("pw", 768, 1152), R("pw", 0, 384))
-    act(R("bot"), IND(R("bw"), R("bo16")))
+
+    quant("xq", R("xt0", 0, 512), 0, 128)
+    laid("urs", 0)
 
     P = [R("p%d" % b, 0, 384) for b in range(8)]
     BANK, FB, LB = ("p4", "p5", "p7"), ("p4", "p5", "p7", "p2"), ("p1", "p0", "p3", "p6")
 
     def piece(xn, i, w="urs"):
-        quant("xq", R(xn, 512 * i, 512 * i + 512), 128 * i, 128 * i + 128)
+        if i or xn != "xt0":
+            quant("xq", R(xn, 512 * i, 512 * i + 512), 128 * i, 128 * i + 128)
         mm(R(BANK[i], 0, 128), w, 0, "xq", 128, lo=128 * i)
         if i == 1 and w == "urs":
             mm(R("p2", 0, 240), w, 0, "xq", 240)
@@ -324,7 +323,9 @@ def rank_program(g, core, T, topo):
 
     for i in range(3):
         piece("xt0", i)
-    quant("vb0", R("zt"))
+    laid("urb", 8)
+    act(R("cm"), IND(R("t16w"), R("pmo1")))
+
     for k in (1, 2):
         dma("s", ap(R("vb%d" % k, 96, 128, 1, "u8")), ap(R("vb0", 96, 128, 1, "u8")), [R("vb0")], [R("vb%d" % k)], "z%d" % (2 + 2 * k))
         dma("s", ap(R("vb%ds" % k, 96, 128)), ap(R("vb0s", 96, 128)), [R("vb0s")], [R("vb%ds" % k)], "z%d" % (3 + 2 * k))
@@ -332,15 +333,6 @@ def rank_program(g, core, T, topo):
         d = 2 ** t
         xn, qk, vb = "xt%d" % (t + 1), "qk%d" % t, "vb%d" % t
         sb, lb, sn, ln, st, lp, lo = ["%s%d" % (n, t) for n in ("sb", "lb", "sn", "ln", "st", "lp", "lo")]
-        for x in PRE[t > 0].split():
-            if x == "q":
-                if t:
-                    piece("xt%d" % t, 2)
-                mm(R("p3", 0, 304), "urs", 0, "xq", 304)
-                mm(P[1], "urb", 0, "xq", 384)
-                mm(R("p0", 0, 368), "urs", 0, "xq", 368)
-            else:
-                {"m": masked, "h": held, "d": diagonal}[x[0]](int(x[1]))
 
         def twins():
             act(R("tw"), IND(R("sg"), R(lp)))
@@ -351,18 +343,20 @@ def rank_program(g, core, T, topo):
         def twins3():
             tt(R(sb), R("twc", 15, 384, 16), R("jc"), AL.add)
             send(rank - d, "rb%d" % t, (R(lb), R(sb)))
+            if t == 0:
+                slots()
 
         def sign(c):
-            act(R("sgl", 384 * SORD.index(c), 384 * SORD.index(c) + 16 * c), R("p2" if c in SORD[:NP2] else "p0", 0, 16 * c), AF.Sign, scale=-1.0,
+            act(R("sgl", 8 * c * (c - 1), 8 * c * (c + 1)), R("p2" if c < 16 else "p0", 0, 16 * c), AF.Sign, scale=-1.0,
                 bias=R("hs", 16 * c + 15, 16 * c + 16))
 
         def relu(c):
             fn, k = LANE[c]
-            act(R(fn, k, 64 * c, 4), R("sgl", 384 * SORD.index(c), 384 * SORD.index(c) + 16 * c), AF.Relu, accum=R("ru", c, c + 1))
+            act(R(fn, k, 64 * c, 4), R("sgl", 8 * c * (c - 1), 8 * c * (c + 1)), AF.Relu, accum=R("ru", c, c + 1))
 
         def layer(c):
             fn, k = LANE[c]
-            ts(R(fn, k, 64 * c, 4), R("p3", 0, 16 * c), R("hs", 16 * c + 15, 16 * c + 16), AL.is_lt)
+            ts(R(fn, k, 64 * c, 4), R("p3" if c > 8 or "F" in made else BANK[0], 0, 16 * c), R("hs", 16 * c + 15, 16 * c + 16), AL.is_lt)
 
         def rowsum(c):
             fn, k = LANE[c]
@@ -371,56 +365,79 @@ def rank_program(g, core, T, topo):
 
         def rowsum2(c):
             fn, k = LANE[c]
-            act(R("sgl", 3072 + 128 * (c % 4), 3072 + 128 * (c % 4) + 16 * c), R(fn, k, 64 * c, 4), accum=R("ru", c, c + 1))
+            act(R("sgl", 8 * c * (c - 1), 8 * c * (c + 1)), R(fn, k, 64 * c, 4), accum=R("ru", c, c + 1))
 
-        order = ["fa"] + [n for n in ORDER[t > 0] if n[0] == "f" and n != "fa"]
-        ready = set()
+        order = [n for n in ORDER[t > 0] if n[0] == "f"]
+        wide = ["fa"] + [n for n in order if WHERE["q" + n][2] > 128 and n != "fa"]
+        ready, waiting = [], list(wide)
 
         def colsum(fn):
-            quant("q" + fn, R(fn))
-            ready.add(fn)
-            while order and order[0] in ready:
-                n = order.pop(0)
-                w = WHERE["q" + n][2]
-                mm(R("p6", 0, w), "bo", 0, "q" + n, w, start=n == "fa", stop=not order)
+            w = WHERE["q" + fn][2]
+            if fn == wide[-1]:
+                quant("q" + fn, R(fn, 512, 4 * w), 128, w)
+            else:
+                quant("q" + fn, R(fn))
+            ready.append(fn)
+            while waiting and waiting[0] in ready:
+                n = waiting.pop(0)
+                mm(R("p1", 0, WHERE["q" + n][2] - 128), "bo", 0, "q" + n, WHERE["q" + n][2] - 128, n == "fa", not waiting, lo=128)
+            if fn == wide[-1]:
+                quant("q" + fn, R(fn, 0, 512), 0, 128)
+            mm(R("p6", 0, 128), "bo", 0, "q" + fn, 128, start=fn == order[0], stop=fn == order[-1])
 
-        nr, nv = NRS, min(SORD) - 1
-        todo = [(sign, SORD[0])]
-        for a, b in zip(SORD, SORD[1:]):
-            todo += [(sign, b), (relu, a)]
-        todo.append((relu, SORD[-1]))
-        for f, c in todo[:T0[t > 0]]:
-            f(c)
-        act(R("sg"), P[1], AF.Sign, bias=-1.0e-36)
-        for f, c in todo[T0[t > 0]:T1[t > 0]]:
-            f(c)
-        twins()
-        for f, c in todo[T1[t > 0]:]:
-            f(c)
-        if t == 0:
-            act(R("cm"), IND(R("t16w"), R("pmo1")))
+        made, sq = set(), list(SQ[t > 0])
+        SORD = [int(x[1:]) for x in sq if x[0] == "s"]
+        nr = max(int(x[1:]) for x in sq if x[0] in "As" and int(x[1:]) < 12)
+
+        def scalar_upto(need):
+            while sq:
+                x, c = sq[0], int(sq[0][1:]) if sq[0][1:].isdigit() else 0
+                src = {"s": ["h%d" % (c // 8)] + ([] if c < 16 else ["q"]), "r": [], "A": ["L%d" % c], "g": ["q"], "t": []}[x[0]]
+                if not all(k in made for k in src):
+                    break
+                sq.pop(0)
+                made.add(x)
+                if x == "g":
+                    act(R("sg"), P[1], AF.Sign, bias=-1.0e-36)
+                elif x == "t":
+                    twins()
+                else:
+                    {"s": sign, "r": relu, "A": rowsum2}[x[0]](c)
+            assert all(k in made for k in need), (need, sq)
+
         for x in ORDER[t > 0]:
             c = int(x[1:]) if x[0] in "LR" else 0
-            if x[0] == "L" and c not in SORD:
-                layer(c)
-                if c <= nr:
-                    rowsum2(c)
-            elif x[0] == "R" and nr < c and c not in SORD:
-                rowsum(c)
-            elif x == "kr3":
-                tt(R("kr", 16, 20), R("kr", 16, 20), R("jk", JW * 17 - 1, JW * 20, JW), AL.subtract)
+            scalar_upto({"bt": ["g"], "tw": ["t"], "cm": [k for k in SQ[t > 0] if k[0] in "rA" and int(k[1:]) >= 8],
+                         "cm2": [k for k in SQ[t > 0] if k[0] in "rA" and int(k[1:]) < 8], "fa": ["g"], "F": ["s%d" % k for k in SORD if k < 16]}.get(x, [])
+                        + ["r%d" % k for k in SORD if LANE[k][0] == x])
+            made.add(x)
+            if x[0] == "L":
+                if c not in SORD:
+                    layer(c)
+            elif x[0] == "R":
+                if nr < c and c not in SORD:
+                    rowsum(c)
             elif x[0] == "f":
                 colsum(x)
-            elif x == "d2":
-                diagonal(2)
-                for b in range(4 if t else 0):
+            elif x == "q1":
+                piece("xt%d" % t, 1)
+            elif x == "q":
+                if t:
+                    piece("xt%d" % t, 2)
+                for k in PEO:
+                    n = {"3": 304, "1": 384, "0": 368}[k]
+                    mm(R("p" + k, 0, n), "urb" if k == "1" else "urs", 0, "xq", n)
+            elif x[0] in "mhd" and x[1].isdigit():
+                {"m": masked, "h": held, "d": diagonal}[x[0]](int(x[1]))
+            elif x == "F":
+                for b in range(4):
                     mm(R(FB[b], 0, 384), "eq", 128 * b, "xq", 384)
             elif x == "rds":
                 scan(R("rds"), R("r0"), R("fa", 3, 1536, 4), AL.mult, AL.add)
             elif x == "kr":
                 tt(R("kr"), R("kcb"), R("rds", 15, 384, 16), AL.subtract)
             elif x == "kr2":
-                tt(R("kr", nr + 1, nv + 1), R("kr", nr + 1, nv + 1), R("jk", JW * (nr + 2) - 1, JW * (nv + 1), JW), AL.subtract)
+                tt(R("kr", nr + 1, 20), R("kr", nr + 1, 20), R("jk", JW * (nr + 2) - 1, JW * 20, JW), AL.subtract)
             elif x == "bt":
                 scan(R("bt"), R("t16h"), R("sg"))
             elif x == "tw":
@@ -429,59 +446,61 @@ def rank_program(g, core, T, topo):
                 twins3()
             elif x == "bo":
                 quant("bo", R("bot"))
-            elif x == "eq":
-                quant("eq", R("iet"))
-                for b in range(4):
-                    mm(R(FB[b], 0, 384), "eq", 128 * b, "xq", 384)
             elif x == "ow":
                 tt(R("ow"), R("bt", 15, 384, 16), R(lb), AL.add)
             elif x == "off":
                 ts(R("off16"), R("ow"), 192.0, AL.mult, 0.25, AL.add)
             elif x == "cm":
-                tt(R("cm", 15, 384, 16), R("kr"), R("ru"), AL.subtract)
+                tt(R("cm", 128 + 15, 384, 16), R("kr", 8, 24), R("ru", 8, 24), AL.subtract)
+            elif x == "cm2":
+                tt(R("cm", 15, 128, 16), R("kr", 0, 8), R("ru", 0, 8), AL.subtract)
+            elif x == "mc":
+                scan(R("mc", 128, 384), R("p1", 0, 256), R("cm", 128, 384), AL.max, AL.add, first=-3 * BV)
+        def unit(b):
+            if t == 0:
+                quant("eq", R("iet", 512 * b, 512 * b + 512), 128 * b, 128 * b + 128)
+                mm(R(FB[b], 0, 384), "eq", 128 * b, "xq", 384)
+
+        if t == 0:
+            for n, a, k, c in (("bb1", "b16", 0.5, 1.0), ("h16", "b16", 1.0, 1.0), ("z2", "b16", 0.5, col["pm"]),
+                               ("s16", "b16", -0.5, 192.0), ("pbe", "b16", -0.5, 256.0)):
+                act(col[n], col[a], AF.Identity, scale=k, bias=c)
+            act(R("j24"), R("j24"), AF.Identity, bias=col["z2"])
+            act(R("alt", 1, 384, 2), R("alt", 1, 384, 2), scale=2.0 ** -10)
         act(R("pay"), IND(R("pw"), R("off16")))
+        scan(R("mc", 0, 128), R("p6", 0, 128), R("cm", 0, 128), AL.max, AL.add, first=-3 * BV)
+        ts(R("rk16", 8, 24), R("mc", 128 + 15, 384, 16), col["f0"], AL.add)
+        unit(0)
+        ts(R("rk16", 0, 8), R("mc", 15, 128, 16), col["f0"], AL.add)
+        unit(1)
         if t == 0:
-            fill(R("alt", 0, 384, 2), 0.0)
-            fill(R("alt", 1, 384, 2), 2.0 ** -12)
-            ts(R("mn"), R("k16", 0, 192), col["pm"], AL.is_le, 1024.0, AL.mult)
-        scan(R("mc"), P[6], R("cm"), AL.max, AL.add, first=-3 * BV)
-        if t == 0:
-            ts(col["bb1"], col["b16"], 0.5, AL.mult, 1.0, AL.add)
-            ts(col["z2"], col["b4"], -2.0, AL.mult, col["b1"], AL.add)
-        ts(R("rk16"), R("mc", 15, 384, 16), col["f0"], AL.add)
-        if t == 0:
-            ts(col["h4"], col["b4"], 1.0, AL.add)
-            tt(col["h16"], col["b16"], col["b1"], AL.add)
+            dma("s", ap(R("wq", bit="u8")), T.wc[:, :], [R("rk16")], [R("wq")], "dw")
+            dma("s", ap(R("wqs")), T.ws[:, :], [], [R("wqs")], "ds")
+            dma("s", ap(R("vt")), T.v[:, :], [], [R("vt")], "dv")
         cp(IND(R("sp"), R("rk16")), R("pay"))
-        if t == 0:
-            ts(col["pbn"], col["z2"], 767.0, AL.add)
-            ts(col["pbe"], col["z2"], 1023.0, AL.add)
-        for b in range(4):
-            act(R("fh", b, 1536, 4), R(FB[b], 0, 384), scale=0.5)
-        if t:
-            act(R("lr"), IND(R("iota0"), R(lo)), AF.Identity, bias=-192.0)
+        unit(2)
+        for b in range(4 if t else 2):
+            act(R("fh", 384 * b, 384 * b + 384), R(FB[b], 0, 384), scale=0.5)
         act(R("spa"), R("sp"), AF.Abs)
-        if t == 0:
-            act(R("t4"), IND(R("t4w"), R("pmo", 0, 12)))
-            act(R("lr"), IND(R("iota0"), R(lo)), AF.Identity, bias=-192.0)
-            act(R("t4h"), IND(R("t4w"), R("pmo")), scale=0.5)
+        ts(R("fl"), R("sp", 1, 384, 2), 0.0, AL.is_lt)
+        unit(3)
+        act(R("lr"), IND(R("iota0"), R(lo)), AF.Identity, bias=-192.0)
+        dma("s", ap(R("tu")), ap(R("lr")), [R("lr")], [R("tu")], "tu%d" % t)
+        for b in range(4 if t else 2, 4):
+            act(R("fh", 384 * b, 384 * b + 384), R(FB[b], 0, 384), scale=0.5)
 
         def bases(b0, b1):
             for b in range(b0, b1):
-                act(R("f32", b, 1536, 4), R(FB[b], 0, 384), scale=32.0)
+                act(R("w%d" % b, 0, 384), R(FB[b], 0, 384), scale=32.0)
 
-        act(R("ew"), R("iota0"), AF.Identity, bias=-256.0)
-        act(R("tu"), R("lr"))
-        bases(0, 4 if t else B0)
+        bases(0, B0[t > 0])
 
         def pairs(a, b):
             scan(R("kq", a, b), R("alt", a, b), R("spa", a, b), AL.mult, AL.add)
 
         mk, jbf, pp1, pp2, nn = [R("pp", 12 * i, 12 * i + 12) for i in range(5)]
         F = R("fcum", 191, 192)
-        ts(R("fl"), R("sp", 1, 384, 2), 0.0, AL.is_lt)
-        if t == 0:
-            ts(col["s16"], col["b16"], -0.5, AL.mult, 192.0, AL.add)
+        if t == 1:
             quant("vq", R("vt"))
         scan(R("fcum"), R("fl"), R("fl"))
         scan(R("flc"), R("t16h", 0, 192), R("fl"))
@@ -491,58 +510,87 @@ def rank_program(g, core, T, topo):
         pairs(0, 96)
         tt(pp1, jbf, R("fc2", 15, 192, 16), AL.subtract)
         tt(pp2, R("fc2", 15, 192, 16), mk, AL.add)
+        ts(R("pp", 84, 85), F, -96.0, AL.add)
         pairs(96, 240)
         tt(nn, pp1, pp2, AL.max)
         pairs(240, 384)
         ts(R("n16"), nn, F, AL.subtract, 191.0, AL.add)
+        ts(R("o12"), nn, R("pp", 84, 85), AL.subtract, 0.0, AL.max)
+        act(R("zr", 1, 384, 2), IND(R("ep", 0, 97), R("o12")))
+        bases(B0[t > 0], B1[t > 0])
+        if EW[t > 0] == 0:
+            act(R("ew"), IND(R("zr"), R("rk16")))
         cp(IND(R("kqs"), R("n16")), R("kq", 1, 384, 2))
-        scan(R("c4"), R("t4", 0, 192), R("kqs"))
-        scan(R("c16"), R("t16", 0, 192), R("kqs"))
-        ts(R("kqi", 0, 48), R("c4", 3, 192, 4), 4096.0, AL.mult)
-        ts(R("t4q"), R("c4", 3, 192, 4), col["h4"], AL.subtract)
-        ts(R("q16", 0, 12), R("c16", 15, 192, 16), col["h16"], AL.subtract, 0.25, AL.mult)
-        ts(R("kqi", 48, 54), R("c16", 96 + 15, 192, 16), 4096.0, AL.mult)
-        ts(R("kqi", 54, 102), R("kqi", 0, 48), 4095, AL.bitwise_and)
-        (cp if LQ else act)(R("lqk"), IND(R("lr"), R("q16", 0, 6)))
-        act(R("fq", 0, 192), IND(R("fh"), R("t4q", 0, 12)))
-        act(R("fq", 192, 384), IND(R("fh"), R("t4q", 12, 24)))
-        act(R("fq", 384, 768), IND(R("fh"), R("t4q", 24, 48)))
-        ts(R("kqi", 102, 108), R("kqi", 48, 54), 4095, AL.bitwise_and)
-        ts(R("t4k"), R("kqi", 54, 102), 1.0, AL.subtract)
-        scan(R("nm4"), R("t4h", 0, 96), R("lqk"))
-        scan(R("nm16"), R("t16h", 0, 96), R("lqk"))
-        ts(R("q16", 12, 18), R("kqi", 102, 108), col["b1"], AL.subtract, 0.25, AL.mult)
-        ts(R(sn, 0, 24), R("nm4", 3, 96, 4), 4.0, AL.mult, col["pbn"], AL.add)
-        ts(R(sn, 24, 30), R("nm16", 15, 96, 16), col["s16"], AL.add)
-        send(rank + d, "rn%d" % t, (R(ln, 0, 30), R(sn, 0, 30)))
-        tt(R("ak", 0, 192), IND(R("fh"), R("t4k", 0, 12)), R("fq", 0, 192), AL.add)
-        tt(R("ak", 192, 384), IND(R("fh"), R("t4k", 12, 24)), R("fq", 192, 384), AL.add)
-        quant(qk, R("ak"))
-        send(rank + d, "rc%d" % t, (R(vb, 0, 96, 1, "u8"), R(qk, 0, 96, 1, "u8")), (R(vb + "s", 0, 96), R(qk + "s", 0, 96)))
+        for x in KEEP.split():
+            if x == "ck":
+                scan(R("c16", 0, 96), R("t16", 0, 96), R("kqs", 0, 96))
+            elif x == "cl":
+                scan(R("c16", 96, 192), R("t16", 0, 96), R("kqs", 96, 192))
+            elif x == "qk":
+                ts(R("q16", 0, 6), R("c16", 15, 96, 16), col["h16"], AL.subtract)
+                for b in range(4):
+                    act(R("fq", 96 * b, 96 * b + 96), IND(R("fh", 384 * b, 384 * b + 384), R("q16", 0, 6)))
+            elif x == "ql":
+                ts(R("q16", 6, 12), R("c16", 96 + 15, 192, 16), col["h16"], AL.subtract)
+                for b in range(4):
+                    act(R("fq", 384 + 96 * b, 480 + 96 * b), IND(R("fh", 384 * b, 384 * b + 384), R("q16", 6, 12)))
+            elif x == "ik":
+                ts(R("kqi", 6, 12), R("c16", 15, 96, 16), 1024.0, AL.mult)
+            elif x == "il":
+                ts(R("kqi", 0, 6), R("c16", 96 + 15, 192, 16), 1024.0, AL.mult)
+            elif x == "and":
+                ts(R("kqi", 12, 24), R("kqi", 0, 12), 1023, AL.bitwise_and)
+            elif x == "k16":
+                ts(R("q16", 12, 24), R("kqi", 12, 24), 1.0, AL.subtract)
+            elif x == "lq":
+                (cp if LQ else act)(R("lqk"), IND(R("lr"), R("q16", 0, 6)))
+            elif x == "n16":
+                scan(R("nm16"), R("t16h", 0, 96), R("lqk"))
+            elif x == "s16":
+                ts(R(sn, 0, 6), R("nm16", 15, 96, 16), col["s16"], AL.add)
+            elif x == "N":
+                send(rank + d, "rn%d" % t, (R(ln, 0, 6), R(sn, 0, 6)))
+            elif x[0] == "a":
+                b = int(x[1])
+                tt(R("ak", b, 384, 4), IND(R("fh", 384 * b, 384 * b + 384), R("q16", 18, 24)), R("fq", 96 * b, 96 * b + 96), AL.add)
+            elif x == "q":
+                quant(qk, R("ak"))
+            elif x == "C":
+                send(rank + d, "rc%d" % t, (R(vb, 0, 96, 1, "u8"), R(qk, 0, 96, 1, "u8")), (R(vb + "s", 0, 96), R(qk + "s", 0, 96)))
         act(R("val", 0, 96), IND(R("lr"), R("q16", 12, 18)))
         act(R("val", 96, 192), IND(R("lr"), R("q16", 6, 12)))
         act(R("fl32"), R("fq", 384, 768), scale=64.0)
-        if t == 0:
-            bases(B0, 4)
+        if EW[t > 0] == 1:
+            act(R("ew"), IND(R("zr"), R("rk16")))
+        bases(B1[t > 0], 4)
         left = LB
+        last = t + 1 == NR
+        w = "vq" if last else "urs"
         for x in WIN[t].split():
             if x == "al":
-                tt(R("al", 0, 384), IND(R("fh"), R("t4k", 24, 48)), R("fq", 384, 768), AL.add)
+                for b in range(4):
+                    tt(R("al", b, 384, 4), IND(R("fh", 384 * b, 384 * b + 384), R("q16", 12, 18)), R("fq", 384 + 96 * b, 480 + 96 * b), AL.add)
             elif x == "tu":
                 cp(IND(R("tu"), R("q16", 6, 18)), R("val"))
+            elif x == "ng":
                 act(R("nl"), IND(R("tu"), R(lp)))
-                act(R("fn32"), IND(R("fh"), R(ln, 0, 24)), scale=64.0)
+            elif x == "fn":
+                for b in range(4):
+                    act(R("fn32", 96 * b, 96 * b + 96), IND(R("w%d" % b, 0, 384), R(ln, 0, 6)))
             elif x == "ql":
                 quant("ql", R("al"))
                 for b in range(4):
                     mm(R(left[b], 0, 128), "wq", 128 * b, "ql", 128)
-            elif x == "e1":
-                cp(IND(R("ew"), R("q16", 6, 12)), R("ep", 0, 96))
             elif x == "e2":
-                cp(IND(R("ew"), R(ln, 24, 30)), R("ep", 96, 192))
+                cp(IND(R("ew"), R(ln, 0, 6)), R("ep", 112, 208))
+            elif x == "e3":
+                tt(R("pp", 60, 84), R("ec", 15, 384, 16), R("j24"), AL.max)
+            elif x == "lk":
+                act(R("lr3"), IND(R("iota0"), R("lo3")))
+                dma("a", T.lk[:, :], T.lr3[0:128:16, :], [R("lr3")], [], "ok")
             elif x[0] == "l":
                 b = int(x[1])
-                tt(R("rl", b, 384, 4), R(left[b], 0, 96), R("fl32", b, 384, 4), AL.add)
+                tt(R("w%d" % b, 384, 480), R(left[b], 0, 96), R("fl32", 96 * b, 96 * b + 96), AL.add)
             elif x == "nl":
                 scan(R("nlc"), R("t16h"), R("nl"))
             elif x == "st":
@@ -552,27 +600,23 @@ def rank_program(g, core, T, topo):
                 else:
                     send(rank - d, "rt%d" % t, (R("lo3"), R(st)))
             elif x == "ec":
-                scan(R("ec"), R("t4h"), R("ew"))
+                scan(R("ec"), R("t16h"), R("ew"))
             elif x == "e4":
-                ts(R("e4"), R("ec", 3, 384, 4), 4.0, AL.mult, col["pbe"], AL.add)
+                ts(R("e4"), R("pp", 60, 84), col["pbe"], AL.add)
             elif x[0] == "a":
                 b = int(x[1])
                 for k in range(0 if b else 4):
                     mm(R(FB[k], 0, 128), "wq", 128 * k, vb, 128)
-                tt(R("ra", b, 768, 8), R(FB[b], 0, 96), R("fn32", b, 384, 4), AL.add)
-        last = t + 1 == NR
-        w, xa = ("vq", XA[1]) if last else ("urs", XA[0])
-        act(R(xn, 512, 1024), IND(R("fw"), R("e4", 32, 64)), scale=2.0 ** -5)
-        act(R(xn, 1024 + 4 * xa, 1536), IND(R("fw"), R("e4", 64 + xa // 4, 96)), scale=2.0 ** -5)
-        ts(R(xn, 0, 512), IND(R("fw"), R("e4", 0, 32)), 2.0 ** -5, AL.mult)
-        if xa:
-            ts(R(xn, 1024, 1024 + 4 * xa), IND(R("fw"), R("e4", 64, 64 + xa // 4)), 2.0 ** -5, AL.mult)
-        piece(xn, 0, w)
-        piece(xn, 1, w)
-        if last:
-            piece(xn, 2, w)
-    act(R("lr3"), IND(R("iota0"), R("lo3")))
-    dma("a", T.lk[:, :], T.lr3[0:128:16, :], [R("lr3")], [], "ok")
+                tt(R("w%d" % b, 514, 706, 2), R(FB[b], 0, 96), R("fn32", 96 * b, 96 * b + 96), AL.add)
+            elif x[0] in "VS":
+                b, lo_, hi_ = int(x[1]), int(x[2], 16), int(x[3], 16)
+                o, i = R(xn, 128 * lo_ + b, 128 * hi_, 4), IND(R("w%d" % b), R("e4", 2 * lo_, 2 * hi_))
+                if x[0] == "V":
+                    ts(o, i, 2.0 ** -5, AL.mult)
+                else:
+                    act(o, i, scale=2.0 ** -5)
+            elif x[0] == "Q":
+                piece(xn, int(x[1]), w)
     dma("s", T.oc[:, 0:1024], ap(R("xq", 0, 256, 1, "u8")), [R("xq", 0, 256)], [], "oc_")
     dma("s", T.oc[:, 1024:1536], ap(R("xq", 256, 384, 1, "u8")), [R("xq", 256, 384)], [], "oc2")
     cp(R("ys", 0, 128), R(BANK[0], 0, 128))

from concourse.bass import DstId, RemoteDMATransfer
from concourse.mybir import dt, AluOpType, ActivationFunctionType

AL, AF = AluOpType, ActivationFunctionType
NR = 3
BIG = 2.0 ** 90
BV = 2048.0
JW = 160
LQ = 1
WIN = (["al tu ng fn ql e2 l0 l1 ec l2 nl e3 l3 st e4 a0 S004 a1 a2 a3 S048 S104 S248 V204 V304 S148 V348 Q0 V38c Q1 S18c V28c S08c"] * 2
       + ["al tu ng fn ql e2 l0 l1 ec l2 nl e3 l3 st e4 a0 S004 a1 a2 a3 S048 S104 S248 V204 V304 S148 V348 Q0 V38c Q1 S18c V28c S08c lk Q2"])
B0, B1, EW = [0, 1], [1, 2], [0, 0]
PEO = "310"
KEEP = "ck cl qk ik il lq and ql n16 k16 s16 N a0 a1 a2 a3 q C"
_A = ("m0 q m1 h0 h1 d0 m2 d1 h2 L11 d2 F L19 rds L18 L17 L16 kr fa tw R19 sb R18 R17 L10 L9 L12 L8 bt R16 R11 R10 R9 fd L7 L6 L5 L4 R12 R8 R7 fe fc L3 L2 L1 "
      "kr2 fb ow cm ff off cm2 mc")
_B = ("q m0 m1 h0 h1 L7 L6 L5 L4 m2 L3 L2 L1 h2 L8 d0 d1 d2 L19 L18 rds L17 R8 R7 L16 kr bo fa ff fe L12 tw L11 sb R19 R18 R17 L10 L9 bt R16 R12 R11 fc fd "
      "R10 R9 kr2 fb ow cm2 cm off mc")
ORDER = [_B.split(), _A.split()]
SQ = ["s15 s14 r15 s13 r14 g s23 r13 t s22 r23 s21 r22 s20 r21 r20 A6 A5 A4 A3 A2 A1".split(),
      "s15 s14 r15 g s13 t r14 s23 r13 s22 r23 s21 r22 s20 r21 r20 A6 A5 A4 A3 A2 A1".split()]
TILES = [("fa", [19, 18, 17], 384), ("fb", [23, 22, 21, 20], 368), ("fc", [15, 14, 13, 12], 256),
         ("fd", [16, 11, 10, 9], 256), ("fe", [8, 7, 6, 5], 128), ("ff", [4, 3, 2, 1], 128)]
LANE = {_c: (_n, _k) for _n, _l, _w in TILES for _k, _c in enumerate(_l)}

SCRATCH, WHERE = {}, {}


def _s(names, dtype, where="sbuf", buf=None):
    buf, n = buf or names[0][0], 0
    for name, w in names:
        WHERE[name] = (buf, n, w)
        if dtype == "codes":
            WHERE[name + "s"] = (buf + "s", n, w)
        n += w
    WHERE.setdefault(buf, (buf, 0, n))
    SCRATCH[buf] = (where, [128, n], "float8_e4m3fn_x4" if dtype == "codes" else dtype)
    if dtype == "codes":
        WHERE.setdefault(buf + "s", (buf + "s", 0, n))
        SCRATCH[buf + "s"] = (where, [128, n], "uint8")


def _each(text, dtype):
    for w in text.split():
        n, c = w.split(":")
        _s([(n, int(c))], dtype)


_each("xt0:1536 xt1:1536 xt2:1536 xt3:1536 ut:512 vt:512 iet:2048 bot:512 zt:512 ak:512 al:512 one:128 sg:384 rds:384 "
      "tw:384 sgl:4416 jk:3200 fh:1536 lr:384 tu:384 ew:384 ep:208 zr:384", "bfloat16")
_s([("k16", 384), ("mb", 128), ("rs", 128), ("r0", 384), ("t16", 384), ("t4", 192), ("t16h", 384), ("t4h", 384), ("alt", 384), ("mn", 192)],
   "bfloat16", buf="kb")
_s([("fl", 192), ("fcum", 192), ("fc2", 192), ("lqk", 96), ("val", 192), ("nl", 384)], "bfloat16", buf="fs")
_s([("nm4", 96), ("nm16", 96), ("nlc", 384), ("ec", 384), ("bt", 384), ("twc", 384), ("flc", 192)], "float16", buf="hf")
_s([("w%d" % _b, 720) for _b in range(4)], "bfloat16", buf="fw")
_s([(_n, 4 * _w) for _n, _l, _w in TILES], "bfloat16", buf="ft")
_s([("q" + _n, _w) for _n, _l, _w in TILES], "codes", buf="qf")
_each("xq:384 uq:128 urs:128 urb:128 vq:128 eq:512 bo:128 wq:512 ql:128", "codes")
for _t in "012":
    _each("qk%s:128 vb%s:128" % (_t, _t), "codes")
    _each("sn%s:32 ln%s:32 st%s:24 lp%s:24 lo%s:24" % (_t, _t, _t, _t, _t), "uint16")
    _each("sb%s:24 lb%s:24" % (_t, _t), "float32")
_each("lo3:24", "uint16")
_s([(_n, 24) for _n in ("ks", "t16w", "ta", "tn", "cols", "kcb", "jc", "j24")] + [(_n, 16) for _n in ("ks4", "t4w", "bw", "ui", "jb")] + [("bi", 32)],
   "float32", buf="kw")
_s([("c4", 192), ("c16", 192), ("kq", 384), ("mc", 384)], "float32", buf="cc")
_each("iota0:384 pw:1152 m2:384 hs:384 cm:384 ru:24 kr:24 ow:24 pay:384 sp:384 spa:384 kqs:192 pp:88 "
      "fq:768 fl32:384 fn32:384 lr3:384 ys:384", "float32")
_each("li:24 pi:6 kqi:108", "int32")
_each("pmo:24 pmo1:24 uo16:16 bo16:32 off16:24 rk16:24 n16:12 q16:24 e4:24 o12:12", "uint16")
_s([("p%d" % _b, 512) for _b in range(8)], "float32", "psum", "ps")

SEMAPHORES = ("v a p gc ls dx0 dx1 dx2 du dw ds dv dl z0 z1 z2 z3 z4 z5 z6 z7 y0 y1 y2 y3 y4 y5 y6 y7 y8 y9 y10 y11 y12 y13 y14 tu0 tu1 tu2 oy oz ok oc_ oc2 o0 o1 o2 o3 "
              "rb0 rb1 rb2 rn0 rn1 rn2 rc0 rc1 rc2 rl0 rt0 rt1 rt2").split()


def R(name, lo=0, hi=None, step=1, bit=None):
    buf, at, w = WHERE[name]
    return (buf, at + lo, at + (w if hi is None else hi), step, bit)


def IND(win, off):
    return ("ind", win, off)


def flat(rs):
    out = [x for r in rs for x in (r[1:] if r[0] == "ind" else (r,))]
    return [(x[0], x[1] // 512 * 512, x[1] // 512 * 512 + 512, 1, None) if x[0] == "ps" else x for x in out]


def meets(x, y):
    if x[1] <= y[0] or y[1] <= x[0]:
        return False
    return not (x[2] == y[2] and x[2] > 1 and (x[0] - y[0]) % x[2])


def rank_program(g, core, T, topo):
    rank = T.rank_of(core)
    if rank is None:
        return
    ENG = {"v": g.vector, "a": g.scalar, "p": g.tensor, "g": g, "s": g.sync}
    CNT = {"v": 0, "a": 0, "p": 0, "gc": 0, "ls": 0}
    know = {q: {} for q in ENG}
    clocks, writes, reads, seq = {}, {}, {}, [0]

    def ap(r):
        if r[0] == "ind":
            return ap(r[1]).indirect(ap(r[2]))
        n, lo, hi, st, bit = r
        w = T[n][:, lo:hi] if st == 1 else T[n][:, lo:hi:st]
        return w if bit is None else w.bitcast(dt.uint8 if bit == "u8" else dt.uint32)

    def hold(q, rd, wr, loose=False):
        need = {}
        for r in flat(rd):
            for x, ev, own in writes.get(r[0], []):
                if meets(x, r[1:4]):
                    need[ev] = 1
            for x, ev, own in reads.get(r[0], []) if r[0] == "ps" else []:
                if own != q and meets(x, r[1:4]):
                    need[ev] = 1
        for r in flat(wr):
            for x, ev, own in writes.get(r[0], []) + reads.get(r[0], []):
                if meets(x, r[1:4]) and not (loose and own == q):
                    need[ev] = 1
        for ev in sorted(need, key=lambda e: -clocks[e]["#"]):
            if know[q].get(ev[0], 0) < ev[1]:
                ENG[q].wait_ge(T.sem[ev[0]], ev[1])
                for k, n in clocks[ev].items():
                    if know[q].get(k, 0) < n:
                        know[q][k] = n

    def done(q, rd, wr, ev):
        c = dict(know[q])
        seq[0] += 1
        c.update({ev[0]: max(c.get(ev[0], 0), ev[1]), "#": seq[0]})
        clocks[ev] = c
        for r in flat(rd):
            reads.setdefault(r[0], []).append((r[1:4], ev, q))
        for r in flat(wr):
            x = r[1:4]
            if x[2] == 1:
                for d in (writes, reads):
                    d[r[0]] = [e for e in d.get(r[0], []) if not (x[0] <= e[0][0] and e[0][1] <= x[1])]
            writes.setdefault(r[0], []).append((x, ev, q))

    def op(q, rd, wr, call, loose=False):
        hold(q, rd, wr, loose)
        sem = "gc" if q == "g" else q
        CNT[sem] += 1
        call().then_inc(T.sem[sem], 1)
        done(q, rd, wr, (sem, CNT[sem]))

    def tt(o, a, b, f):
        op("v", [a, b], [o], lambda: g.vector.tensor_tensor(ap(o), ap(a), ap(b), f))

    def ts(o, a, s1, f1, s2=None, f2=None):
        rd = [a] + [s for s in (s1, s2) if isinstance(s, tuple)]
        x1, x2 = [ap(s) if isinstance(s, tuple) else s for s in (s1, s2)]
        op("v", rd, [o], lambda: g.vector.tensor_scalar(ap(o), ap(a), x1, x2, f1, *([f2] if f2 is not None else [])))

    def cp(o, a):
        rd, wr = ([a, o[2]], [o[1]]) if o[0] == "ind" else ([a], [o])
        op("v", rd, wr, lambda: g.vector.tensor_copy(ap(o), ap(a)))

    def scan(o, d0, d1, f0=AL.add, f1=AL.max, first=0.0):
        op("v", [d0, d1], [o], lambda: g.vector.tensor_tensor_scan(ap(o), ap(d0), ap(d1), first, f0, f1))

    def fill(o, x):
        op("v", [], [o], lambda: g.vector.memset(ap(o), x))

    def quant(qn, i, lo=0, hi=None):
        a, b = R(qn, lo, hi), R(qn + "s", lo, hi)
        op("v", [i], [a, b], lambda: g.vector.quantize_mx(ap(a), ap(b), ap(i)))

    def act(o, i, f=AF.Copy, scale=None, accum=None, bias=None):
        kw = {} if scale is None else {"scale": scale}
        if bias is not None:
            kw["bias"] = ap(bias) if isinstance(bias, tuple) else bias
        if accum is not None:
            kw["accum_out"] = ap(accum)
        op("a", [i] + ([bias] if isinstance(bias, tuple) else []), [o] + ([accum] if accum else []), lambda: g.scalar.activation(ap(o), ap(i), f, **kw))

    def mm(o, wn, wlo, xn, n, start=True, stop=True, lo=0):
        w, ws = R(wn, wlo, wlo + 128), R(wn + "s", wlo, wlo + 128)
        x, xs = R(xn, lo, lo + n), R(xn + "s", lo, lo + n)
        op("p", [w, ws, x, xs], [o], lambda: g.tensor.matmul_mx(ap(o), ap(w), ap(ws), ap(x), ap(xs), start, stop), loose=not start)

    def iota(o, pat, cm=0, base=0, **kw):
        op("g", [], [o], lambda: g.iota(ap(o), pat, base, cm, **kw))

    def asel(o, i, pat, f, base, cm):
        op("g", [i], [o], lambda: g.affine_select(ap(o), ap(i), pat, f, 0.0, base, cm))

    def dma(q, o, i, rd, wr, sem):
        hold(q, rd, wr)
        ENG[q].dma_start(o, i).then_inc(T.sem[sem], 16)
        done(q, rd, wr, (sem, 16))

    def landed(rsem, n, places):
        seq[0] += 1
        clocks[rsem, n] = {rsem: n, "#": seq[0]}
        for r in places:
            writes.setdefault(r[0], []).append((r[1:4], (rsem, n), "far"))

    def send(to, rsem, *pairs):
        c = T.cores[to % 8]
        adr, ne = topo.addr(c), len(topo.engines(core, c))
        for dst, src in pairs:
            hold("g", [src], [])
            CNT["ls"] += ne
            g.remote_dma(ap(dst), ap(src), T.sem[rsem], T.sem["ls"], adr[1], adr[0], topo.mask(core, c))
        landed(rsem, ne * len(pairs), [r for r, src in pairs])

    def send2(src, rsem, *ends):
        cs = [T.cores[to % 8] for to, dst in ends]
        mask = topo.mask(core, cs[0]) & topo.mask(core, cs[-1])
        ne = len([e for e in topo.engines(core, cs[0]) if mask >> e & 1])
        hold("g", [src], [])
        CNT["ls"] += ne
        g.remote_dma_fused([RemoteDMATransfer(dst_ids=[DstId(rid=topo.addr(c)[0], pnc=topo.addr(c)[1]) for c in cs], dma_engine_mask=mask,
                                              remote_sem=T.sem[rsem], srcs=[ap(src)], dsts=[ap(dst) for to, dst in ends])], local_sem=T.sem["ls"])
        landed(rsem, ne * len(ends), [dst for to, dst in ends])

    dma("a", ap(R("li")), T.link[:, :], [], [R("li")], "dl")
    dma("s", ap(R("ut")), T.u[:, :], [], [R("ut")], "du")
    for i, q in ((0, "a"), (1, "s"), (2, "a")):
        dma(q, ap(R("xt0", 512 * i, 512 * i + 512)), T.x[:, 512 * i:512 * i + 512], [], [R("xt0", 512 * i, 512 * i + 512)], "dx%d" % i)
    fill(R("zt"), 0.0)
    fill(R("one"), 1.0)
    dma("s", ap(R("bot")), ap(R("zt")), [R("zt")], [R("bot")], "y13")
    for i, (n, ls, w) in enumerate(TILES):
        z = R(n, 64 * ls[-1], 4 * w)
        dma("s", ap(z), ap(R("zt", 0, z[2] - z[1])), [R("zt")], [z], "y%d" % i)
    for b in range(4):
        dma("s", ap(R("iet", 512 * b, 512 * b + 512)), ap(R("zt")), [R("zt")], [R("iet", 512 * b, 512 * b + 512)], "z%d" % b)
    for i, z in enumerate([R("ak", 384, 512), R("al", 384, 512)] + [R("w%d" % b, 480, 720) for b in range(4)]):
        dma("s", ap(z), ap(R("zt", 0, z[2] - z[1])), [R("zt")], [z], "y%d" % (6 + i))
    hold("s", [R("one")], [R("bot")])
    for k in range(8):
        g.sync.dma_start(T.bot[16 * k:16 * k + 16, 64 * k:64 * k + 64], T.one[16 * k:16 * k + 16, 0:64]).then_inc(T.sem.y12, 16)
    done("s", [R("one")], [R("bot")], ("y12", 128))

    fine = {"allow_small_or_imprecise_dtypes": True}
    iota(R("pi", 0, 1), [[1, 1]], 1)
    iota(R("ks"), [[1, 24]], **fine)
    iota(R("iota0"), [[1, 384]], **fine)
    iota(R("ui"), [[1, 2], [16, 8]], **fine)
    iota(R("kcb"), [[16, 24]], **fine)

    col = {n: R("cols", i, i + 1) for i, n in enumerate(("pm", "pm1", "b16", "bb1", "h16", "pbe", "s16", "z", "z2", "f0", "kc"))}
    ts(R("pi", 1, 2), R("pi", 0, 1), 15, AL.bitwise_and)
    fill(R("ru"), 0.0)
    fill(R("jk", JW * 13 - 1, JW * 16, JW), 0.0)
    cp(col["pm"], R("pi", 1, 2))
    ts(col["pm1"], R("pi", 1, 2), 1.0, AL.add)
    fill(R("ru", 17, 20), 128.0)
    ts(R("pmo"), R("zt", 0, 24), col["pm"], AL.add)
    ts(R("ta"), R("ks"), col["pm"], AL.is_equal, -3 * BV, AL.mult)
    ts(R("tn"), R("ks"), col["pm1"], AL.is_equal, BV, AL.mult)
    act(R("k16"), IND(R("ks"), R("pmo")))
    ts(R("pmo1"), R("zt", 0, 24), col["pm1"], AL.add)
    ts(col["b16"], col["pm"], 14.5, AL.is_lt, BV, AL.mult)
    tt(R("t16w"), R("ta"), R("tn"), AL.add)
    ts(col["f0"], col["pm"], 0.5, AL.is_lt, 3 * BV, AL.mult)
    act(R("t16"), IND(R("t16w"), R("pmo")))
    act(R("pw", 0, 384), R("iota0"), AF.Identity, bias=1.0)
    act(R("pw", 384, 768), R("iota0"), AF.Identity, scale=-1.0, bias=-1.0)
    ts(col["z"], col["b16"], -192.0, AL.mult, col["pm"], AL.add)
    ts(col["kc"], col["b16"], col["f0"], AL.add, col["pm"], AL.add)
    quant("vb0", R("zt"))
    cp(R("uo16"), R("ui"))
    ts(R("mn"), R("k16", 0, 192), col["pm"], AL.is_le, 1024.0, AL.mult)
    ts(R("mb"), R("k16", 0, 128), col["pm"], AL.not_equal, -BIG, AL.mult)
    ts(R("rs"), R("k16", 0, 128), 0.5, AL.is_lt, -4 * BIG, AL.mult)
    ts(R("jc"), R("kcb"), col["z"], AL.add, 384.0, AL.add)
    ts(R("jb", 0, 12), R("kcb", 0, 12), col["pm"], AL.add, -191.0, AL.add)
    cp(R("lo0"), R("li"))
    ts(R("r0"), R("k16"), 0.5, AL.is_gt)
    send(rank + 1, "rl0", (R("lp0"), R("lo0")))
    for b in range(4):
        asel(R("iet", 512 * b + b, 512 * b + 512, 4), R("one"), [[-1, 128]], AL.is_equal, 0, 1)
    iota(R("alt"), [[0, 192], [1, 2]], **fine)
    iota(R("j24"), [[16, 24]], base=-256, **fine)

    def slots():
        iota(R("ep", 0, 1), [[0, 1]], base=-512, **fine)
        iota(R("ep", 1, 97), [[1, 96]], base=128, **fine)
        iota(R("ep", 112, 208), [[2, 96]], base=258, **fine)
        iota(R("zr", 0, 384, 2), [[0, 192]], base=-512, **fine)

    ts(R("kcb"), R("kcb"), 15.0, AL.add, col["kc"], AL.subtract)
    ts(R("jc"), R("jc"), 1.0 / 192.0, AL.mult)
    ts(R("t16h"), R("t16"), 0.5, AL.mult)
    dma("s", ap(R("pw", 768, 1152)), ap(R("pw", 0, 384)), [R("pw", 0, 384)], [R("pw", 768, 1152)], "y14")
    quant("uq", R("ut"))

    def laid(n, lo):
        cp(R(n, bit="u32"), IND(R("uq", bit="u32"), R("uo16", lo, lo + 8)))
        act(R(n + "s"), IND(R("uqs"), R("uo16", lo, lo + 8)))

    quant("xq", R("xt0", 0, 512), 0, 128)
    laid("urs", 0)

    P = [R("p%d" % b, 0, 384) for b in range(8)]
    BANK, FB, LB = ("p4", "p5", "p7"), ("p4", "p5", "p7", "p2"), ("p1", "p0", "p3", "p6")

    def piece(xn, i, w="urs"):
        if i or xn != "xt0":
            quant("xq", R(xn, 512 * i, 512 * i + 512), 128 * i, 128 * i + 128)
        mm(R(BANK[i], 0, 128), w, 0, "xq", 128, lo=128 * i)
        if i == 1 and w == "urs":
            mm(R("p2", 0, 240), w, 0, "xq", 240)

    def masked(i):
        tt(R("m2", 128 * i, 128 * i + 128), R(BANK[i], 0, 128), R("mb", 0, 128), AL.add)

    def held(i):
        scan(R("hs", 128 * i, 128 * i + 128), R("rs", 0, 128), R("m2", 128 * i, 128 * i + 128))

    def diagonal(i):
        tt(R("fa", 512 * i + 3, 512 * i + 512, 4), R(BANK[i], 0, 128), R("hs", 128 * i, 128 * i + 128), AL.is_le)

    for i in range(3):
        piece("xt0", i)
    laid("urb", 8)
    act(R("cm"), IND(R("t16w"), R("pmo1")))

    for k in (1, 2):
        dma("s", ap(R("vb%d" % k, 96, 128, 1, "u8")), ap(R("vb0", 96, 128, 1, "u8")), [R("vb0")], [R("vb%d" % k)], "z%d" % (2 + 2 * k))
        dma("s", ap(R("vb%ds" % k, 96, 128)), ap(R("vb0s", 96, 128)), [R("vb0s")], [R("vb%ds" % k)], "z%d" % (3 + 2 * k))
    for t in range(NR):
        d = 2 ** t
        xn, qk, vb = "xt%d" % (t + 1), "qk%d" % t, "vb%d" % t
        sb, lb, sn, ln, st, lp, lo = ["%s%d" % (n, t) for n in ("sb", "lb", "sn", "ln", "st", "lp", "lo")]

        def twins():
            act(R("tw"), IND(R("sg"), R(lp)))

        def twins2():
            scan(R("twc"), R("t16h"), R("tw"))

        def twins3():
            tt(R(sb), R("twc", 15, 384, 16), R("jc"), AL.add)
            send(rank - d, "rb%d" % t, (R(lb), R(sb)))
            if t == 0:
                slots()

        def sign(c):
            act(R("sgl", 8 * c * (c - 1), 8 * c * (c + 1)), R("p2" if c < 16 else "p0", 0, 16 * c), AF.Sign, scale=-1.0,
                bias=R("hs", 16 * c + 15, 16 * c + 16))

        def relu(c):
            fn, k = LANE[c]
            act(R(fn, k, 64 * c, 4), R("sgl", 8 * c * (c - 1), 8 * c * (c + 1)), AF.Relu, accum=R("ru", c, c + 1))

        def layer(c):
            fn, k = LANE[c]
            ts(R(fn, k, 64 * c, 4), R("p3" if c > 8 or "F" in made else BANK[0], 0, 16 * c), R("hs", 16 * c + 15, 16 * c + 16), AL.is_lt)

        def rowsum(c):
            fn, k = LANE[c]
            scan(R("jk", JW * c + JW - 8 * c, JW * c + JW), R(fn, k, 32 * c, 4), R(fn, 32 * c + k, 64 * c, 4), AL.add, AL.add,
                 first=-128.0 if c > 16 else 0.0)

        def rowsum2(c):
            fn, k = LANE[c]
            act(R("sgl", 8 * c * (c - 1), 8 * c * (c + 1)), R(fn, k, 64 * c, 4), accum=R("ru", c, c + 1))

        order = [n for n in ORDER[t > 0] if n[0] == "f"]
        wide = ["fa"] + [n for n in order if WHERE["q" + n][2] > 128 and n != "fa"]
        ready, waiting = [], list(wide)

        def colsum(fn):
            w = WHERE["q" + fn][2]
            if fn == wide[-1]:
                quant("q" + fn, R(fn, 512, 4 * w), 128, w)
            else:
                quant("q" + fn, R(fn))
            ready.append(fn)
            while waiting and waiting[0] in ready:
                n = waiting.pop(0)
                mm(R("p1", 0, WHERE["q" + n][2] - 128), "bo", 0, "q" + n, WHERE["q" + n][2] - 128, n == "fa", not waiting, lo=128)
            if fn == wide[-1]:
                quant("q" + fn, R(fn, 0, 512), 0, 128)
            mm(R("p6", 0, 128), "bo", 0, "q" + fn, 128, start=fn == order[0], stop=fn == order[-1])

        made, sq = set(), list(SQ[t > 0])
        SORD = [int(x[1:]) for x in sq if x[0] == "s"]
        nr = max(int(x[1:]) for x in sq if x[0] in "As" and int(x[1:]) < 12)

        def scalar_upto(need):
            while sq:
                x, c = sq[0], int(sq[0][1:]) if sq[0][1:].isdigit() else 0
                src = {"s": ["h%d" % (c // 8)] + ([] if c < 16 else ["q"]), "r": [], "A": ["L%d" % c], "g": ["q"], "t": []}[x[0]]
                if not all(k in made for k in src):
                    break
                sq.pop(0)
                made.add(x)
                if x == "g":
                    act(R("sg"), P[1], AF.Sign, bias=-1.0e-36)
                elif x == "t":
                    twins()
                else:
                    {"s": sign, "r": relu, "A": rowsum2}[x[0]](c)
            assert all(k in made for k in need), (need, sq)

        for x in ORDER[t > 0]:
            c = int(x[1:]) if x[0] in "LR" else 0
            scalar_upto({"bt": ["g"], "tw": ["t"], "cm": [k for k in SQ[t > 0] if k[0] in "rA" and int(k[1:]) >= 8],
                         "cm2": [k for k in SQ[t > 0] if k[0] in "rA" and int(k[1:]) < 8], "fa": ["g"], "F": ["s%d" % k for k in SORD if k < 16]}.get(x, [])
                        + ["r%d" % k for k in SORD if LANE[k][0] == x])
            made.add(x)
            if x[0] == "L":
                if c not in SORD:
                    layer(c)
            elif x[0] == "R":
                if nr < c and c not in SORD:
                    rowsum(c)
            elif x[0] == "f":
                colsum(x)
            elif x == "q1":
                piece("xt%d" % t, 1)
            elif x == "q":
                if t:
                    piece("xt%d" % t, 2)
                for k in PEO:
                    n = {"3": 304, "1": 384, "0": 368}[k]
                    mm(R("p" + k, 0, n), "urb" if k == "1" else "urs", 0, "xq", n)
            elif x[0] in "mhd" and x[1].isdigit():
                {"m": masked, "h": held, "d": diagonal}[x[0]](int(x[1]))
            elif x == "F":
                for b in range(4):
                    mm(R(FB[b], 0, 384), "eq", 128 * b, "xq", 384)
            elif x == "rds":
                scan(R("rds"), R("r0"), R("fa", 3, 1536, 4), AL.mult, AL.add)
            elif x == "kr":
                tt(R("kr"), R("kcb"), R("rds", 15, 384, 16), AL.subtract)
            elif x == "kr2":
                tt(R("kr", nr + 1, 20), R("kr", nr + 1, 20), R("jk", JW * (nr + 2) - 1, JW * 20, JW), AL.subtract)
            elif x == "bt":
                scan(R("bt"), R("t16h"), R("sg"))
            elif x == "tw":
                twins2()
            elif x == "sb":
                twins3()
            elif x == "bo":
                quant("bo", R("bot"))
            elif x == "ow":
                tt(R("ow"), R("bt", 15, 384, 16), R(lb), AL.add)
            elif x == "off":
                ts(R("off16"), R("ow"), 192.0, AL.mult, 0.25, AL.add)
            elif x == "cm":
                tt(R("cm", 128 + 15, 384, 16), R("kr", 8, 24), R("ru", 8, 24), AL.subtract)
            elif x == "cm2":
                tt(R("cm", 15, 128, 16), R("kr", 0, 8), R("ru", 0, 8), AL.subtract)
            elif x == "mc":
                scan(R("mc", 128, 384), R("p1", 0, 256), R("cm", 128, 384), AL.max, AL.add, first=-3 * BV)
        def unit(b):
            if t == 0:
                quant("eq", R("iet", 512 * b, 512 * b + 512), 128 * b, 128 * b + 128)
                mm(R(FB[b], 0, 384), "eq", 128 * b, "xq", 384)

        if t == 0:
            for n, a, k, c in (("bb1", "b16", 0.5, 1.0), ("h16", "b16", 1.0, 1.0), ("z2", "b16", 0.5, col["pm"]),
                               ("s16", "b16", -0.5, 192.0), ("pbe", "b16", -0.5, 256.0)):
                act(col[n], col[a], AF.Identity, scale=k, bias=c)
            act(R("j24"), R("j24"), AF.Identity, bias=col["z2"])
            act(R("alt", 1, 384, 2), R("alt", 1, 384, 2), scale=2.0 ** -10)
        act(R("pay"), IND(R("pw"), R("off16")))
        scan(R("mc", 0, 128), R("p6", 0, 128), R("cm", 0, 128), AL.max, AL.add, first=-3 * BV)
        ts(R("rk16", 8, 24), R("mc", 128 + 15, 384, 16), col["f0"], AL.add)
        unit(0)
        ts(R("rk16", 0, 8), R("mc", 15, 128, 16), col["f0"], AL.add)
        unit(1)
        if t == 0:
            dma("s", ap(R("wq", bit="u8")), T.wc[:, :], [R("rk16")], [R("wq")], "dw")
            dma("s", ap(R("wqs")), T.ws[:, :], [], [R("wqs")], "ds")
            dma("s", ap(R("vt")), T.v[:, :], [], [R("vt")], "dv")
        cp(IND(R("sp"), R("rk16")), R("pay"))
        unit(2)
        for b in range(4 if t else 2):
            act(R("fh", 384 * b, 384 * b + 384), R(FB[b], 0, 384), scale=0.5)
        act(R("spa"), R("sp"), AF.Abs)
        ts(R("fl"), R("sp", 1, 384, 2), 0.0, AL.is_lt)
        unit(3)
        act(R("lr"), IND(R("iota0"), R(lo)), AF.Identity, bias=-192.0)
        dma("s", ap(R("tu")), ap(R("lr")), [R("lr")], [R("tu")], "tu%d" % t)
        for b in range(4 if t else 2, 4):
            act(R("fh", 384 * b, 384 * b + 384), R(FB[b], 0, 384), scale=0.5)

        def bases(b0, b1):
            for b in range(b0, b1):
                act(R("w%d" % b, 0, 384), R(FB[b], 0, 384), scale=32.0)

        bases(0, B0[t > 0])

        def pairs(a, b):
            scan(R("kq", a, b), R("alt", a, b), R("spa", a, b), AL.mult, AL.add)

        mk, jbf, pp1, pp2, nn = [R("pp", 12 * i, 12 * i + 12) for i in range(5)]
        F = R("fcum", 191, 192)
        if t == 1:
            quant("vq", R("vt"))
        scan(R("fcum"), R("fl"), R("fl"))
        scan(R("flc"), R("t16h", 0, 192), R("fl"))
        scan(R("fc2"), R("mn"), R("fcum"), AL.add, AL.min)
        ts(jbf, R("jb", 0, 12), F, AL.add)
        ts(mk, R("flc", 15, 192, 16), col["bb1"], AL.subtract, 1024.0, AL.mult)
        pairs(0, 96)
        tt(pp1, jbf, R("fc2", 15, 192, 16), AL.subtract)
        tt(pp2, R("fc2", 15, 192, 16), mk, AL.add)
        ts(R("pp", 84, 85), F, -96.0, AL.add)
        pairs(96, 240)
        tt(nn, pp1, pp2, AL.max)
        pairs(240, 384)
        ts(R("n16"), nn, F, AL.subtract, 191.0, AL.add)
        ts(R("o12"), nn, R("pp", 84, 85), AL.subtract, 0.0, AL.max)
        act(R("zr", 1, 384, 2), IND(R("ep", 0, 97), R("o12")))
        bases(B0[t > 0], B1[t > 0])
        if EW[t > 0] == 0:
            act(R("ew"), IND(R("zr"), R("rk16")))
        cp(IND(R("kqs"), R("n16")), R("kq", 1, 384, 2))
        for x in KEEP.split():
            if x == "ck":
                scan(R("c16", 0, 96), R("t16", 0, 96), R("kqs", 0, 96))
            elif x == "cl":
                scan(R("c16", 96, 192), R("t16", 0, 96), R("kqs", 96, 192))
            elif x == "qk":
                ts(R("q16", 0, 6), R("c16", 15, 96, 16), col["h16"], AL.subtract)
                for b in range(4):
                    act(R("fq", 96 * b, 96 * b + 96), IND(R("fh", 384 * b, 384 * b + 384), R("q16", 0, 6)))
            elif x == "ql":
                ts(R("q16", 6, 12), R("c16", 96 + 15, 192, 16), col["h16"], AL.subtract)
                for b in range(4):
                    act(R("fq", 384 + 96 * b, 480 + 96 * b), IND(R("fh", 384 * b, 384 * b + 384), R("q16", 6, 12)))
            elif x == "ik":
                ts(R("kqi", 6, 12), R("c16", 15, 96, 16), 1024.0, AL.mult)
            elif x == "il":
                ts(R("kqi", 0, 6), R("c16", 96 + 15, 192, 16), 1024.0, AL.mult)
            elif x == "and":
                ts(R("kqi", 12, 24), R("kqi", 0, 12), 1023, AL.bitwise_and)
            elif x == "k16":
                ts(R("q16", 12, 24), R("kqi", 12, 24), 1.0, AL.subtract)
            elif x == "lq":
                (cp if LQ else act)(R("lqk"), IND(R("lr"), R("q16", 0, 6)))
            elif x == "n16":
                scan(R("nm16"), R("t16h", 0, 96), R("lqk"))
            elif x == "s16":
                ts(R(sn, 0, 6), R("nm16", 15, 96, 16), col["s16"], AL.add)
            elif x == "N":
                send(rank + d, "rn%d" % t, (R(ln, 0, 6), R(sn, 0, 6)))
            elif x[0] == "a":
                b = int(x[1])
                tt(R("ak", b, 384, 4), IND(R("fh", 384 * b, 384 * b + 384), R("q16", 18, 24)), R("fq", 96 * b, 96 * b + 96), AL.add)
            elif x == "q":
                quant(qk, R("ak"))
            elif x == "C":
                send(rank + d, "rc%d" % t, (R(vb, 0, 96, 1, "u8"), R(qk, 0, 96, 1, "u8")), (R(vb + "s", 0, 96), R(qk + "s", 0, 96)))
        act(R("val", 0, 96), IND(R("lr"), R("q16", 12, 18)))
        act(R("val", 96, 192), IND(R("lr"), R("q16", 6, 12)))
        act(R("fl32"), R("fq", 384, 768), scale=64.0)
        if EW[t > 0] == 1:
            act(R("ew"), IND(R("zr"), R("rk16")))
        bases(B1[t > 0], 4)
        left = LB
        last = t + 1 == NR
        w = "vq" if last else "urs"
        for x in WIN[t].split():
            if x == "al":
                for b in range(4):
                    tt(R("al", b, 384, 4), IND(R("fh", 384 * b, 384 * b + 384), R("q16", 12, 18)), R("fq", 384 + 96 * b, 480 + 96 * b), AL.add)
            elif x == "tu":
                cp(IND(R("tu"), R("q16", 6, 18)), R("val"))
            elif x == "ng":
                act(R("nl"), IND(R("tu"), R(lp)))
            elif x == "fn":
                for b in range(4):
                    act(R("fn32", 96 * b, 96 * b + 96), IND(R("w%d" % b, 0, 384), R(ln, 0, 6)))
            elif x == "ql":
                quant("ql", R("al"))
                for b in range(4):
                    mm(R(left[b], 0, 128), "wq", 128 * b, "ql", 128)
            elif x == "e2":
                cp(IND(R("ew"), R(ln, 0, 6)), R("ep", 112, 208))
            elif x == "e3":
                tt(R("pp", 60, 84), R("ec", 15, 384, 16), R("j24"), AL.max)
            elif x == "lk":
                act(R("lr3"), IND(R("iota0"), R("lo3")))
                dma("a", T.lk[:, :], T.lr3[0:128:16, :], [R("lr3")], [], "ok")
            elif x[0] == "l":
                b = int(x[1])
                tt(R("w%d" % b, 384, 480), R(left[b], 0, 96), R("fl32", 96 * b, 96 * b + 96), AL.add)
            elif x == "nl":
                scan(R("nlc"), R("t16h"), R("nl"))
            elif x == "st":
                ts(R(st), R("nlc", 15, 384, 16), col["s16"], AL.add)
                if t + 1 < NR:
                    send2(R(st), "rt%d" % t, (rank - d, R("lo%d" % (t + 1))), (rank + d, R("lp%d" % (t + 1))))
                else:
                    send(rank - d, "rt%d" % t, (R("lo3"), R(st)))
            elif x == "ec":
                scan(R("ec"), R("t16h"), R("ew"))
            elif x == "e4":
                ts(R("e4"), R("pp", 60, 84), col["pbe"], AL.add)
            elif x[0] == "a":
                b = int(x[1])
                for k in range(0 if b else 4):
                    mm(R(FB[k], 0, 128), "wq", 128 * k, vb, 128)
                tt(R("w%d" % b, 514, 706, 2), R(FB[b], 0, 96), R("fn32", 96 * b, 96 * b + 96), AL.add)
            elif x[0] in "VS":
                b, lo_, hi_ = int(x[1]), int(x[2], 16), int(x[3], 16)
                o, i = R(xn, 128 * lo_ + b, 128 * hi_, 4), IND(R("w%d" % b), R("e4", 2 * lo_, 2 * hi_))
                if x[0] == "V":
                    ts(o, i, 2.0 ** -5, AL.mult)
                else:
                    act(o, i, scale=2.0 ** -5)
            elif x[0] == "Q":
                piece(xn, int(x[1]), w)
    dma("s", T.oc[:, 0:1024], ap(R("xq", 0, 256, 1, "u8")), [R("xq", 0, 256)], [], "oc_")
    dma("s", T.oc[:, 1024:1536], ap(R("xq", 256, 384, 1, "u8")), [R("xq", 256, 384)], [], "oc2")
    cp(R("ys", 0, 128), R(BANK[0], 0, 128))
    cp(R("ys", 128, 256), R(BANK[1], 0, 128))
    dma("s", T.y[:, 0:256], ap(R("ys", 0, 256)), [R("ys", 0, 256)], [], "oy")
    cp(R("ys", 256, 384), R(BANK[2], 0, 128))
    dma("s", T.y[:, 256:384], ap(R("ys", 256, 384)), [R("ys", 256, 384)], [], "oz")
    for k in range(4):
        dma("a", T.osc[4 * k:4 * k + 4, :], T.xqs[32 * k:32 * k + 4, 0:384], [R("xqs")], [], "o%d" % k)
    for s in ("oc_", "oc2", "o0", "o1", "o2", "o3", "oy", "oz", "ok"):
        g.wait_ge(T.sem[s], 16)
    for s in ("v", "a", "p", "gc", "ls"):
        g.wait_ge(T.sem[s], CNT[s])
